import numpy as np
import ml_dtypes


def mxq(x, axis, fmt="e4m3"):
    dtype, down = {"e4m3": (ml_dtypes.float8_e4m3fn, 7), "e5m2": (ml_dtypes.float8_e5m2, 14)}[fmt]
    v = np.moveaxis(np.asarray(x, np.float32).astype(ml_dtypes.bfloat16).astype(np.float64), axis, -1)
    blocks = v.reshape(v.shape[:-1] + (-1, 32))
    amax = np.abs(blocks).max(-1, keepdims=True)
    byte = np.maximum(np.where(amax > 0, np.frexp(amax)[1] - 1 + 127, 0) - down, 1)
    scale = np.exp2(byte - 127.0)
    codes = (blocks / scale).astype(np.float32).astype(dtype).astype(np.float64)
    return np.moveaxis((codes * scale).reshape(v.shape), -1, axis)


WIDE = False


def mx_kscale(k):
    if not WIDE:
        return np.ones(k)
    levels = np.array([10, -10, 5, -5, 0])
    if k % 512:
        return np.exp2(np.random.permutation(np.resize(levels, k // 32))).repeat(32)
    a = np.empty((k // 512, 16))
    for p in range(k // 512):
        a[p, :8] = np.random.permutation(np.resize(levels, 8))
        for g in range(8):
            far = levels[np.abs(levels - a[p, g]) >= 10]
            a[p, g + 8] = far[np.random.randint(len(far))]
    return np.exp2(a.ravel()).repeat(32)


def f64(x):
    return np.asarray(x).astype(np.float64)


def striped(idx):
    return np.tile(idx.reshape(-1, 16).T, (8, 1)).astype(np.uint16)


def unstriped(offs):
    return offs[:16].T.reshape(-1).astype(np.int64)


E2M1 = np.array([0.0, 0.5, 1.0, 1.5, 2.0, 3.0, 4.0, 6.0, -0.0, -0.5, -1.0, -1.5, -2.0, -3.0, -4.0, -6.0])


def pack_weight(w, fmt):
    k, n = w.shape
    w = f64(np.asarray(w, np.float32).astype(ml_dtypes.bfloat16)).reshape(k // 32, 32, n)
    amax = np.abs(w).max(1)
    if fmt == "e4m3":
        byte = np.frexp(amax)[1] - 1 + 127 - 7
    else:
        mant, ex = np.frexp(amax / 6.0)
        byte = np.where(mant > 0.5, ex, ex - 1) + 127
    byte = np.clip(np.where(amax > 0, byte, 1), 1, 254)
    scaled = (w * np.exp2(127.0 - byte)[:, None, :]).reshape(k, n).astype(np.float32)
    by_word = np.ascontiguousarray(scaled.reshape(k // 512, 128, 4, n).transpose(0, 1, 3, 2))
    if fmt == "e4m3":
        words = by_word.astype(ml_dtypes.float8_e4m3fn).view(np.uint8)
    else:
        c = by_word.astype(ml_dtypes.float4_e2m1fn).view(np.uint8) & 0xF
        words = (c[..., 0::2] | (c[..., 1::2] << 4)).reshape(k // 512, 128, 2 * n)
    return np.ascontiguousarray(words), np.ascontiguousarray(byte.astype(np.uint8).reshape(k // 512, 16, n))


def unpack_weight(words, scales, fmt):
    g, _, n = scales.shape
    words = np.ascontiguousarray(words).reshape(g, 128, n, -1)
    if fmt == "e4m3":
        vals = words.view(ml_dtypes.float8_e4m3fn).astype(np.float64)
    else:
        nib = np.empty((g, 128, n, 4), np.uint8)
        nib[..., 0::2] = words & 0xF
        nib[..., 1::2] = words >> 4
        vals = E2M1[nib]
    vals = vals * np.repeat(np.exp2(scales.astype(np.float64) - 127.0), 8, axis=1)[..., None]
    return vals.transpose(0, 1, 3, 2).reshape(g * 512, n)


def gelu(v):
    return 0.5 * v * (1.0 + np.tanh(np.sqrt(2.0 / np.pi) * (v + 0.044715 * v**3)))


def often(T, S):
    return np.random.permutation(T)[(T * np.random.uniform(0, 1, S) ** 4).astype(np.int64)]


K, K2, H, N, T, S = 1024, 512, 1024, 384, 4096, 1024

def setup_inputs():
    n = np.random.standard_normal
    s = mx_kscale(K)[:, None]
    s2 = mx_kscale(K2)[:, None]
    u = mx_kscale(H)[:, None]
    tab_words, tab_scales = pack_weight(n((K, T)) * s, "e4m3")
    tab2_words, tab2_scales = pack_weight(n((K2, T)) * s2, "e2m1")
    w1_words, w1_scales = pack_weight(n((K, H)) / np.sqrt(K) / s * u.T, "e2m1")
    w2 = (n((K2, H)) / np.sqrt(K2) / s2).astype(np.float32)
    w3_words, w3_scales = pack_weight(1.5 * n((H, N)) / np.sqrt(H) / u, "e4m3")
    w4 = (1.5 * n((H, N)) / np.sqrt(H) / u).astype(np.float32)
    bv = (0.5 * n(N)).astype(np.float32)
    return {"tab_words": tab_words, "tab_scales": tab_scales, "offs": striped(often(T, S)),
            "tab2_words": tab2_words, "tab2_scales": tab2_scales, "offs2": striped(often(T, S)),
            "w1_words": w1_words, "w1_scales": w1_scales, "w2": w2,
            "w3_words": w3_words, "w3_scales": w3_scales, "w4": w4, "bv": bv}

def reference(tab_words, tab_scales, offs, tab2_words, tab2_scales, offs2,
              w1_words, w1_scales, w2, w3_words, w3_scales, w4, bv):
    v = unpack_weight(tab_words, tab_scales, "e4m3")[:, unstriped(offs)]
    v2 = unpack_weight(tab2_words, tab2_scales, "e2m1")[:, unstriped(offs2)]
    a = unpack_weight(w1_words, w1_scales, "e2m1").T @ v
    b = mxq(f64(w2), 0, "e4m3").T @ v2
    h = mxq(a * b, 0, "e4m3")
    d = unpack_weight(w3_words, w3_scales, "e4m3").T @ h
    o = mxq(f64(w4), 0, "e4m3").T @ h
    return d / (1.0 + np.exp(-o)) + f64(bv)[:, None]

@@ -1,0 +1,294 @@
+from contextlib import ExitStack
+
+import concourse.mybir as mybir
+
+K, K2, H, N, T, S = 1024, 512, 1024, 384, 4096, 1024
+FLOPS = 2 * S * (K * H + K2 * H + 2 * H * N)
+
+F32 = mybir.dt.float32
+BF16 = mybir.dt.bfloat16
+I32 = mybir.dt.int32
+U32 = mybir.dt.uint32
+U16 = mybir.dt.uint16
+U8 = mybir.dt.uint8
+FP8X4 = mybir.dt.float8_e4m3fn_x4
+FP4X4 = mybir.dt.float4_e2m1fn_x4
+MULT = mybir.AluOpType.mult
+ADD = mybir.AluOpType.add
+SIGMOID = mybir.ActivationFunctionType.Sigmoid
+IDENTITY = mybir.ActivationFunctionType.Identity
+
+P = 128
+HALF = 512
+JT = 128
+TAB_AT, W1_AT, W3_AT, TAB2_AT = 0, S, S + H, S + H + N
+STAGED = S + H + N + S
+
+
+def tile_list_soft_gripper_valves_kernel(
+    tc, tab_words, tab_scales, offs, tab2_words, tab2_scales, offs2,
+    w1_words, w1_scales, w2, w3_words, w3_scales, w4, bv, out,
+):
+    nc = tc.nc
+    with ExitStack() as ctx:
+        lists = ctx.enter_context(tc.tile_pool(name="lists", bufs=1))
+        keep = ctx.enter_context(tc.tile_pool(name="keep", bufs=1))
+        ring = ctx.enter_context(tc.tile_pool(name="ring", bufs=6))
+        psum = ctx.enter_context(tc.psum_pool(name="psum", bufs=6))
+        psum_b = ctx.enter_context(tc.psum_pool(name="psum_b", bufs=2))
+
+        def held(shape, dtype, name, tag=None):
+            return keep.tile(shape, dtype, name=name, tag=tag or name, align_bytes=64)
+
+        idx = lists.tile([P, S // 16], U16, name="idx")
+        idx2 = lists.tile([P, S // 16], U16, name="idx2")
+
+        tab_rows = held([P, T], U8, "tab_rows")
+        tab2_rows = held([P, T], U8, "tab2_rows")
+        w1_rows = held([P, H], U8, "w1_rows")
+        staged = held([P, STAGED], U8, "staged", tag="slot_s")
+        planes = [held([P, TAB2_AT], U8, "planes0"), held([P, STAGED], U8, "planes1")]
+
+        nc.vector.memset(tab_rows[0:96, :].bitcast(I32), 0)
+        nc.vector.memset(w1_rows[0:96, :].bitcast(I32), 0)
+        nc.vector.memset(tab2_rows[0:112, :].bitcast(I32), 0)
+        for plane in planes:
+            nc.gpsimd.memset(plane[:].bitcast(I32), 0)
+
+        warm = held([P, 8], F32, "warm")
+        warm_out = held([P, 8], F32, "warm_out")
+        nc.gpsimd.memset(warm[:], 0.0)
+        nc.scalar.activation(warm_out[:], warm[:], SIGMOID)
+
+        nc.sync.dma_start(idx[:], offs)
+        nc.sync.dma_start(tab_rows[96:128, :].bitcast(I32), tab_scales.rearrange("a q t -> (a q) t").bitcast(I32))
+        nc.sync.dma_start(w1_rows[96:128, :].bitcast(I32), w1_scales.rearrange("a q c -> (a q) c").bitcast(I32))
+        nc.sync.dma_start(idx2[:], offs2)
+        nc.sync.dma_start(tab2_rows[112:128, :].bitcast(I32), tab2_scales[0].bitcast(I32))
+        nc.sync.dma_start(
+            staged[96:128, W3_AT:TAB2_AT].bitcast(I32), w3_scales.rearrange("a q c -> (a q) c").bitcast(I32)
+        )
+        w1_raw = held([P, 2, H // 2], I32, "w1_raw", tag="slot_a")
+        nc.sync.dma_start(w1_raw[:], w1_words.bitcast(I32).rearrange("a p w -> p a w"))
+        tab_w = [held([P, T], I32, "tab_w0", tag="slot_b"), held([P, T], I32, "tab_w1", tag="slot_c")]
+        for a in range(2):
+            nc.sync.dma_start(tab_w[a][:], tab_words[a].rearrange("p t i -> p (t i)").bitcast(I32))
+
+        tab_picked = held([P, S], U8, "tab_picked")
+        tab2_picked = held([P, S], U8, "tab2_picked")
+        nc.vector.tensor_copy(tab_picked[:], tab_rows[:].indirect(idx[:]))
+        nc.vector.tensor_copy(
+            staged[:, W1_AT:W3_AT].rearrange("p (b t c i) -> p b c t i", b=2, t=4, i=16),
+            w1_rows[:].rearrange("p (b c i t) -> p b c t i", b=2, t=4, i=16),
+        )
+        nc.vector.tensor_copy(staged[:, TAB_AT:W1_AT].bitcast(I32), tab_picked[:].bitcast(I32))
+        nc.vector.tensor_copy(tab2_picked[:], tab2_rows[:].indirect(idx2[:]))
+        nc.vector.tensor_copy(staged[:, TAB2_AT:STAGED].bitcast(I32), tab2_picked[:].bitcast(I32))
+        for a in range(2):
+            width = STAGED if a == 1 else TAB2_AT
+            for q in range(4):
+                nc.scalar.dma_start(
+                    planes[a][32 * q : 32 * q + 4, :].bitcast(I32),
+                    staged[96 + 16 * a + 4 * q : 96 + 16 * a + 4 * q + 4, 0:width].bitcast(I32),
+                )
+
+        w1_codes = held([P, 2 * 2 * H], U8, "w1_codes")
+        nc.vector.tensor_copy(
+            w1_codes[:].bitcast(U16).rearrange("p (g t c i) -> p g c t i", g=4, t=4, i=8),
+            w1_raw[:].rearrange("p a w -> p (a w)").bitcast(U16).rearrange("p (g c i t) -> p g c t i", g=4, t=4, i=8),
+        )
+
+        v = {}
+        for a in range(2):
+            for jh in range(2):
+                v[a, jh] = held([P, HALF], U32, "v%d%d" % (a, jh))
+                nc.vector.tensor_copy(
+                    v[a, jh][:], tab_w[a][:].bitcast(U32).indirect(idx[:, 32 * jh : 32 * (jh + 1)])
+                )
+
+        w2_raw = [held([P, 4, HALF], F32, "w2_raw0", tag="slot_a"), None]
+        nc.sync.dma_start(w2_raw[0][:], w2[:, 0:HALF].rearrange("(p i) c -> p i c", i=4))
+        tab2_w = held([P, T // 2], I32, "tab2_w", tag="slot_b")
+        nc.sync.dma_start(tab2_w[:], tab2_words[0].bitcast(I32))
+        w2_raw[1] = held([P, 4, HALF], F32, "w2_raw1", tag="slot_c")
+        nc.sync.dma_start(w2_raw[1][:], w2[:, HALF:H].rearrange("(p i) c -> p i c", i=4))
+        bias = held([P, N // P], F32, "bias", tag="slot_s")
+        with nc.allow_non_contiguous_dma(reason="one bias value a partition"):
+            nc.sync.dma_start(bias[:], bv.rearrange("(c p) -> p c", p=P))
+
+        a_sb = {}
+
+        def first_product(b, jt):
+            jh, jl = divmod(jt, 4)
+            bank = psum.tile([P, 4, JT], F32, name="bank")
+            for a in range(2):
+                for t in range(4):
+                    col = 512 * b + 128 * t
+                    nc.tensor.matmul_mx(
+                        bank[:, t, :],
+                        lhsT=w1_codes[:, 2 * (H * a + col) : 2 * (H * a + col + 128)].bitcast(FP4X4),
+                        lhsT_scale=planes[a][:, W1_AT + col : W1_AT + col + 128],
+                        rhs=v[a, jh][:, JT * jl : JT * (jl + 1)].bitcast(FP8X4),
+                        rhs_scale=planes[a][:, TAB_AT + JT * jt : TAB_AT + JT * (jt + 1)],
+                        start=(a == 0 and t == 0),
+                        stop=(a == 1 and t == 3),
+                    )
+            a_sb[b, jt] = held([P, JT, 4], F32, "a_sb%d%d" % (b, jt))
+            nc.scalar.copy(a_sb[b, jt][:], bank[:].rearrange("p t j -> p j t"))
+
+        w2_codes, w2_scales = {}, {}
+
+        def prepare_w2(b, copies):
+            grouped = held([P, 4 * HALF], BF16, "w2_grouped%d" % b)
+            share = P // len(copies)
+            for part, copy in enumerate(copies):
+                ms = slice(share * part, share * (part + 1))
+                copy(
+                    grouped[:].rearrange("p (t m i) -> p m t i", t=4, i=4)[:, ms],
+                    w2_raw[b][:].rearrange("p i (m t) -> p m t i", t=4)[:, ms],
+                )
+            w2_codes[b] = held([P, HALF], U32, "w2_codes%d" % b)
+            w2_scales[b] = held([P, HALF], U8, "w2_scales%d" % b)
+            nc.vector.quantize_mx(w2_codes[b][:].bitcast(FP8X4), w2_scales[b][:], grouped[:])
+
+        v2 = {}
+
+        def gather_v2(jh):
+            v2[jh] = held([P, 2 * HALF], U8, "v2%d" % jh)
+            nc.vector.tensor_copy(
+                v2[jh][:].bitcast(U16), tab2_w[:].bitcast(U16).indirect(idx2[:, 32 * jh : 32 * (jh + 1)])
+            )
+
+        h = {}
+        h_codes = {}
+        h_scales = {}
+        for b in range(2):
+            for jh in range(2):
+                h[b, jh] = held([P, HALF, 4], BF16, "h%d%d" % (b, jh))
+
+        def grasp_code(b, tiles):
+            for jt in tiles:
+                jh, jl = divmod(jt, 4)
+                bank = psum_b.tile([P, 4, JT], F32, name="bank_b")
+                for t in range(4):
+                    nc.tensor.matmul_mx(
+                        bank[:, t, :],
+                        lhsT=w2_codes[b][:, 128 * t : 128 * (t + 1)].bitcast(FP8X4),
+                        lhsT_scale=w2_scales[b][:, 128 * t : 128 * (t + 1)],
+                        rhs=v2[jh][:, 2 * JT * jl : 2 * JT * (jl + 1)].bitcast(FP4X4),
+                        rhs_scale=planes[1][:, TAB2_AT + JT * jt : TAB2_AT + JT * (jt + 1)],
+                        start=True,
+                        stop=True,
+                    )
+                nc.vector.tensor_tensor(
+                    h[b, jh][:, JT * jl : JT * (jl + 1), :], bank[:].rearrange("p t j -> p j t"), a_sb[b, jt][:], MULT
+                )
+
+        def quantise_h(b, lo, width):
+            jh, at = divmod(lo, HALF)
+            codes = held([P, width], U32, "h_codes%d_%d" % (b, lo))
+            scales = held([P, width], U8, "h_scales%d_%d" % (b, lo))
+            nc.vector.quantize_mx(
+                codes[:].bitcast(FP8X4), scales[:], h[b, jh][:, at : at + width, :].rearrange("p j t -> p (j t)")
+            )
+            for off in range(0, width, 256):
+                h_codes[b, lo + off] = codes[:, off:width]
+                h_scales[b, lo + off] = scales[:, off:width]
+
+        def valves(lo, width):
+            gates, drives = [], []
+            for n in range(N // P):
+                if width == HALF:
+                    o_sum = psum.tile([P, HALF], F32, name="bank")[:]
+                    d_sum = psum.tile([P, HALF], F32, name="bank")[:]
+                else:
+                    both = psum.tile([P, 2, width], F32, name="bank")
+                    o_sum, d_sum = both[:, 0, :], both[:, 1, :]
+                for b in range(2):
+                    col = N * b + P * n
+                    nc.tensor.matmul_mx(
+                        o_sum,
+                        lhsT=w4_codes[:, col : col + P].bitcast(FP8X4),
+                        lhsT_scale=w4_scales[:, col : col + P],
+                        rhs=h_codes[b, lo][:, 0:width].bitcast(FP8X4),
+                        rhs_scale=h_scales[b, lo][:, 0:width],
+                        start=(b == 0),
+                        stop=(b == 1 and width == HALF),
+                    )
+                    nc.tensor.matmul_mx(
+                        d_sum,
+                        lhsT=w3_codes[:, b, P * n : P * (n + 1)].bitcast(FP8X4),
+                        lhsT_scale=planes[b][:, W3_AT + P * n : W3_AT + P * (n + 1)],
+                        rhs=h_codes[b, lo][:, 0:width].bitcast(FP8X4),
+                        rhs_scale=h_scales[b, lo][:, 0:width],
+                        start=(b == 0 and width == HALF),
+                        stop=(b == 1),
+                    )
+                gate = ring.tile([P, width], F32, name="gate")
+                nc.scalar.activation(gate[:], o_sum, SIGMOID)
+                gates.append(gate)
+                drives.append(d_sum)
+            return gates, drives
+
+        def finish(lo, width, gates, drives):
+            for n in range(N // P):
+                gated = ring.tile([P, width], F32, name="gated")
+                nc.vector.tensor_tensor(gated[:], drives[n], gates[n][:], MULT)
+                result = ring.tile([P, width], F32, name="result")
+                nc.scalar.activation(result[:], gated[:], IDENTITY, bias=bias[:, n : n + 1])
+                nc.sync.dma_start(out[P * n : P * (n + 1), lo : lo + width], result[:])
+
+        for jt in range(4):
+            first_product(0, jt)
+        prepare_w2(0, [nc.vector.tensor_copy, nc.scalar.copy])
+
+        w4_raw = held([P, 2, 4, N], F32, "w4_raw", tag="slot_a")
+        nc.sync.dma_start(
+            w4_raw[:].rearrange("p a i n -> p a (i n)"), w4.rearrange("(a p i) n -> p a (i n)", a=2, i=4)
+        )
+
+        gather_v2(0)
+        grasp_code(0, range(4))
+        for jt in range(4):
+            first_product(1, jt)
+        gather_v2(1)
+        w3_codes = held([P, 2, N], I32, "w3_codes", tag="slot_b")
+        nc.sync.dma_start(w3_codes[:], w3_words.rearrange("a p c i -> p a (c i)").bitcast(I32))
+        prepare_w2(1, [nc.scalar.copy])
+        quantise_h(0, 0, HALF)
+        for jt in range(4, 8):
+            first_product(0, jt)
+        grasp_code(1, range(4))
+        quantise_h(1, 0, HALF)
+        for jt in range(4, 8):
+            first_product(1, jt)
+
+        w4_grouped = held([P, 2, N, 4], BF16, "w4_grouped")
+        for a in range(2):
+            for n in range(N // P):
+                nc.gpsimd.tensor_scalar(
+                    w4_grouped[:, a, P * n : P * (n + 1), :],
+                    w4_raw[:, a, :, P * n : P * (n + 1)].rearrange("p i n -> p n i"),
+                    1.0, 0.0, MULT, ADD,
+                )
+        w4_codes = held([P, 2 * N], U32, "w4_codes")
+        w4_scales = held([P, 2 * N], U8, "w4_scales")
+        for lo, hi in ((0, 512), (512, 768)):
+            nc.vector.quantize_mx(
+                w4_codes[:, lo:hi].bitcast(FP8X4),
+                w4_scales[:, lo:hi],
+                w4_grouped[:].rearrange("p a n i -> p (a n i)")[:, 4 * lo : 4 * hi],
+            )
+
+        first = valves(0, HALF)
+        grasp_code(0, range(4, 8))
+        quantise_h(0, HALF, HALF)
+        finish(0, HALF, *first)
+        grasp_code(1, range(4, 6))
+        quantise_h(1, 512, 256)
+        second = valves(512, 256)
+        grasp_code(1, range(6, 8))
+        quantise_h(1, 768, 256)
+        third = valves(768, 256)
+        finish(512, 256, *second)
+        finish(768, 256, *third)

@@ -34,8 +34,8 @@ def tile_list_soft_gripper_valves_kernel(
         lists = ctx.enter_context(tc.tile_pool(name="lists", bufs=1))
         keep = ctx.enter_context(tc.tile_pool(name="keep", bufs=1))
         ring = ctx.enter_context(tc.tile_pool(name="ring", bufs=6))
-        psum = ctx.enter_context(tc.psum_pool(name="psum", bufs=6))
-        psum_b = ctx.enter_context(tc.psum_pool(name="psum_b", bufs=2))
+        psum = ctx.enter_context(tc.psum_pool(name="psum", bufs=4))
+        psum_b = ctx.enter_context(tc.psum_pool(name="psum_b", bufs=4))
 
         def held(shape, dtype, name, tag=None):
             return keep.tile(shape, dtype, name=name, tag=tag or name, align_bytes=64)
@@ -118,23 +118,22 @@ def tile_list_soft_gripper_valves_kernel(
 
         a_sb = {}
 
-        def first_product(b, jt):
-            jh, jl = divmod(jt, 4)
-            bank = psum.tile([P, 4, JT], F32, name="bank")
-            for a in range(2):
-                for t in range(4):
-                    col = 512 * b + 128 * t
+        def first_product(b, jh):
+            a_sb[b, jh] = held([P, 4, HALF], F32, "a_sb%d%d" % (b, jh))
+            for t in range(4):
+                bank = psum.tile([P, HALF], F32, name="bank")
+                col = 512 * b + 128 * t
+                for a in range(2):
                     nc.tensor.matmul_mx(
-                        bank[:, t, :],
+                        bank[:],
                         lhsT=w1_codes[:, 2 * (H * a + col) : 2 * (H * a + col + 128)].bitcast(FP4X4),
                         lhsT_scale=planes[a][:, W1_AT + col : W1_AT + col + 128],
-                        rhs=v[a, jh][:, JT * jl : JT * (jl + 1)].bitcast(FP8X4),
-                        rhs_scale=planes[a][:, TAB_AT + JT * jt : TAB_AT + JT * (jt + 1)],
-                        start=(a == 0 and t == 0),
-                        stop=(a == 1 and t == 3),
+                        rhs=v[a, jh][:].bitcast(FP8X4),
+                        rhs_scale=planes[a][:, TAB_AT + HALF * jh : TAB_AT + HALF * (jh + 1)],
+                        start=(a == 0),
+                        stop=(a == 1),
                     )
-            a_sb[b, jt] = held([P, JT, 4], F32, "a_sb%d%d" % (b, jt))
-            nc.scalar.copy(a_sb[b, jt][:], bank[:].rearrange("p t j -> p j t"))
+                nc.scalar.copy(a_sb[b, jh][:, t, :], bank[:])
 
         w2_codes, w2_scales = {}, {}
 
@@ -180,8 +179,12 @@ def tile_list_soft_gripper_valves_kernel(
                         start=True,
                         stop=True,
                     )
+                records = slice(JT * jl, JT * (jl + 1))
                 nc.vector.tensor_tensor(
-                    h[b, jh][:, JT * jl : JT * (jl + 1), :], bank[:].rearrange("p t j -> p j t"), a_sb[b, jt][:], MULT
+                    h[b, jh][:, records, :].rearrange("p (c i) t -> p c t i", i=2),
+                    bank[:].rearrange("p t (c i) -> p c t i", i=2),
+                    a_sb[b, jh][:, :, records].rearrange("p t (c i) -> p c t i", i=2),
+                    MULT,
                 )
 
         def quantise_h(b, lo, width):
@@ -195,14 +198,14 @@ def tile_list_soft_gripper_valves_kernel(
                 h_codes[b, lo + off] = codes[:, off:width]
                 h_scales[b, lo + off] = scales[:, off:width]
 
-        def valves(lo, width):
+        def valves(lo, width, pool, tag):
             gates, drives = [], []
             for n in range(N // P):
                 if width == HALF:
-                    o_sum = psum.tile([P, HALF], F32, name="bank")[:]
-                    d_sum = psum.tile([P, HALF], F32, name="bank")[:]
+                    o_sum = pool.tile([P, HALF], F32, name=tag)[:]
+                    d_sum = pool.tile([P, HALF], F32, name=tag)[:]
                 else:
-                    both = psum.tile([P, 2, width], F32, name="bank")
+                    both = pool.tile([P, 2, width], F32, name=tag)
                     o_sum, d_sum = both[:, 0, :], both[:, 1, :]
                 for b in range(2):
                     col = N * b + P * n
@@ -238,8 +241,7 @@ def tile_list_soft_gripper_valves_kernel(
                 nc.scalar.activation(result[:], gated[:], IDENTITY, bias=bias[:, n : n + 1])
                 nc.sync.dma_start(out[P * n : P * (n + 1), lo : lo + width], result[:])
 
-        for jt in range(4):
-            first_product(0, jt)
+        first_product(0, 0)
         prepare_w2(0, [nc.vector.tensor_copy, nc.scalar.copy])
 
         w4_raw = held([P, 2, 4, N], F32, "w4_raw", tag="slot_a")
@@ -249,19 +251,16 @@ def tile_list_soft_gripper_valves_kernel(
 
         gather_v2(0)
         grasp_code(0, range(4))
-        for jt in range(4):
-            first_product(1, jt)
+        first_product(1, 0)
         gather_v2(1)
         w3_codes = held([P, 2, N], I32, "w3_codes", tag="slot_b")
         nc.sync.dma_start(w3_codes[:], w3_words.rearrange("a p c i -> p a (c i)").bitcast(I32))
         prepare_w2(1, [nc.scalar.copy])
         quantise_h(0, 0, HALF)
-        for jt in range(4, 8):
-            first_product(0, jt)
+        first_product(0, 1)
         grasp_code(1, range(4))
         quantise_h(1, 0, HALF)
-        for jt in range(4, 8):
-            first_product(1, jt)
+        first_product(1, 1)
 
         w4_grouped = held([P, 2, N, 4], BF16, "w4_grouped")
         for a in range(2):
@@ -280,15 +279,15 @@ def tile_list_soft_gripper_valves_kernel(
                 w4_grouped[:].rearrange("p a n i -> p (a n i)")[:, 4 * lo : 4 * hi],
             )
 
-        first = valves(0, HALF)
+        first = valves(0, HALF, psum, "bank")
         grasp_code(0, range(4, 8))
         quantise_h(0, HALF, HALF)
         finish(0, HALF, *first)
         grasp_code(1, range(4, 6))
         quantise_h(1, 512, 256)
-        second = valves(512, 256)
+        second = valves(512, 256, psum, "bank")
         grasp_code(1, range(6, 8))
         quantise_h(1, 768, 256)
-        third = valves(768, 256)
+        third = valves(768, 256, psum_b, "bank_b")
         finish(512, 256, *second)
         finish(768, 256, *third)

@@ -49,8 +49,8 @@ def tile_list_soft_gripper_valves_kernel(
         staged = held([P, STAGED], U8, "staged", tag="slot_s")
         planes = [held([P, TAB2_AT], U8, "planes0"), held([P, STAGED], U8, "planes1")]
 
-        nc.vector.memset(tab_rows[0:96, :].bitcast(I32), 0)
         nc.vector.memset(w1_rows[0:96, :].bitcast(I32), 0)
+        nc.vector.memset(tab_rows[0:96, :].bitcast(I32), 0)
         nc.vector.memset(tab2_rows[0:112, :].bitcast(I32), 0)
         for plane in planes:
             nc.gpsimd.memset(plane[:].bitcast(I32), 0)
@@ -60,9 +60,9 @@ def tile_list_soft_gripper_valves_kernel(
         nc.gpsimd.memset(warm[:], 0.0)
         nc.scalar.activation(warm_out[:], warm[:], SIGMOID)
 
+        nc.sync.dma_start(w1_rows[96:128, :].bitcast(I32), w1_scales.rearrange("a q c -> (a q) c").bitcast(I32))
         nc.sync.dma_start(idx[:], offs)
         nc.sync.dma_start(tab_rows[96:128, :].bitcast(I32), tab_scales.rearrange("a q t -> (a q) t").bitcast(I32))
-        nc.sync.dma_start(w1_rows[96:128, :].bitcast(I32), w1_scales.rearrange("a q c -> (a q) c").bitcast(I32))
         nc.sync.dma_start(idx2[:], offs2)
         nc.sync.dma_start(tab2_rows[112:128, :].bitcast(I32), tab2_scales[0].bitcast(I32))
         nc.sync.dma_start(
@@ -76,11 +76,11 @@ def tile_list_soft_gripper_valves_kernel(
 
         tab_picked = held([P, S], U8, "tab_picked")
         tab2_picked = held([P, S], U8, "tab2_picked")
-        nc.vector.tensor_copy(tab_picked[:], tab_rows[:].indirect(idx[:]))
         nc.vector.tensor_copy(
             staged[:, W1_AT:W3_AT].rearrange("p (b t c i) -> p b c t i", b=2, t=4, i=16),
             w1_rows[:].rearrange("p (b c i t) -> p b c t i", b=2, t=4, i=16),
         )
+        nc.vector.tensor_copy(tab_picked[:], tab_rows[:].indirect(idx[:]))
         nc.vector.tensor_copy(staged[:, TAB_AT:W1_AT].bitcast(I32), tab_picked[:].bitcast(I32))
         nc.vector.tensor_copy(tab2_picked[:], tab2_rows[:].indirect(idx2[:]))
         nc.vector.tensor_copy(staged[:, TAB2_AT:STAGED].bitcast(I32), tab2_picked[:].bitcast(I32))
@@ -112,9 +112,6 @@ def tile_list_soft_gripper_valves_kernel(
         nc.sync.dma_start(tab2_w[:], tab2_words[0].bitcast(I32))
         w2_raw[1] = held([P, 4, HALF], F32, "w2_raw1", tag="slot_c")
         nc.sync.dma_start(w2_raw[1][:], w2[:, HALF:H].rearrange("(p i) c -> p i c", i=4))
-        bias = held([P, N // P], F32, "bias", tag="slot_s")
-        with nc.allow_non_contiguous_dma(reason="one bias value a partition"):
-            nc.sync.dma_start(bias[:], bv.rearrange("(c p) -> p c", p=P))
 
         a_sb = {}
 
@@ -233,12 +230,18 @@ def tile_list_soft_gripper_valves_kernel(
                 drives.append(d_sum)
             return gates, drives
 
-        def finish(lo, width, gates, drives):
+        def add_on_gpsimd(result, gated, column):
+            nc.gpsimd.tensor_scalar(result, gated, 1.0, column, MULT, ADD)
+
+        def add_on_scalar(result, gated, column):
+            nc.scalar.activation(result, gated, IDENTITY, bias=column)
+
+        def finish(lo, width, add_bias, gates, drives):
             for n in range(N // P):
                 gated = ring.tile([P, width], F32, name="gated")
                 nc.vector.tensor_tensor(gated[:], drives[n], gates[n][:], MULT)
                 result = ring.tile([P, width], F32, name="result")
-                nc.scalar.activation(result[:], gated[:], IDENTITY, bias=bias[:, n : n + 1])
+                add_bias(result[:], gated[:], bias[:, n : n + 1])
                 nc.sync.dma_start(out[P * n : P * (n + 1), lo : lo + width], result[:])
 
         first_product(0, 0)
@@ -249,6 +252,9 @@ def tile_list_soft_gripper_valves_kernel(
             w4_raw[:].rearrange("p a i n -> p a (i n)"), w4.rearrange("(a p i) n -> p a (i n)", a=2, i=4)
         )
 
+        bias = held([P, N // P], F32, "bias", tag="w2_grouped0")
+        with nc.allow_non_contiguous_dma(reason="one bias value a partition"):
+            nc.sync.dma_start(bias[:], bv.rearrange("(c p) -> p c", p=P))
         gather_v2(0)
         grasp_code(0, range(4))
         first_product(1, 0)
@@ -260,34 +266,28 @@ def tile_list_soft_gripper_valves_kernel(
         first_product(0, 1)
         grasp_code(1, range(4))
         quantise_h(1, 0, HALF)
-        first_product(1, 1)
-
-        w4_grouped = held([P, 2, N, 4], BF16, "w4_grouped")
+        w4_grouped = held([P, 2 * N * 4], BF16, "w4_grouped")
         for a in range(2):
-            for n in range(N // P):
-                nc.gpsimd.tensor_scalar(
-                    w4_grouped[:, a, P * n : P * (n + 1), :],
-                    w4_raw[:, a, :, P * n : P * (n + 1)].rearrange("p i n -> p n i"),
-                    1.0, 0.0, MULT, ADD,
-                )
+            nc.scalar.copy(
+                w4_grouped[:, 4 * N * a : 4 * N * (a + 1)].rearrange("p (c n i) -> p c i n", n=4, i=4),
+                w4_raw[:, a].rearrange("p i (c n) -> p c i n", n=4),
+            )
+        first_product(1, 1)
+        grasp_code(0, range(4, 8))
         w4_codes = held([P, 2 * N], U32, "w4_codes")
         w4_scales = held([P, 2 * N], U8, "w4_scales")
         for lo, hi in ((0, 512), (512, 768)):
             nc.vector.quantize_mx(
-                w4_codes[:, lo:hi].bitcast(FP8X4),
-                w4_scales[:, lo:hi],
-                w4_grouped[:].rearrange("p a n i -> p (a n i)")[:, 4 * lo : 4 * hi],
+                w4_codes[:, lo:hi].bitcast(FP8X4), w4_scales[:, lo:hi], w4_grouped[:, 4 * lo : 4 * hi]
             )
-
         first = valves(0, HALF, psum, "bank")
-        grasp_code(0, range(4, 8))
         quantise_h(0, HALF, HALF)
-        finish(0, HALF, *first)
+        finish(0, HALF, add_on_gpsimd, *first)
         grasp_code(1, range(4, 6))
         quantise_h(1, 512, 256)
         second = valves(512, 256, psum, "bank")
         grasp_code(1, range(6, 8))
         quantise_h(1, 768, 256)
         third = valves(768, 256, psum_b, "bank_b")
-        finish(512, 256, *second)
-        finish(768, 256, *third)
+        finish(512, 256, add_on_gpsimd, *second)
+        finish(768, 256, add_on_scalar, *third)

@@ -134,15 +134,12 @@ def tile_list_soft_gripper_valves_kernel(
 
         w2_codes, w2_scales = {}, {}
 
-        def prepare_w2(b, copies):
+        def prepare_w2(b, copy):
             grouped = held([P, 4 * HALF], BF16, "w2_grouped%d" % b)
-            share = P // len(copies)
-            for part, copy in enumerate(copies):
-                ms = slice(share * part, share * (part + 1))
-                copy(
-                    grouped[:].rearrange("p (t m i) -> p m t i", t=4, i=4)[:, ms],
-                    w2_raw[b][:].rearrange("p i (m t) -> p m t i", t=4)[:, ms],
-                )
+            copy(
+                grouped[:].rearrange("p (t m i) -> p m t i", t=4, i=4),
+                w2_raw[b][:].rearrange("p i (m t) -> p m t i", t=4),
+            )
             w2_codes[b] = held([P, HALF], U32, "w2_codes%d" % b)
             w2_scales[b] = held([P, HALF], U8, "w2_scales%d" % b)
             nc.vector.quantize_mx(w2_codes[b][:].bitcast(FP8X4), w2_scales[b][:], grouped[:])
@@ -245,7 +242,7 @@ def tile_list_soft_gripper_valves_kernel(
                 nc.sync.dma_start(out[P * n : P * (n + 1), lo : lo + width], result[:])
 
         first_product(0, 0)
-        prepare_w2(0, [nc.vector.tensor_copy, nc.scalar.copy])
+        prepare_w2(0, nc.vector.tensor_copy)
 
         w4_raw = held([P, 2, 4, N], F32, "w4_raw", tag="slot_a")
         nc.sync.dma_start(
@@ -257,37 +254,43 @@ def tile_list_soft_gripper_valves_kernel(
             nc.sync.dma_start(bias[:], bv.rearrange("(c p) -> p c", p=P))
         gather_v2(0)
         grasp_code(0, range(4))
-        first_product(1, 0)
+        first_product(0, 1)
         gather_v2(1)
         w3_codes = held([P, 2, N], I32, "w3_codes", tag="slot_b")
         nc.sync.dma_start(w3_codes[:], w3_words.rearrange("a p c i -> p a (c i)").bitcast(I32))
-        prepare_w2(1, [nc.scalar.copy])
-        quantise_h(0, 0, HALF)
-        first_product(0, 1)
-        grasp_code(1, range(4))
-        quantise_h(1, 0, HALF)
-        w4_grouped = held([P, 2 * N * 4], BF16, "w4_grouped")
-        for a in range(2):
-            nc.scalar.copy(
-                w4_grouped[:, 4 * N * a : 4 * N * (a + 1)].rearrange("p (c n i) -> p c i n", n=4, i=4),
-                w4_raw[:, a].rearrange("p i (c n) -> p c i n", n=4),
-            )
-        first_product(1, 1)
         grasp_code(0, range(4, 8))
+        prepare_w2(1, nc.scalar.copy)
+        first_product(1, 0)
+        quantise_h(0, 0, HALF)
+        quantise_h(0, HALF, HALF)
+
+        w4_grouped = held([P, 2 * N * 4], BF16, "w4_grouped")
+        for n in range(N // P):
+            nc.gpsimd.tensor_scalar(
+                w4_grouped[:, 4 * P * n : 4 * P * (n + 1)].rearrange("p (n i) -> p n i", i=4),
+                w4_raw[:, 0, :, P * n : P * (n + 1)].rearrange("p i n -> p n i"),
+                1.0, 0.0, MULT, ADD,
+            )
+        nc.scalar.copy(
+            w4_grouped[:, 4 * N : 8 * N].rearrange("p (c n i) -> p c i n", n=4, i=4),
+            w4_raw[:, 1].rearrange("p i (c n) -> p c i n", n=4),
+        )
+        first_product(1, 1)
+        grasp_code(1, range(4))
         w4_codes = held([P, 2 * N], U32, "w4_codes")
         w4_scales = held([P, 2 * N], U8, "w4_scales")
         for lo, hi in ((0, 512), (512, 768)):
             nc.vector.quantize_mx(
                 w4_codes[:, lo:hi].bitcast(FP8X4), w4_scales[:, lo:hi], w4_grouped[:, 4 * lo : 4 * hi]
             )
+        quantise_h(1, 0, HALF)
         first = valves(0, HALF, psum, "bank")
-        quantise_h(0, HALF, HALF)
-        finish(0, HALF, add_on_gpsimd, *first)
         grasp_code(1, range(4, 6))
         quantise_h(1, 512, 256)
         second = valves(512, 256, psum, "bank")
         grasp_code(1, range(6, 8))
         quantise_h(1, 768, 256)
         third = valves(768, 256, psum_b, "bank_b")
+        finish(0, HALF, add_on_scalar, *first)
         finish(512, 256, add_on_gpsimd, *second)
         finish(768, 256, add_on_scalar, *third)

@@ -55,14 +55,9 @@ def tile_list_soft_gripper_valves_kernel(
         for plane in planes:
             nc.gpsimd.memset(plane[:].bitcast(I32), 0)
 
-        warm = held([P, 8], F32, "warm")
-        warm_out = held([P, 8], F32, "warm_out")
-        nc.gpsimd.memset(warm[:], 0.0)
-        nc.scalar.activation(warm_out[:], warm[:], SIGMOID)
-
-        nc.sync.dma_start(w1_rows[96:128, :].bitcast(I32), w1_scales.rearrange("a q c -> (a q) c").bitcast(I32))
         nc.sync.dma_start(idx[:], offs)
         nc.sync.dma_start(tab_rows[96:128, :].bitcast(I32), tab_scales.rearrange("a q t -> (a q) t").bitcast(I32))
+        nc.sync.dma_start(w1_rows[96:128, :].bitcast(I32), w1_scales.rearrange("a q c -> (a q) c").bitcast(I32))
         nc.sync.dma_start(idx2[:], offs2)
         nc.sync.dma_start(tab2_rows[112:128, :].bitcast(I32), tab2_scales[0].bitcast(I32))
         nc.sync.dma_start(
@@ -70,27 +65,31 @@ def tile_list_soft_gripper_valves_kernel(
         )
         w1_raw = held([P, 2, H // 2], I32, "w1_raw", tag="slot_a")
         nc.sync.dma_start(w1_raw[:], w1_words.bitcast(I32).rearrange("a p w -> p a w"))
-        tab_w = [held([P, T], I32, "tab_w0", tag="slot_b"), held([P, T], I32, "tab_w1", tag="slot_c")]
-        for a in range(2):
-            nc.sync.dma_start(tab_w[a][:], tab_words[a].rearrange("p t i -> p (t i)").bitcast(I32))
+        tab_w = [held([P, T], I32, "tab_w0", tag="slot_b"), None]
+        nc.sync.dma_start(tab_w[0][:], tab_words[0].rearrange("p t i -> p (t i)").bitcast(I32))
 
-        tab_picked = held([P, S], U8, "tab_picked")
+        tab_picked = held([P, S], U8, "tab_picked", tag="slot_c")
         tab2_picked = held([P, S], U8, "tab2_picked")
+        nc.vector.tensor_copy(tab_picked[:], tab_rows[:].indirect(idx[:]))
         nc.vector.tensor_copy(
             staged[:, W1_AT:W3_AT].rearrange("p (b t c i) -> p b c t i", b=2, t=4, i=16),
             w1_rows[:].rearrange("p (b c i t) -> p b c t i", b=2, t=4, i=16),
         )
-        nc.vector.tensor_copy(tab_picked[:], tab_rows[:].indirect(idx[:]))
         nc.vector.tensor_copy(staged[:, TAB_AT:W1_AT].bitcast(I32), tab_picked[:].bitcast(I32))
-        nc.vector.tensor_copy(tab2_picked[:], tab2_rows[:].indirect(idx2[:]))
-        nc.vector.tensor_copy(staged[:, TAB2_AT:STAGED].bitcast(I32), tab2_picked[:].bitcast(I32))
-        for a in range(2):
-            width = STAGED if a == 1 else TAB2_AT
+
+        def move_rows(a, width):
             for q in range(4):
-                nc.scalar.dma_start(
+                nc.sync.dma_start(
                     planes[a][32 * q : 32 * q + 4, :].bitcast(I32),
                     staged[96 + 16 * a + 4 * q : 96 + 16 * a + 4 * q + 4, 0:width].bitcast(I32),
                 )
+
+        move_rows(0, TAB2_AT)
+        tab_w[1] = held([P, T], I32, "tab_w1", tag="slot_c")
+        nc.sync.dma_start(tab_w[1][:], tab_words[1].rearrange("p t i -> p (t i)").bitcast(I32))
+        nc.vector.tensor_copy(tab2_picked[:], tab2_rows[:].indirect(idx2[:]))
+        nc.vector.tensor_copy(staged[:, TAB2_AT:STAGED].bitcast(I32), tab2_picked[:].bitcast(I32))
+        move_rows(1, STAGED)
 
         w1_codes = held([P, 2 * 2 * H], U8, "w1_codes")
         nc.vector.tensor_copy(
@@ -155,9 +154,8 @@ def tile_list_soft_gripper_valves_kernel(
         h = {}
         h_codes = {}
         h_scales = {}
-        for b in range(2):
-            for jh in range(2):
-                h[b, jh] = held([P, HALF, 4], BF16, "h%d%d" % (b, jh))
+        for b, lo, width in ((0, 0, HALF), (0, HALF, HALF), (1, 0, HALF), (1, HALF, 256)):
+            h[b, lo] = held([P, width, 4], BF16, "h%d_%d" % (b, lo))
 
         def grasp_code(b, tiles):
             for jt in tiles:
@@ -174,19 +172,19 @@ def tile_list_soft_gripper_valves_kernel(
                         stop=True,
                     )
                 records = slice(JT * jl, JT * (jl + 1))
+                lo = max(first for (block, first) in h if block == b and first <= JT * jt)
                 nc.vector.tensor_tensor(
-                    h[b, jh][:, records, :].rearrange("p (c i) t -> p c t i", i=2),
+                    h[b, lo][:, JT * jt - lo : JT * (jt + 1) - lo, :].rearrange("p (c i) t -> p c t i", i=2),
                     bank[:].rearrange("p t (c i) -> p c t i", i=2),
                     a_sb[b, jh][:, :, records].rearrange("p t (c i) -> p c t i", i=2),
                     MULT,
                 )
 
         def quantise_h(b, lo, width):
-            jh, at = divmod(lo, HALF)
             codes = held([P, width], U32, "h_codes%d_%d" % (b, lo))
             scales = held([P, width], U8, "h_scales%d_%d" % (b, lo))
             nc.vector.quantize_mx(
-                codes[:].bitcast(FP8X4), scales[:], h[b, jh][:, at : at + width, :].rearrange("p j t -> p (j t)")
+                codes[:].bitcast(FP8X4), scales[:], h[b, lo][:].rearrange("p j t -> p (j t)")
             )
             for off in range(0, width, 256):
                 h_codes[b, lo + off] = codes[:, off:width]
@@ -221,7 +219,10 @@ def tile_list_soft_gripper_valves_kernel(
                         start=(b == 0 and width == HALF),
                         stop=(b == 1),
                     )
-                gate = ring.tile([P, width], F32, name="gate")
+                if lo == 0 and n == 1:
+                    gate = held([P, width], F32, "held_gate", tag="slot_f")
+                else:
+                    gate = ring.tile([P, width], F32, name="gate")
                 nc.scalar.activation(gate[:], o_sum, SIGMOID)
                 gates.append(gate)
                 drives.append(d_sum)
@@ -229,6 +230,9 @@ def tile_list_soft_gripper_valves_kernel(
 
         def add_on_gpsimd(result, gated, column):
             nc.gpsimd.tensor_scalar(result, gated, 1.0, column, MULT, ADD)
+
+        def add_on_vector(result, gated, column):
+            nc.vector.tensor_scalar(result, gated, 1.0, column, MULT, ADD)
 
         def add_on_scalar(result, gated, column):
             nc.scalar.activation(result, gated, IDENTITY, bias=column)
@@ -244,20 +248,20 @@ def tile_list_soft_gripper_valves_kernel(
         first_product(0, 0)
         prepare_w2(0, nc.vector.tensor_copy)
 
-        w4_raw = held([P, 2, 4, N], F32, "w4_raw", tag="slot_a")
+        w3_codes = held([P, 2, N], I32, "w3_codes", tag="slot_a")
+        nc.sync.dma_start(w3_codes[:], w3_words.rearrange("a p c i -> p a (c i)").bitcast(I32))
+        w4_raw = held([P, 2, 4, N], F32, "w4_raw", tag="w2_grouped0")
         nc.sync.dma_start(
             w4_raw[:].rearrange("p a i n -> p a (i n)"), w4.rearrange("(a p i) n -> p a (i n)", a=2, i=4)
         )
 
-        bias = held([P, N // P], F32, "bias", tag="w2_grouped0")
-        with nc.allow_non_contiguous_dma(reason="one bias value a partition"):
-            nc.sync.dma_start(bias[:], bv.rearrange("(c p) -> p c", p=P))
         gather_v2(0)
         grasp_code(0, range(4))
         first_product(0, 1)
         gather_v2(1)
-        w3_codes = held([P, 2, N], I32, "w3_codes", tag="slot_b")
-        nc.sync.dma_start(w3_codes[:], w3_words.rearrange("a p c i -> p a (c i)").bitcast(I32))
+        bias = held([P, N // P], F32, "bias", tag="slot_b")
+        with nc.allow_non_contiguous_dma(reason="one bias value a partition"):
+            nc.sync.dma_start(bias[:], bv.rearrange("(c p) -> p c", p=P))
         grasp_code(0, range(4, 8))
         prepare_w2(1, nc.scalar.copy)
         first_product(1, 0)
@@ -287,10 +291,11 @@ def tile_list_soft_gripper_valves_kernel(
         first = valves(0, HALF, psum, "bank")
         grasp_code(1, range(4, 6))
         quantise_h(1, 512, 256)
+        finish(0, HALF, add_on_scalar, *first)
         second = valves(512, 256, psum, "bank")
+        h[1, 768] = held([P, 256, 4], BF16, "h1_768", tag="slot_f")
         grasp_code(1, range(6, 8))
         quantise_h(1, 768, 256)
         third = valves(768, 256, psum_b, "bank_b")
-        finish(0, HALF, add_on_scalar, *first)
         finish(512, 256, add_on_gpsimd, *second)
-        finish(768, 256, add_on_scalar, *third)
+        finish(768, 256, add_on_vector, *third)

@@ -15,12 +15,14 @@ FP8X4 = mybir.dt.float8_e4m3fn_x4
 FP4X4 = mybir.dt.float4_e2m1fn_x4
 MULT = mybir.AluOpType.mult
 ADD = mybir.AluOpType.add
-SIGMOID = mybir.ActivationFunctionType.Sigmoid
+TANH = mybir.ActivationFunctionType.Tanh
 IDENTITY = mybir.ActivationFunctionType.Identity
 
 P = 128
 HALF = 512
+QUARTER = 256
 JT = 128
+KIB = 1024
 TAB_AT, W1_AT, W3_AT, TAB2_AT = 0, S, S + H, S + H + N
 STAGED = S + H + N + S
 
@@ -33,12 +35,18 @@ def tile_list_soft_gripper_valves_kernel(
     with ExitStack() as ctx:
         lists = ctx.enter_context(tc.tile_pool(name="lists", bufs=1))
         keep = ctx.enter_context(tc.tile_pool(name="keep", bufs=1))
+        laid = ctx.enter_context(tc.tile_pool(name="laid", bufs=1))
         ring = ctx.enter_context(tc.tile_pool(name="ring", bufs=6))
-        psum = ctx.enter_context(tc.psum_pool(name="psum", bufs=4))
-        psum_b = ctx.enter_context(tc.psum_pool(name="psum_b", bufs=4))
+        psum = ctx.enter_context(tc.psum_pool(name="psum", bufs=1))
 
         def held(shape, dtype, name, tag=None):
             return keep.tile(shape, dtype, name=name, tag=tag or name, align_bytes=64)
+
+        def placed(shape, dtype, name, at):
+            return laid.tile(shape, dtype, name=name, tag=name, align_bytes=64, offset=at)
+
+        def bank(number, shape):
+            return psum.tile(shape, F32, name="bank%d" % number, tag="bank%d" % number)
 
         idx = lists.tile([P, S // 16], U16, name="idx")
         idx2 = lists.tile([P, S // 16], U16, name="idx2")
@@ -46,7 +54,7 @@ def tile_list_soft_gripper_valves_kernel(
         tab_rows = held([P, T], U8, "tab_rows")
         tab2_rows = held([P, T], U8, "tab2_rows")
         w1_rows = held([P, H], U8, "w1_rows")
-        staged = held([P, STAGED], U8, "staged", tag="slot_s")
+        staged = held([P, STAGED], U8, "staged")
         planes = [held([P, TAB2_AT], U8, "planes0"), held([P, STAGED], U8, "planes1")]
 
         nc.vector.memset(w1_rows[0:96, :].bitcast(I32), 0)
@@ -55,73 +63,92 @@ def tile_list_soft_gripper_valves_kernel(
         for plane in planes:
             nc.gpsimd.memset(plane[:].bitcast(I32), 0)
 
+        tab_w = [placed([P, T], I32, "tab_w0", 0), None]
+        w1_raw = held([P, 2, H // 2], I32, "w1_raw", tag="slot_a")
+        nc.sync.dma_start(w1_rows[96:128, :].bitcast(I32), w1_scales.rearrange("a q c -> (a q) c").bitcast(I32))
         nc.sync.dma_start(idx[:], offs)
         nc.sync.dma_start(tab_rows[96:128, :].bitcast(I32), tab_scales.rearrange("a q t -> (a q) t").bitcast(I32))
-        nc.sync.dma_start(w1_rows[96:128, :].bitcast(I32), w1_scales.rearrange("a q c -> (a q) c").bitcast(I32))
-        nc.sync.dma_start(idx2[:], offs2)
-        nc.sync.dma_start(tab2_rows[112:128, :].bitcast(I32), tab2_scales[0].bitcast(I32))
         nc.sync.dma_start(
             staged[96:128, W3_AT:TAB2_AT].bitcast(I32), w3_scales.rearrange("a q c -> (a q) c").bitcast(I32)
         )
-        w1_raw = held([P, 2, H // 2], I32, "w1_raw", tag="slot_a")
-        nc.sync.dma_start(w1_raw[:], w1_words.bitcast(I32).rearrange("a p w -> p a w"))
-        tab_w = [held([P, T], I32, "tab_w0", tag="slot_b"), None]
+        nc.sync.dma_start(idx2[:], offs2)
+        nc.sync.dma_start(tab2_rows[112:128, :].bitcast(I32), tab2_scales[0].bitcast(I32))
         nc.sync.dma_start(tab_w[0][:], tab_words[0].rearrange("p t i -> p (t i)").bitcast(I32))
+        nc.sync.dma_start(w1_raw[:], w1_words.bitcast(I32).rearrange("a p w -> p a w"))
 
-        tab_picked = held([P, S], U8, "tab_picked", tag="slot_c")
-        tab2_picked = held([P, S], U8, "tab2_picked")
-        nc.vector.tensor_copy(tab_picked[:], tab_rows[:].indirect(idx[:]))
+        tab_picked = placed([P, S], U8, "tab_picked", 24 * KIB)
+        tab2_picked = held([P, S], U8, "tab2_picked", tag="slot_b")
         nc.vector.tensor_copy(
             staged[:, W1_AT:W3_AT].rearrange("p (b t c i) -> p b c t i", b=2, t=4, i=16),
             w1_rows[:].rearrange("p (b c i t) -> p b c t i", b=2, t=4, i=16),
         )
+        nc.vector.tensor_copy(tab_picked[:], tab_rows[:].indirect(idx[:]))
         nc.vector.tensor_copy(staged[:, TAB_AT:W1_AT].bitcast(I32), tab_picked[:].bitcast(I32))
 
-        def move_rows(a, width):
+        def move_rows(queue, a, width):
             for q in range(4):
-                nc.sync.dma_start(
+                queue.dma_start(
                     planes[a][32 * q : 32 * q + 4, :].bitcast(I32),
                     staged[96 + 16 * a + 4 * q : 96 + 16 * a + 4 * q + 4, 0:width].bitcast(I32),
                 )
 
-        move_rows(0, TAB2_AT)
-        tab_w[1] = held([P, T], I32, "tab_w1", tag="slot_c")
+        move_rows(nc.sync, 0, TAB2_AT)
+        tab_w[1] = placed([P, T], I32, "tab_w1", 24 * KIB)
         nc.sync.dma_start(tab_w[1][:], tab_words[1].rearrange("p t i -> p (t i)").bitcast(I32))
         nc.vector.tensor_copy(tab2_picked[:], tab2_rows[:].indirect(idx2[:]))
         nc.vector.tensor_copy(staged[:, TAB2_AT:STAGED].bitcast(I32), tab2_picked[:].bitcast(I32))
-        move_rows(1, STAGED)
+        move_rows(nc.sync, 1, STAGED)
 
+        v = {}
+
+        def gather_v(a, jh):
+            v[a, jh] = held([P, HALF], U32, "v%d%d" % (a, jh), tag="slot_a" if (a, jh) == (0, 1) else None)
+            nc.vector.tensor_copy(v[a, jh][:], tab_w[a][:].bitcast(U32).indirect(idx[:, 32 * jh : 32 * (jh + 1)]))
+
+        gather_v(0, 0)
         w1_codes = held([P, 2 * 2 * H], U8, "w1_codes")
         nc.vector.tensor_copy(
             w1_codes[:].bitcast(U16).rearrange("p (g t c i) -> p g c t i", g=4, t=4, i=8),
             w1_raw[:].rearrange("p a w -> p (a w)").bitcast(U16).rearrange("p (g c i t) -> p g c t i", g=4, t=4, i=8),
         )
+        gather_v(0, 1)
+        gather_v(1, 0)
+        gather_v(1, 1)
 
-        v = {}
-        for a in range(2):
-            for jh in range(2):
-                v[a, jh] = held([P, HALF], U32, "v%d%d" % (a, jh))
-                nc.vector.tensor_copy(
-                    v[a, jh][:], tab_w[a][:].bitcast(U32).indirect(idx[:, 32 * jh : 32 * (jh + 1)])
-                )
-
-        w2_raw = [held([P, 4, HALF], F32, "w2_raw0", tag="slot_a"), None]
-        nc.sync.dma_start(w2_raw[0][:], w2[:, 0:HALF].rearrange("(p i) c -> p i c", i=4))
-        tab2_w = held([P, T // 2], I32, "tab2_w", tag="slot_b")
+        w2_first = held([P, 4, HALF], F32, "w2_first", tag="slot_b")
+        nc.sync.dma_start(w2_first[:], w2[:, 0:HALF].rearrange("(p i) c -> p i c", i=4))
+        tab2_w = placed([P, T // 2], I32, "tab2_w", 0)
         nc.sync.dma_start(tab2_w[:], tab2_words[0].bitcast(I32))
-        w2_raw[1] = held([P, 4, HALF], F32, "w2_raw1", tag="slot_c")
-        nc.sync.dma_start(w2_raw[1][:], w2[:, HALF:H].rearrange("(p i) c -> p i c", i=4))
+        w2_late = [placed([P, 4, QUARTER], F32, "w2_late%d" % u, (20, 24)[u] * KIB + (64, 256)[u]) for u in range(2)]
+        for u in range(2):
+            nc.sync.dma_start(
+                w2_late[u][:], w2[:, HALF + QUARTER * u : HALF + QUARTER * (u + 1)].rearrange("(p i) c -> p i c", i=4)
+            )
+        w4_raw = [placed([P, 4, N], F32, "w4_raw%d" % b, at * KIB + 256) for b, at in enumerate((28, 37))]
+        for b in range(2):
+            nc.sync.dma_start(
+                w4_raw[b][:].rearrange("p i n -> p (i n)"),
+                w4[HALF * b : HALF * (b + 1), :].rearrange("(p i) n -> p (i n)", i=4),
+            )
+        w3_codes = placed([P, 2, N], I32, "w3_codes", 34 * KIB + 256)
+        nc.sync.dma_start(w3_codes[:], w3_words.rearrange("a p c i -> p a (c i)").bitcast(I32))
+        bias = placed([P, N // P], F32, "bias", 24 * KIB + 64)
+        with nc.allow_non_contiguous_dma(reason="one bias value a partition"):
+            nc.sync.dma_start(bias[:], bv.rearrange("(c p) -> p c", p=P))
 
         a_sb = {}
 
         def first_product(b, jh):
-            a_sb[b, jh] = held([P, 4, HALF], F32, "a_sb%d%d" % (b, jh))
+            if (b, jh) == (1, 0):
+                a_sb[b, jh] = placed([P, 4, HALF], F32, "a_sb10", 16 * KIB)
+            else:
+                a_sb[b, jh] = held([P, 4, HALF], F32, "a_sb%d%d" % (b, jh))
             for t in range(4):
-                bank = psum.tile([P, HALF], F32, name="bank")
+                sums = bank(t, [P, HALF])
                 col = 512 * b + 128 * t
                 for a in range(2):
                     nc.tensor.matmul_mx(
-                        bank[:],
+                        sums[:],
                         lhsT=w1_codes[:, 2 * (H * a + col) : 2 * (H * a + col + 128)].bitcast(FP4X4),
                         lhsT_scale=planes[a][:, W1_AT + col : W1_AT + col + 128],
                         rhs=v[a, jh][:].bitcast(FP8X4),
@@ -129,19 +156,23 @@ def tile_list_soft_gripper_valves_kernel(
                         start=(a == 0),
                         stop=(a == 1),
                     )
-                nc.scalar.copy(a_sb[b, jh][:, t, :], bank[:])
+                nc.scalar.copy(a_sb[b, jh][:, t, :], sums[:])
 
-        w2_codes, w2_scales = {}, {}
+        w2_grouped = [held([P, 4 * HALF], BF16, "w2_grouped%d" % b) for b in range(2)]
+        w2_codes = [held([P, HALF], U32, "w2_codes%d" % b) for b in range(2)]
+        w2_scales = [held([P, HALF], U8, "w2_scales%d" % b) for b in range(2)]
 
-        def prepare_w2(b, copy):
-            grouped = held([P, 4 * HALF], BF16, "w2_grouped%d" % b)
+        def round_on_gpsimd(dst, src):
+            nc.gpsimd.tensor_scalar(dst, src, 1.0, 0.0, MULT, ADD)
+
+        def round_w2(raw, b, lo, hi, copy, order):
             copy(
-                grouped[:].rearrange("p (t m i) -> p m t i", t=4, i=4),
-                w2_raw[b][:].rearrange("p i (m t) -> p m t i", t=4),
+                w2_grouped[b][:].rearrange("p (t m i) -> p t m i", t=4, i=4)[:, :, lo:hi, :].rearrange("p t m i -> " + order),
+                raw[:].rearrange("p i (m t) -> " + order, t=4),
             )
-            w2_codes[b] = held([P, HALF], U32, "w2_codes%d" % b)
-            w2_scales[b] = held([P, HALF], U8, "w2_scales%d" % b)
-            nc.vector.quantize_mx(w2_codes[b][:].bitcast(FP8X4), w2_scales[b][:], grouped[:])
+
+        def quantise_w2(b):
+            nc.vector.quantize_mx(w2_codes[b][:].bitcast(FP8X4), w2_scales[b][:], w2_grouped[b][:])
 
         v2 = {}
 
@@ -151,19 +182,13 @@ def tile_list_soft_gripper_valves_kernel(
                 v2[jh][:].bitcast(U16), tab2_w[:].bitcast(U16).indirect(idx2[:, 32 * jh : 32 * (jh + 1)])
             )
 
-        h = {}
-        h_codes = {}
-        h_scales = {}
-        for b, lo, width in ((0, 0, HALF), (0, HALF, HALF), (1, 0, HALF), (1, HALF, 256)):
-            h[b, lo] = held([P, width, 4], BF16, "h%d_%d" % (b, lo))
-
-        def grasp_code(b, tiles):
-            for jt in tiles:
+        def grasp_code(h, b, lo, tiles, banks):
+            for jt, number in zip(tiles, banks):
                 jh, jl = divmod(jt, 4)
-                bank = psum_b.tile([P, 4, JT], F32, name="bank_b")
+                sums = bank(number, [P, 4, JT])
                 for t in range(4):
                     nc.tensor.matmul_mx(
-                        bank[:, t, :],
+                        sums[:, t, :],
                         lhsT=w2_codes[b][:, 128 * t : 128 * (t + 1)].bitcast(FP8X4),
                         lhsT_scale=w2_scales[b][:, 128 * t : 128 * (t + 1)],
                         rhs=v2[jh][:, 2 * JT * jl : 2 * JT * (jl + 1)].bitcast(FP4X4),
@@ -172,130 +197,121 @@ def tile_list_soft_gripper_valves_kernel(
                         stop=True,
                     )
                 records = slice(JT * jl, JT * (jl + 1))
-                lo = max(first for (block, first) in h if block == b and first <= JT * jt)
                 nc.vector.tensor_tensor(
-                    h[b, lo][:, JT * jt - lo : JT * (jt + 1) - lo, :].rearrange("p (c i) t -> p c t i", i=2),
-                    bank[:].rearrange("p t (c i) -> p c t i", i=2),
+                    h[:, JT * jt - lo : JT * (jt + 1) - lo, :].rearrange("p (c i) t -> p c t i", i=2),
+                    sums[:].rearrange("p t (c i) -> p c t i", i=2),
                     a_sb[b, jh][:, :, records].rearrange("p t (c i) -> p c t i", i=2),
                     MULT,
                 )
 
-        def quantise_h(b, lo, width):
-            codes = held([P, width], U32, "h_codes%d_%d" % (b, lo))
-            scales = held([P, width], U8, "h_scales%d_%d" % (b, lo))
-            nc.vector.quantize_mx(
-                codes[:].bitcast(FP8X4), scales[:], h[b, lo][:].rearrange("p j t -> p (j t)")
+        h_codes = {}
+        h_scales = {}
+
+        def quantise_h(h, b, lo, codes):
+            width = h.shape[1]
+            h_codes[b, lo] = codes
+            h_scales[b, lo] = held([P, width], U8, "h_scales%d_%d" % (b, lo))
+            nc.vector.quantize_mx(codes[:].bitcast(FP8X4), h_scales[b, lo][:], h[:].rearrange("p j t -> p (j t)"))
+
+        def valve_pass(sums, weights, scales, b, lo, start, stop):
+            nc.tensor.matmul_mx(
+                sums, lhsT=weights.bitcast(FP8X4), lhsT_scale=scales,
+                rhs=h_codes[b, lo][:].bitcast(FP8X4), rhs_scale=h_scales[b, lo][:], start=start, stop=stop,
             )
-            for off in range(0, width, 256):
-                h_codes[b, lo + off] = codes[:, off:width]
-                h_scales[b, lo + off] = scales[:, off:width]
 
-        def valves(lo, width, pool, tag):
-            gates, drives = [], []
-            for n in range(N // P):
-                if width == HALF:
-                    o_sum = pool.tile([P, HALF], F32, name=tag)[:]
-                    d_sum = pool.tile([P, HALF], F32, name=tag)[:]
-                else:
-                    both = pool.tile([P, 2, width], F32, name=tag)
-                    o_sum, d_sum = both[:, 0, :], both[:, 1, :]
-                for b in range(2):
-                    col = N * b + P * n
-                    nc.tensor.matmul_mx(
-                        o_sum,
-                        lhsT=w4_codes[:, col : col + P].bitcast(FP8X4),
-                        lhsT_scale=w4_scales[:, col : col + P],
-                        rhs=h_codes[b, lo][:, 0:width].bitcast(FP8X4),
-                        rhs_scale=h_scales[b, lo][:, 0:width],
-                        start=(b == 0),
-                        stop=(b == 1 and width == HALF),
-                    )
-                    nc.tensor.matmul_mx(
-                        d_sum,
-                        lhsT=w3_codes[:, b, P * n : P * (n + 1)].bitcast(FP8X4),
-                        lhsT_scale=planes[b][:, W3_AT + P * n : W3_AT + P * (n + 1)],
-                        rhs=h_codes[b, lo][:, 0:width].bitcast(FP8X4),
-                        rhs_scale=h_scales[b, lo][:, 0:width],
-                        start=(b == 0 and width == HALF),
-                        stop=(b == 1),
-                    )
-                if lo == 0 and n == 1:
-                    gate = held([P, width], F32, "held_gate", tag="slot_f")
-                else:
-                    gate = ring.tile([P, width], F32, name="gate")
-                nc.scalar.activation(gate[:], o_sum, SIGMOID)
-                gates.append(gate)
-                drives.append(d_sum)
-            return gates, drives
+        def valve(n, lo, width, banks, gate_tag=None):
+            apart = len(banks) == 2
+            if apart:
+                o_sum, d_sum = bank(banks[0], [P, width])[:], bank(banks[1], [P, width])[:]
+            else:
+                both = bank(banks[0], [P, 2, width])
+                o_sum, d_sum = both[:, 0, :], both[:, 1, :]
+            cols = slice(P * n, P * (n + 1))
+            for b in range(2):
+                valve_pass(o_sum, w4_codes[b][:, cols], w4_scales[b][:, cols], b, lo, b == 0, b == 1 and apart)
+                valve_pass(
+                    d_sum, w3_codes[:, b, cols], planes[b][:, W3_AT + P * n : W3_AT + P * (n + 1)],
+                    b, lo, b == 0 and apart, b == 1,
+                )
+            if gate_tag:
+                gate = held([P, width], F32, "gate_" + gate_tag, tag=gate_tag)
+            else:
+                gate = ring.tile([P, width], F32, name="gate")
+            nc.scalar.activation(gate[:], o_sum, TANH, scale=0.5)
+            return gate, d_sum
 
-        def add_on_gpsimd(result, gated, column):
-            nc.gpsimd.tensor_scalar(result, gated, 1.0, column, MULT, ADD)
+        def gate_drive(width, gate, d_sum):
+            gated = ring.tile([P, width], F32, name="gated")
+            nc.vector.scalar_tensor_tensor(gated[:], gate[:], 1.0, d_sum, ADD, MULT)
+            return gated
 
         def add_on_vector(result, gated, column):
-            nc.vector.tensor_scalar(result, gated, 1.0, column, MULT, ADD)
+            nc.vector.tensor_scalar(result, gated, 0.5, column, MULT, ADD)
 
         def add_on_scalar(result, gated, column):
-            nc.scalar.activation(result, gated, IDENTITY, bias=column)
+            nc.scalar.activation(result, gated, IDENTITY, bias=column, scale=0.5)
 
-        def finish(lo, width, add_bias, gates, drives):
-            for n in range(N // P):
-                gated = ring.tile([P, width], F32, name="gated")
-                nc.vector.tensor_tensor(gated[:], drives[n], gates[n][:], MULT)
-                result = ring.tile([P, width], F32, name="result")
-                add_bias(result[:], gated[:], bias[:, n : n + 1])
-                nc.sync.dma_start(out[P * n : P * (n + 1), lo : lo + width], result[:])
+        def store(n, lo, width, gated, add_bias):
+            result = ring.tile([P, width], F32, name="result")
+            add_bias(result[:], gated[:], bias[:, n : n + 1])
+            nc.sync.dma_start(out[P * n : P * (n + 1), lo : lo + width], result[:])
 
         first_product(0, 0)
-        prepare_w2(0, nc.vector.tensor_copy)
-
-        w3_codes = held([P, 2, N], I32, "w3_codes", tag="slot_a")
-        nc.sync.dma_start(w3_codes[:], w3_words.rearrange("a p c i -> p a (c i)").bitcast(I32))
-        w4_raw = held([P, 2, 4, N], F32, "w4_raw", tag="w2_grouped0")
-        nc.sync.dma_start(
-            w4_raw[:].rearrange("p a i n -> p a (i n)"), w4.rearrange("(a p i) n -> p a (i n)", a=2, i=4)
-        )
-
+        round_w2(w2_first, 0, 0, P, nc.vector.tensor_copy, "p m t i")
+        quantise_w2(0)
         gather_v2(0)
-        grasp_code(0, range(4))
-        first_product(0, 1)
         gather_v2(1)
-        bias = held([P, N // P], F32, "bias", tag="slot_b")
-        with nc.allow_non_contiguous_dma(reason="one bias value a partition"):
-            nc.sync.dma_start(bias[:], bv.rearrange("(c p) -> p c", p=P))
-        grasp_code(0, range(4, 8))
-        prepare_w2(1, nc.scalar.copy)
+        first_product(0, 1)
+        h00 = held([P, HALF, 4], BF16, "h00", tag="h0")
+        grasp_code(h00, 0, 0, range(4), (4, 5, 6, 7))
+        round_w2(w2_late[0], 1, 0, P // 2, nc.scalar.copy, "p m t i")
+        round_w2(w2_late[1], 1, P // 2, P, round_on_gpsimd, "p t m i")
         first_product(1, 0)
-        quantise_h(0, 0, HALF)
-        quantise_h(0, HALF, HALF)
+        h02 = held([P, QUARTER, 4], BF16, "h02")
+        grasp_code(h02, 0, HALF, (4, 5), (4, 5))
+        quantise_w2(1)
 
-        w4_grouped = held([P, 2 * N * 4], BF16, "w4_grouped")
-        for n in range(N // P):
-            nc.gpsimd.tensor_scalar(
-                w4_grouped[:, 4 * P * n : 4 * P * (n + 1)].rearrange("p (n i) -> p n i", i=4),
-                w4_raw[:, 0, :, P * n : P * (n + 1)].rearrange("p i n -> p n i"),
-                1.0, 0.0, MULT, ADD,
-            )
-        nc.scalar.copy(
-            w4_grouped[:, 4 * N : 8 * N].rearrange("p (c n i) -> p c i n", n=4, i=4),
-            w4_raw[:, 1].rearrange("p i (c n) -> p c i n", n=4),
-        )
+        w4_grouped = [held([P, N * 4], BF16, "w4_grouped%d" % b) for b in range(2)]
+        for b in range(2):
+            round_on_gpsimd(w4_grouped[b][:].rearrange("p (n i) -> p n i", i=4), w4_raw[b][:].rearrange("p i n -> p n i"))
+        h10 = held([P, HALF, 4], BF16, "h10", tag="h1")
+        grasp_code(h10, 1, 0, range(4), (6, 7, 4, 5))
         first_product(1, 1)
-        grasp_code(1, range(4))
-        w4_codes = held([P, 2 * N], U32, "w4_codes")
-        w4_scales = held([P, 2 * N], U8, "w4_scales")
-        for lo, hi in ((0, 512), (512, 768)):
-            nc.vector.quantize_mx(
-                w4_codes[:, lo:hi].bitcast(FP8X4), w4_scales[:, lo:hi], w4_grouped[:, 4 * lo : 4 * hi]
-            )
-        quantise_h(1, 0, HALF)
-        first = valves(0, HALF, psum, "bank")
-        grasp_code(1, range(4, 6))
-        quantise_h(1, 512, 256)
-        finish(0, HALF, add_on_scalar, *first)
-        second = valves(512, 256, psum, "bank")
-        h[1, 768] = held([P, 256, 4], BF16, "h1_768", tag="slot_f")
-        grasp_code(1, range(6, 8))
-        quantise_h(1, 768, 256)
-        third = valves(768, 256, psum_b, "bank_b")
-        finish(512, 256, add_on_gpsimd, *second)
-        finish(768, 256, add_on_vector, *third)
+
+        w4_codes = [held([P, N], U32, "w4_codes%d" % b) for b in range(2)]
+        w4_scales = [held([P, N], U8, "w4_scales%d" % b) for b in range(2)]
+
+        def quantise_w4(b):
+            for lo, hi in ((0, 256), (256, N)):
+                nc.vector.quantize_mx(
+                    w4_codes[b][:, lo:hi].bitcast(FP8X4), w4_scales[b][:, lo:hi], w4_grouped[b][:, 4 * lo : 4 * hi]
+                )
+
+        quantise_h(h00, 0, 0, placed([P, HALF], U32, "h_codes00", 38 * KIB))
+        quantise_w4(0)
+        quantise_h(h10, 1, 0, held([P, HALF], U32, "h_codes10"))
+        quantise_w4(1)
+        first = [valve(0, 0, HALF, (7, 0)), valve(1, 0, HALF, (1, 2), "h13")]
+        h03 = held([P, QUARTER, 4], BF16, "h03", tag="h0")
+        grasp_code(h03, 0, 768, (6, 7), (6, 4))
+        first.append(valve(2, 0, HALF, (3, 6)))
+        h12 = held([P, QUARTER, 4], BF16, "h12", tag="h1")
+        grasp_code(h12, 1, HALF, (4,), (5,))
+        quantise_h(h02, 0, HALF, placed([P, QUARTER], U32, "h_codes02", 40 * KIB))
+        quantise_h(h03, 0, 768, held([P, QUARTER], U32, "h_codes03"))
+        grasp_code(h12, 1, HALF, (5,), (7,))
+        store(0, 0, HALF, gate_drive(HALF, *first[0]), add_on_scalar)
+        quantise_h(h12, 1, HALF, held([P, QUARTER], U32, "h_codes12"))
+        store(1, 0, HALF, gate_drive(HALF, *first[1]), add_on_scalar)
+        h13 = held([P, QUARTER, 4], BF16, "h13")
+        grasp_code(h13, 1, 768, (6,), (1,))
+        second = [valve(n, HALF, QUARTER, (number,)) for n, number in enumerate((4, 5, 7))]
+        grasp_code(h13, 1, 768, (7,), (3,))
+        store(2, 0, HALF, gate_drive(HALF, *first[2]), add_on_scalar)
+        quantise_h(h13, 1, 768, held([P, QUARTER], U32, "h_codes13"))
+        third = [valve(n, 768, QUARTER, (number,)) for n, number in enumerate((0, 2, 6))]
+        for n in range(N // P):
+            store(n, HALF, QUARTER, gate_drive(QUARTER, *second[n]), add_on_scalar)
+        gated = [gate_drive(QUARTER, *third[n]) for n in range(N // P)]
+        for n in range(N // P):
+            store(n, 768, QUARTER, gated[n], add_on_vector)

@@ -36,7 +36,7 @@ def tile_list_soft_gripper_valves_kernel(
         lists = ctx.enter_context(tc.tile_pool(name="lists", bufs=1))
         keep = ctx.enter_context(tc.tile_pool(name="keep", bufs=1))
         laid = ctx.enter_context(tc.tile_pool(name="laid", bufs=1))
-        ring = ctx.enter_context(tc.tile_pool(name="ring", bufs=6))
+        ring = ctx.enter_context(tc.tile_pool(name="ring", bufs=9))
         psum = ctx.enter_context(tc.psum_pool(name="psum", bufs=1))
 
         def held(shape, dtype, name, tag=None):
@@ -124,7 +124,7 @@ def tile_list_soft_gripper_valves_kernel(
             nc.sync.dma_start(
                 w2_late[u][:], w2[:, HALF + QUARTER * u : HALF + QUARTER * (u + 1)].rearrange("(p i) c -> p i c", i=4)
             )
-        w4_raw = [placed([P, 4, N], F32, "w4_raw%d" % b, at * KIB + 256) for b, at in enumerate((28, 37))]
+        w4_raw = [placed([P, 4, N], F32, "w4_raw%d" % b, at * KIB + 256) for b, at in enumerate((39, 28))]
         for b in range(2):
             nc.sync.dma_start(
                 w4_raw[b][:].rearrange("p i n -> p (i n)"),
@@ -139,8 +139,8 @@ def tile_list_soft_gripper_valves_kernel(
         a_sb = {}
 
         def first_product(b, jh):
-            if (b, jh) == (1, 0):
-                a_sb[b, jh] = placed([P, 4, HALF], F32, "a_sb10", 16 * KIB)
+            if b == 1:
+                a_sb[b, jh] = placed([P, 4, HALF], F32, "a_sb1%d" % jh, (16, 44)[jh] * KIB)
             else:
                 a_sb[b, jh] = held([P, 4, HALF], F32, "a_sb%d%d" % (b, jh))
             for t in range(4):
@@ -207,11 +207,16 @@ def tile_list_soft_gripper_valves_kernel(
         h_codes = {}
         h_scales = {}
 
-        def quantise_h(h, b, lo, codes):
+        def quantise_h(h, b, lo, scales_at=None):
             width = h.shape[1]
-            h_codes[b, lo] = codes
-            h_scales[b, lo] = held([P, width], U8, "h_scales%d_%d" % (b, lo))
-            nc.vector.quantize_mx(codes[:].bitcast(FP8X4), h_scales[b, lo][:], h[:].rearrange("p j t -> p (j t)"))
+            h_codes[b, lo] = held([P, width], U32, "h_codes%d_%d" % (b, lo))
+            if scales_at:
+                h_scales[b, lo] = placed([P, width], U8, "h_scales%d_%d" % (b, lo), scales_at)
+            else:
+                h_scales[b, lo] = held([P, width], U8, "h_scales%d_%d" % (b, lo))
+            nc.vector.quantize_mx(
+                h_codes[b, lo][:].bitcast(FP8X4), h_scales[b, lo][:], h[:].rearrange("p j t -> p (j t)")
+            )
 
         def valve_pass(sums, weights, scales, b, lo, start, stop):
             nc.tensor.matmul_mx(
@@ -245,8 +250,8 @@ def tile_list_soft_gripper_valves_kernel(
             nc.vector.scalar_tensor_tensor(gated[:], gate[:], 1.0, d_sum, ADD, MULT)
             return gated
 
-        def add_on_vector(result, gated, column):
-            nc.vector.tensor_scalar(result, gated, 0.5, column, MULT, ADD)
+        def add_on_gpsimd(result, gated, column):
+            nc.gpsimd.tensor_scalar(result, gated, 0.5, column, MULT, ADD)
 
         def add_on_scalar(result, gated, column):
             nc.scalar.activation(result, gated, IDENTITY, bias=column, scale=0.5)
@@ -271,15 +276,18 @@ def tile_list_soft_gripper_valves_kernel(
         grasp_code(h02, 0, HALF, (4, 5), (4, 5))
         quantise_w2(1)
 
-        w4_grouped = [held([P, N * 4], BF16, "w4_grouped%d" % b) for b in range(2)]
-        for b in range(2):
-            round_on_gpsimd(w4_grouped[b][:].rearrange("p (n i) -> p n i", i=4), w4_raw[b][:].rearrange("p i n -> p n i"))
+        w4_grouped = [held([P, N * 4], BF16, "w4_grouped0"), held([P, N * 4], BF16, "w4_grouped1", tag="w2_grouped1")]
+        nc.scalar.copy(
+            w4_grouped[0][:].rearrange("p (c n i) -> p c i n", n=4, i=4),
+            w4_raw[0][:].rearrange("p i (c n) -> p c i n", n=4),
+        )
+        round_on_gpsimd(w4_grouped[1][:].rearrange("p (n i) -> p n i", i=4), w4_raw[1][:].rearrange("p i n -> p n i"))
         h10 = held([P, HALF, 4], BF16, "h10", tag="h1")
         grasp_code(h10, 1, 0, range(4), (6, 7, 4, 5))
         first_product(1, 1)
 
         w4_codes = [held([P, N], U32, "w4_codes%d" % b) for b in range(2)]
-        w4_scales = [held([P, N], U8, "w4_scales%d" % b) for b in range(2)]
+        w4_scales = [placed([P, N], U8, "w4_scales0", 32 * KIB), held([P, N], U8, "w4_scales1")]
 
         def quantise_w4(b):
             for lo, hi in ((0, 256), (256, N)):
@@ -287,9 +295,9 @@ def tile_list_soft_gripper_valves_kernel(
                     w4_codes[b][:, lo:hi].bitcast(FP8X4), w4_scales[b][:, lo:hi], w4_grouped[b][:, 4 * lo : 4 * hi]
                 )
 
-        quantise_h(h00, 0, 0, placed([P, HALF], U32, "h_codes00", 38 * KIB))
+        quantise_h(h00, 0, 0, 29 * KIB)
         quantise_w4(0)
-        quantise_h(h10, 1, 0, held([P, HALF], U32, "h_codes10"))
+        quantise_h(h10, 1, 0, 30 * KIB)
         quantise_w4(1)
         first = [valve(0, 0, HALF, (7, 0)), valve(1, 0, HALF, (1, 2), "h13")]
         h03 = held([P, QUARTER, 4], BF16, "h03", tag="h0")
@@ -297,21 +305,20 @@ def tile_list_soft_gripper_valves_kernel(
         first.append(valve(2, 0, HALF, (3, 6)))
         h12 = held([P, QUARTER, 4], BF16, "h12", tag="h1")
         grasp_code(h12, 1, HALF, (4,), (5,))
-        quantise_h(h02, 0, HALF, placed([P, QUARTER], U32, "h_codes02", 40 * KIB))
-        quantise_h(h03, 0, 768, held([P, QUARTER], U32, "h_codes03"))
+        quantise_h(h02, 0, HALF, 31 * KIB)
+        quantise_h(h03, 0, 768)
         grasp_code(h12, 1, HALF, (5,), (7,))
         store(0, 0, HALF, gate_drive(HALF, *first[0]), add_on_scalar)
-        quantise_h(h12, 1, HALF, held([P, QUARTER], U32, "h_codes12"))
+        quantise_h(h12, 1, HALF)
         store(1, 0, HALF, gate_drive(HALF, *first[1]), add_on_scalar)
         h13 = held([P, QUARTER, 4], BF16, "h13")
         grasp_code(h13, 1, 768, (6,), (1,))
         second = [valve(n, HALF, QUARTER, (number,)) for n, number in enumerate((4, 5, 7))]
         grasp_code(h13, 1, 768, (7,), (3,))
         store(2, 0, HALF, gate_drive(HALF, *first[2]), add_on_scalar)
-        quantise_h(h13, 1, 768, held([P, QUARTER], U32, "h_codes13"))
+        quantise_h(h13, 1, 768)
         third = [valve(n, 768, QUARTER, (number,)) for n, number in enumerate((0, 2, 6))]
         for n in range(N // P):
-            store(n, HALF, QUARTER, gate_drive(QUARTER, *second[n]), add_on_scalar)
-        gated = [gate_drive(QUARTER, *third[n]) for n in range(N // P)]
+            store(n, HALF, QUARTER, gate_drive(QUARTER, *second[n]), add_on_gpsimd)
         for n in range(N // P):
-            store(n, 768, QUARTER, gated[n], add_on_vector)
+            store(n, 768, QUARTER, gate_drive(QUARTER, *third[n]), add_on_scalar)

@@ -86,10 +86,10 @@ def tile_list_soft_gripper_valves_kernel(
         nc.vector.tensor_copy(staged[:, TAB_AT:W1_AT].bitcast(I32), tab_picked[:].bitcast(I32))
 
         def move_rows(queue, a, width):
-            for q in range(4):
+            for r in range(4):
                 queue.dma_start(
-                    planes[a][32 * q : 32 * q + 4, :].bitcast(I32),
-                    staged[96 + 16 * a + 4 * q : 96 + 16 * a + 4 * q + 4, 0:width].bitcast(I32),
+                    planes[a][r:P:32, :].bitcast(I32),
+                    staged[96 + 16 * a + r : 96 + 16 * (a + 1) : 4, 0:width].bitcast(I32),
                 )
 
         move_rows(nc.sync, 0, TAB2_AT)

@@ -23,8 +23,10 @@ HALF = 512
 QUARTER = 256
 JT = 128
 KIB = 1024
-TAB_AT, W1_AT, W3_AT, TAB2_AT = 0, S, S + H, S + H + N
-STAGED = S + H + N + S
+TAB_AT, W1_AT, LATE_AT = 0, S, S + HALF
+W3_AT = LATE_AT + 2 * HALF
+TAB2_AT = W3_AT + 2 * N
+STAGED = TAB2_AT + S
 
 
 def tile_list_soft_gripper_valves_kernel(
@@ -53,51 +55,64 @@ def tile_list_soft_gripper_valves_kernel(
 
         tab_rows = held([P, T], U8, "tab_rows")
         tab2_rows = held([P, T], U8, "tab2_rows")
-        w1_rows = held([P, H], U8, "w1_rows")
+        w1_rows = held([P, 3 * HALF], U8, "w1_rows")
         staged = held([P, STAGED], U8, "staged")
-        planes = [held([P, TAB2_AT], U8, "planes0"), held([P, STAGED], U8, "planes1")]
+        planes = [held([P, LATE_AT], U8, "planes%d" % a) for a in range(2)]
 
-        nc.vector.memset(w1_rows[0:96, :].bitcast(I32), 0)
+        nc.vector.memset(w1_rows[0:96, 0:HALF].bitcast(I32), 0)
         nc.vector.memset(tab_rows[0:96, :].bitcast(I32), 0)
+        nc.vector.memset(w1_rows[0:112, HALF : 3 * HALF].bitcast(I32), 0)
         nc.vector.memset(tab2_rows[0:112, :].bitcast(I32), 0)
         for plane in planes:
             nc.gpsimd.memset(plane[:].bitcast(I32), 0)
 
         tab_w = [placed([P, T], I32, "tab_w0", 0), None]
         w1_raw = held([P, 2, H // 2], I32, "w1_raw", tag="slot_a")
-        nc.sync.dma_start(w1_rows[96:128, :].bitcast(I32), w1_scales.rearrange("a q c -> (a q) c").bitcast(I32))
+        w1_scale_words = w1_scales.bitcast(I32)
+        nc.sync.dma_start(
+            w1_rows[96:128, 0:HALF].bitcast(I32), w1_scale_words.rearrange("a q c -> (a q) c")[:, 0 : HALF // 4]
+        )
         nc.sync.dma_start(idx[:], offs)
         nc.sync.dma_start(tab_rows[96:128, :].bitcast(I32), tab_scales.rearrange("a q t -> (a q) t").bitcast(I32))
         nc.sync.dma_start(
-            staged[96:128, W3_AT:TAB2_AT].bitcast(I32), w3_scales.rearrange("a q c -> (a q) c").bitcast(I32)
+            w1_rows[112:128, HALF : 3 * HALF].bitcast(I32).rearrange("q (a c) -> q a c", a=2),
+            w1_scale_words.rearrange("a q c -> q a c")[:, :, HALF // 4 : H // 4],
         )
         nc.sync.dma_start(idx2[:], offs2)
         nc.sync.dma_start(tab2_rows[112:128, :].bitcast(I32), tab2_scales[0].bitcast(I32))
         nc.sync.dma_start(tab_w[0][:], tab_words[0].rearrange("p t i -> p (t i)").bitcast(I32))
         nc.sync.dma_start(w1_raw[:], w1_words.bitcast(I32).rearrange("a p w -> p a w"))
+        nc.sync.dma_start(
+            staged[112:128, W3_AT:TAB2_AT].bitcast(I32).rearrange("q (a c) -> q a c", a=2),
+            w3_scales.bitcast(I32).rearrange("a q c -> q a c"),
+        )
 
         tab_picked = placed([P, S], U8, "tab_picked", 24 * KIB)
         tab2_picked = held([P, S], U8, "tab2_picked", tag="slot_b")
-        nc.vector.tensor_copy(
-            staged[:, W1_AT:W3_AT].rearrange("p (b t c i) -> p b c t i", b=2, t=4, i=16),
-            w1_rows[:].rearrange("p (b c i t) -> p b c t i", b=2, t=4, i=16),
-        )
+
+        def deal_w1_scales(lo, hi):
+            nc.vector.tensor_copy(
+                staged[:, W1_AT + lo : W1_AT + hi].rearrange("p (b t c i) -> p c b t i", c=8, t=4, i=16),
+                w1_rows[:, lo:hi].rearrange("p (b c i t) -> p c b t i", c=8, t=4, i=16),
+            )
+
+        deal_w1_scales(0, HALF)
         nc.vector.tensor_copy(tab_picked[:], tab_rows[:].indirect(idx[:]))
         nc.vector.tensor_copy(staged[:, TAB_AT:W1_AT].bitcast(I32), tab_picked[:].bitcast(I32))
 
-        def move_rows(queue, a, width):
+        def move_rows(plane, first, lo, hi):
             for r in range(4):
-                queue.dma_start(
-                    planes[a][r:P:32, :].bitcast(I32),
-                    staged[96 + 16 * a + r : 96 + 16 * (a + 1) : 4, 0:width].bitcast(I32),
+                nc.sync.dma_start(
+                    plane[r:P:32, :].bitcast(I32), staged[first + r : first + 16 : 4, lo:hi].bitcast(I32)
                 )
 
-        move_rows(nc.sync, 0, TAB2_AT)
+        move_rows(planes[0], 96, 0, LATE_AT)
         tab_w[1] = placed([P, T], I32, "tab_w1", 24 * KIB)
         nc.sync.dma_start(tab_w[1][:], tab_words[1].rearrange("p t i -> p (t i)").bitcast(I32))
+        move_rows(planes[1], 112, 0, LATE_AT)
+        deal_w1_scales(HALF, 3 * HALF)
         nc.vector.tensor_copy(tab2_picked[:], tab2_rows[:].indirect(idx2[:]))
         nc.vector.tensor_copy(staged[:, TAB2_AT:STAGED].bitcast(I32), tab2_picked[:].bitcast(I32))
-        move_rows(nc.sync, 1, STAGED)
 
         v = {}
 
@@ -112,6 +127,8 @@ def tile_list_soft_gripper_valves_kernel(
             w1_raw[:].rearrange("p a w -> p (a w)").bitcast(U16).rearrange("p (g c i t) -> p g c t i", g=4, t=4, i=8),
         )
         gather_v(0, 1)
+        late = placed([P, STAGED - LATE_AT], U8, "late", 8 * KIB)
+        nc.gpsimd.memset(late[:].bitcast(I32), 0)
         gather_v(1, 0)
         gather_v(1, 1)
 
@@ -119,6 +136,16 @@ def tile_list_soft_gripper_valves_kernel(
         nc.sync.dma_start(w2_first[:], w2[:, 0:HALF].rearrange("(p i) c -> p i c", i=4))
         tab2_w = placed([P, T // 2], I32, "tab2_w", 0)
         nc.sync.dma_start(tab2_w[:], tab2_words[0].bitcast(I32))
+        move_rows(late, 112, LATE_AT, STAGED)
+
+        def late_scales(lo, width):
+            return late[:, lo - LATE_AT : lo - LATE_AT + width]
+
+        def w1_scales_of(a, b, t):
+            if b == 0:
+                return planes[a][:, W1_AT + P * t : W1_AT + P * (t + 1)]
+            return late_scales(LATE_AT + HALF * a + P * t, P)
+
         w2_late = [placed([P, 4, QUARTER], F32, "w2_late%d" % u, (20, 24)[u] * KIB + (64, 256)[u]) for u in range(2)]
         for u in range(2):
             nc.sync.dma_start(
@@ -150,7 +177,7 @@ def tile_list_soft_gripper_valves_kernel(
                     nc.tensor.matmul_mx(
                         sums[:],
                         lhsT=w1_codes[:, 2 * (H * a + col) : 2 * (H * a + col + 128)].bitcast(FP4X4),
-                        lhsT_scale=planes[a][:, W1_AT + col : W1_AT + col + 128],
+                        lhsT_scale=w1_scales_of(a, b, t),
                         rhs=v[a, jh][:].bitcast(FP8X4),
                         rhs_scale=planes[a][:, TAB_AT + HALF * jh : TAB_AT + HALF * (jh + 1)],
                         start=(a == 0),
@@ -158,7 +185,7 @@ def tile_list_soft_gripper_valves_kernel(
                     )
                 nc.scalar.copy(a_sb[b, jh][:, t, :], sums[:])
 
-        w2_grouped = [held([P, 4 * HALF], BF16, "w2_grouped%d" % b) for b in range(2)]
+        w2_grouped = [held([P, 4 * HALF], BF16, "w2_grouped0"), placed([P, 4 * HALF], BF16, "w2_grouped1", 52 * KIB)]
         w2_codes = [held([P, HALF], U32, "w2_codes%d" % b) for b in range(2)]
         w2_scales = [held([P, HALF], U8, "w2_scales%d" % b) for b in range(2)]
 
@@ -192,7 +219,7 @@ def tile_list_soft_gripper_valves_kernel(
                         lhsT=w2_codes[b][:, 128 * t : 128 * (t + 1)].bitcast(FP8X4),
                         lhsT_scale=w2_scales[b][:, 128 * t : 128 * (t + 1)],
                         rhs=v2[jh][:, 2 * JT * jl : 2 * JT * (jl + 1)].bitcast(FP4X4),
-                        rhs_scale=planes[1][:, TAB2_AT + JT * jt : TAB2_AT + JT * (jt + 1)],
+                        rhs_scale=late_scales(TAB2_AT + JT * jt, JT),
                         start=True,
                         stop=True,
                     )
@@ -235,7 +262,7 @@ def tile_list_soft_gripper_valves_kernel(
             for b in range(2):
                 valve_pass(o_sum, w4_codes[b][:, cols], w4_scales[b][:, cols], b, lo, b == 0, b == 1 and apart)
                 valve_pass(
-                    d_sum, w3_codes[:, b, cols], planes[b][:, W3_AT + P * n : W3_AT + P * (n + 1)],
+                    d_sum, w3_codes[:, b, cols], late_scales(W3_AT + N * b + P * n, P),
                     b, lo, b == 0 and apart, b == 1,
                 )
             if gate_tag:
@@ -272,11 +299,11 @@ def tile_list_soft_gripper_valves_kernel(
         round_w2(w2_late[0], 1, 0, P // 2, nc.scalar.copy, "p m t i")
         round_w2(w2_late[1], 1, P // 2, P, round_on_gpsimd, "p t m i")
         first_product(1, 0)
-        h02 = held([P, QUARTER, 4], BF16, "h02")
-        grasp_code(h02, 0, HALF, (4, 5), (4, 5))
         quantise_w2(1)
+        h02 = placed([P, QUARTER, 4], BF16, "h02", 52 * KIB)
+        grasp_code(h02, 0, HALF, (4, 5), (4, 5))
 
-        w4_grouped = [held([P, N * 4], BF16, "w4_grouped0"), held([P, N * 4], BF16, "w4_grouped1", tag="w2_grouped1")]
+        w4_grouped = [held([P, N * 4], BF16, "w4_grouped0"), placed([P, N * 4], BF16, "w4_grouped1", 54 * KIB)]
         nc.scalar.copy(
             w4_grouped[0][:].rearrange("p (c n i) -> p c i n", n=4, i=4),
             w4_raw[0][:].rearrange("p i (c n) -> p c i n", n=4),

@@ -163,15 +163,11 @@ def tile_list_soft_gripper_valves_kernel(
         with nc.allow_non_contiguous_dma(reason="one bias value a partition"):
             nc.sync.dma_start(bias[:], bv.rearrange("(c p) -> p c", p=P))
 
-        a_sb = {}
+        a_sb, a_sums = {}, {}
 
-        def first_product(b, jh):
-            if b == 1:
-                a_sb[b, jh] = placed([P, 4, HALF], F32, "a_sb1%d" % jh, (16, 44)[jh] * KIB)
-            else:
-                a_sb[b, jh] = held([P, 4, HALF], F32, "a_sb%d%d" % (b, jh))
-            for t in range(4):
-                sums = bank(t, [P, HALF])
+        def first_passes(b, jh, slots):
+            for t in slots:
+                sums = a_sums[b, jh, t] = bank(t, [P, HALF])
                 col = 512 * b + 128 * t
                 for a in range(2):
                     nc.tensor.matmul_mx(
@@ -183,7 +179,18 @@ def tile_list_soft_gripper_valves_kernel(
                         start=(a == 0),
                         stop=(a == 1),
                     )
-                nc.scalar.copy(a_sb[b, jh][:, t, :], sums[:])
+
+        def first_copies(b, jh):
+            if b == 1:
+                a_sb[b, jh] = placed([P, 4, HALF], F32, "a_sb1%d" % jh, (16, 44)[jh] * KIB)
+            else:
+                a_sb[b, jh] = held([P, 4, HALF], F32, "a_sb%d%d" % (b, jh))
+            for t in range(4):
+                nc.scalar.copy(a_sb[b, jh][:, t, :], a_sums[b, jh, t][:])
+
+        def first_product(b, jh):
+            first_passes(b, jh, range(4))
+            first_copies(b, jh)
 
         w2_grouped = [held([P, 4 * HALF], BF16, "w2_grouped0"), placed([P, 4 * HALF], BF16, "w2_grouped1", 52 * KIB)]
         w2_codes = [held([P, HALF], U32, "w2_codes%d" % b) for b in range(2)]
@@ -294,11 +301,13 @@ def tile_list_soft_gripper_valves_kernel(
         gather_v2(0)
         gather_v2(1)
         first_product(0, 1)
+        first_passes(1, 0, (0, 1))
         h00 = held([P, HALF, 4], BF16, "h00", tag="h0")
         grasp_code(h00, 0, 0, range(4), (4, 5, 6, 7))
+        first_passes(1, 0, (2, 3))
         round_w2(w2_late[0], 1, 0, P // 2, nc.scalar.copy, "p m t i")
         round_w2(w2_late[1], 1, P // 2, P, round_on_gpsimd, "p t m i")
-        first_product(1, 0)
+        first_copies(1, 0)
         quantise_w2(1)
         h02 = placed([P, QUARTER, 4], BF16, "h02", 52 * KIB)
         grasp_code(h02, 0, HALF, (4, 5), (4, 5))

@@ -267,7 +267,8 @@ def tile_list_soft_gripper_valves_kernel(
                 o_sum, d_sum = both[:, 0, :], both[:, 1, :]
             cols = slice(P * n, P * (n + 1))
             for b in range(2):
-                valve_pass(o_sum, w4_codes[b][:, cols], w4_scales[b][:, cols], b, lo, b == 0, b == 1 and apart)
+                w4_cols = slice(N * b + P * n, N * b + P * (n + 1))
+                valve_pass(o_sum, w4_codes[:, w4_cols], w4_scales[:, w4_cols], b, lo, b == 0, b == 1 and apart)
                 valve_pass(
                     d_sum, w3_codes[:, b, cols], late_scales(W3_AT + N * b + P * n, P),
                     b, lo, b == 0 and apart, b == 1,
@@ -302,43 +303,39 @@ def tile_list_soft_gripper_valves_kernel(
         gather_v2(1)
         first_product(0, 1)
         first_passes(1, 0, (0, 1))
-        h00 = held([P, HALF, 4], BF16, "h00", tag="h0")
+        h00 = held([P, HALF, 4], BF16, "h00")
         grasp_code(h00, 0, 0, range(4), (4, 5, 6, 7))
         first_passes(1, 0, (2, 3))
         round_w2(w2_late[0], 1, 0, P // 2, nc.scalar.copy, "p m t i")
         round_w2(w2_late[1], 1, P // 2, P, round_on_gpsimd, "p t m i")
         first_copies(1, 0)
-        quantise_w2(1)
-        h02 = placed([P, QUARTER, 4], BF16, "h02", 52 * KIB)
+        h02 = held([P, QUARTER, 4], BF16, "h02")
         grasp_code(h02, 0, HALF, (4, 5), (4, 5))
+        quantise_w2(1)
+        h03 = placed([P, QUARTER, 4], BF16, "h03", 52 * KIB)
+        grasp_code(h03, 0, 768, (6,), (6,))
 
-        w4_grouped = [held([P, N * 4], BF16, "w4_grouped0"), placed([P, N * 4], BF16, "w4_grouped1", 54 * KIB)]
-        nc.scalar.copy(
-            w4_grouped[0][:].rearrange("p (c n i) -> p c i n", n=4, i=4),
-            w4_raw[0][:].rearrange("p i (c n) -> p c i n", n=4),
-        )
-        round_on_gpsimd(w4_grouped[1][:].rearrange("p (n i) -> p n i", i=4), w4_raw[1][:].rearrange("p i n -> p n i"))
+        w4_first = held([P, 4 * HALF], BF16, "w4_first")
+        w4_rest = placed([P, 4 * QUARTER], BF16, "w4_rest", 54 * KIB)
+        for b, lo, width in ((0, 0, N), (1, N, P)):
+            nc.scalar.copy(
+                w4_first[:, 4 * lo : 4 * (lo + width)].rearrange("p (c n i) -> p c i n", n=4, i=4),
+                w4_raw[b][:, :, 0:width].rearrange("p i (c n) -> p c i n", n=4),
+            )
+        round_on_gpsimd(w4_rest[:].rearrange("p (n i) -> p n i", i=4), w4_raw[1][:, :, P:N].rearrange("p i n -> p n i"))
         h10 = held([P, HALF, 4], BF16, "h10", tag="h1")
-        grasp_code(h10, 1, 0, range(4), (6, 7, 4, 5))
+        grasp_code(h10, 1, 0, range(4), (7, 4, 5, 6))
         first_product(1, 1)
 
-        w4_codes = [held([P, N], U32, "w4_codes%d" % b) for b in range(2)]
-        w4_scales = [placed([P, N], U8, "w4_scales0", 32 * KIB), held([P, N], U8, "w4_scales1")]
-
-        def quantise_w4(b):
-            for lo, hi in ((0, 256), (256, N)):
-                nc.vector.quantize_mx(
-                    w4_codes[b][:, lo:hi].bitcast(FP8X4), w4_scales[b][:, lo:hi], w4_grouped[b][:, 4 * lo : 4 * hi]
-                )
-
+        w4_codes = held([P, 2 * N], U32, "w4_codes")
+        w4_scales = placed([P, 2 * N], U8, "w4_scales", 32 * KIB)
         quantise_h(h00, 0, 0, 29 * KIB)
-        quantise_w4(0)
+        nc.vector.quantize_mx(w4_codes[:, 0:HALF].bitcast(FP8X4), w4_scales[:, 0:HALF], w4_first[:])
         quantise_h(h10, 1, 0, 30 * KIB)
-        quantise_w4(1)
+        nc.vector.quantize_mx(w4_codes[:, HALF : 2 * N].bitcast(FP8X4), w4_scales[:, HALF : 2 * N], w4_rest[:])
         first = [valve(0, 0, HALF, (7, 0)), valve(1, 0, HALF, (1, 2), "h13")]
-        h03 = held([P, QUARTER, 4], BF16, "h03", tag="h0")
-        grasp_code(h03, 0, 768, (6, 7), (6, 4))
-        first.append(valve(2, 0, HALF, (3, 6)))
+        grasp_code(h03, 0, 768, (7,), (6,))
+        first.append(valve(2, 0, HALF, (3, 4)))
         h12 = held([P, QUARTER, 4], BF16, "h12", tag="h1")
         grasp_code(h12, 1, HALF, (4,), (5,))
         quantise_h(h02, 0, HALF, 31 * KIB)
@@ -349,11 +346,11 @@ def tile_list_soft_gripper_valves_kernel(
         store(1, 0, HALF, gate_drive(HALF, *first[1]), add_on_scalar)
         h13 = held([P, QUARTER, 4], BF16, "h13")
         grasp_code(h13, 1, 768, (6,), (1,))
-        second = [valve(n, HALF, QUARTER, (number,)) for n, number in enumerate((4, 5, 7))]
+        second = [valve(n, HALF, QUARTER, (number,)) for n, number in enumerate((6, 5, 7))]
         grasp_code(h13, 1, 768, (7,), (3,))
         store(2, 0, HALF, gate_drive(HALF, *first[2]), add_on_scalar)
         quantise_h(h13, 1, 768)
-        third = [valve(n, 768, QUARTER, (number,)) for n, number in enumerate((0, 2, 6))]
+        third = [valve(n, 768, QUARTER, (number,)) for n, number in enumerate((0, 2, 4))]
         for n in range(N // P):
             store(n, HALF, QUARTER, gate_drive(QUARTER, *second[n]), add_on_gpsimd)
         for n in range(N // P):

@@ -69,23 +69,23 @@ def tile_list_soft_gripper_valves_kernel(
         tab_w = [placed([P, T], I32, "tab_w0", 0), None]
         w1_raw = held([P, 2, H // 2], I32, "w1_raw", tag="slot_a")
         w1_scale_words = w1_scales.bitcast(I32)
-        nc.sync.dma_start(
+        nc.sync.dma_start(idx[:], offs)
+        nc.scalar.dma_start(
             w1_rows[96:128, 0:HALF].bitcast(I32), w1_scale_words.rearrange("a q c -> (a q) c")[:, 0 : HALF // 4]
         )
-        nc.sync.dma_start(idx[:], offs)
-        nc.sync.dma_start(tab_rows[96:128, :].bitcast(I32), tab_scales.rearrange("a q t -> (a q) t").bitcast(I32))
-        nc.sync.dma_start(
-            w1_rows[112:128, HALF : 3 * HALF].bitcast(I32).rearrange("q (a c) -> q a c", a=2),
-            w1_scale_words.rearrange("a q c -> q a c")[:, :, HALF // 4 : H // 4],
-        )
         nc.sync.dma_start(idx2[:], offs2)
-        nc.sync.dma_start(tab2_rows[112:128, :].bitcast(I32), tab2_scales[0].bitcast(I32))
-        nc.sync.dma_start(tab_w[0][:], tab_words[0].rearrange("p t i -> p (t i)").bitcast(I32))
-        nc.sync.dma_start(w1_raw[:], w1_words.bitcast(I32).rearrange("a p w -> p a w"))
+        nc.scalar.dma_start(tab_rows[96:128, :].bitcast(I32), tab_scales.rearrange("a q t -> (a q) t").bitcast(I32))
         nc.sync.dma_start(
             staged[112:128, W3_AT:TAB2_AT].bitcast(I32).rearrange("q (a c) -> q a c", a=2),
             w3_scales.bitcast(I32).rearrange("a q c -> q a c"),
         )
+        nc.scalar.dma_start(
+            w1_rows[112:128, HALF : 3 * HALF].bitcast(I32).rearrange("q (a c) -> q a c", a=2),
+            w1_scale_words.rearrange("a q c -> q a c")[:, :, HALF // 4 : H // 4],
+        )
+        nc.sync.dma_start(tab_w[0][:], tab_words[0].rearrange("p t i -> p (t i)").bitcast(I32))
+        nc.scalar.dma_start(tab2_rows[112:128, :].bitcast(I32), tab2_scales[0].bitcast(I32))
+        nc.sync.dma_start(w1_raw[:], w1_words.bitcast(I32).rearrange("a p w -> p a w"))
 
         tab_picked = placed([P, S], U8, "tab_picked", 24 * KIB)
         tab2_picked = held([P, S], U8, "tab2_picked", tag="slot_b")

@@ -70,21 +70,21 @@ def tile_list_soft_gripper_valves_kernel(
         w1_raw = held([P, 2, H // 2], I32, "w1_raw", tag="slot_a")
         w1_scale_words = w1_scales.bitcast(I32)
         nc.sync.dma_start(idx[:], offs)
-        nc.scalar.dma_start(
+        nc.sync.dma_start(
             w1_rows[96:128, 0:HALF].bitcast(I32), w1_scale_words.rearrange("a q c -> (a q) c")[:, 0 : HALF // 4]
         )
+        nc.sync.dma_start(tab_rows[96:128, :].bitcast(I32), tab_scales.rearrange("a q t -> (a q) t").bitcast(I32))
         nc.sync.dma_start(idx2[:], offs2)
-        nc.scalar.dma_start(tab_rows[96:128, :].bitcast(I32), tab_scales.rearrange("a q t -> (a q) t").bitcast(I32))
+        nc.sync.dma_start(tab2_rows[112:128, :].bitcast(I32), tab2_scales[0].bitcast(I32))
+        nc.sync.dma_start(
+            w1_rows[112:128, HALF : 3 * HALF].bitcast(I32).rearrange("q (a c) -> q a c", a=2),
+            w1_scale_words.rearrange("a q c -> q a c")[:, :, HALF // 4 : H // 4],
+        )
         nc.sync.dma_start(
             staged[112:128, W3_AT:TAB2_AT].bitcast(I32).rearrange("q (a c) -> q a c", a=2),
             w3_scales.bitcast(I32).rearrange("a q c -> q a c"),
         )
-        nc.scalar.dma_start(
-            w1_rows[112:128, HALF : 3 * HALF].bitcast(I32).rearrange("q (a c) -> q a c", a=2),
-            w1_scale_words.rearrange("a q c -> q a c")[:, :, HALF // 4 : H // 4],
-        )
         nc.sync.dma_start(tab_w[0][:], tab_words[0].rearrange("p t i -> p (t i)").bitcast(I32))
-        nc.scalar.dma_start(tab2_rows[112:128, :].bitcast(I32), tab2_scales[0].bitcast(I32))
         nc.sync.dma_start(w1_raw[:], w1_words.bitcast(I32).rearrange("a p w -> p a w"))
 
         tab_picked = placed([P, S], U8, "tab_picked", 24 * KIB)
@@ -151,7 +151,7 @@ def tile_list_soft_gripper_valves_kernel(
             nc.sync.dma_start(
                 w2_late[u][:], w2[:, HALF + QUARTER * u : HALF + QUARTER * (u + 1)].rearrange("(p i) c -> p i c", i=4)
             )
-        w4_raw = [placed([P, 4, N], F32, "w4_raw%d" % b, at * KIB + 256) for b, at in enumerate((39, 28))]
+        w4_raw = [placed([P, 4, N], F32, "w4_raw%d" % b, at * KIB + 256) for b, at in enumerate((28, 39))]
         for b in range(2):
             nc.sync.dma_start(
                 w4_raw[b][:].rearrange("p i n -> p (i n)"),
@@ -307,7 +307,7 @@ def tile_list_soft_gripper_valves_kernel(
         grasp_code(h00, 0, 0, range(4), (4, 5, 6, 7))
         first_passes(1, 0, (2, 3))
         round_w2(w2_late[0], 1, 0, P // 2, nc.scalar.copy, "p m t i")
-        round_w2(w2_late[1], 1, P // 2, P, round_on_gpsimd, "p t m i")
+        round_w2(w2_late[1], 1, P // 2, P, nc.scalar.copy, "p m t i")
         first_copies(1, 0)
         h02 = held([P, QUARTER, 4], BF16, "h02")
         grasp_code(h02, 0, HALF, (4, 5), (4, 5))
@@ -315,14 +315,21 @@ def tile_list_soft_gripper_valves_kernel(
         h03 = placed([P, QUARTER, 4], BF16, "h03", 52 * KIB)
         grasp_code(h03, 0, 768, (6,), (6,))
 
-        w4_first = held([P, 4 * HALF], BF16, "w4_first")
-        w4_rest = placed([P, 4 * QUARTER], BF16, "w4_rest", 54 * KIB)
-        for b, lo, width in ((0, 0, N), (1, N, P)):
+        w4_first = placed([P, 4 * HALF], BF16, "w4_first", 54 * KIB)
+        w4_rest = held([P, 4 * QUARTER], BF16, "w4_rest")
+        round_on_gpsimd(
+            w4_first[:, 0 : 4 * QUARTER].rearrange("p (n i) -> p n i", i=4),
+            w4_raw[0][:, :, 0:QUARTER].rearrange("p i n -> p n i"),
+        )
+        for rounded, b, lo, hi in (
+            (w4_first[:, 4 * QUARTER : 4 * N], 0, QUARTER, N),
+            (w4_first[:, 4 * N : 4 * HALF], 1, 0, P),
+            (w4_rest[:], 1, P, N),
+        ):
             nc.scalar.copy(
-                w4_first[:, 4 * lo : 4 * (lo + width)].rearrange("p (c n i) -> p c i n", n=4, i=4),
-                w4_raw[b][:, :, 0:width].rearrange("p i (c n) -> p c i n", n=4),
+                rounded.rearrange("p (c n i) -> p c i n", n=4, i=4),
+                w4_raw[b][:, :, lo:hi].rearrange("p i (c n) -> p c i n", n=4),
             )
-        round_on_gpsimd(w4_rest[:].rearrange("p (n i) -> p n i", i=4), w4_raw[1][:, :, P:N].rearrange("p i n -> p n i"))
         h10 = held([P, HALF, 4], BF16, "h10", tag="h1")
         grasp_code(h10, 1, 0, range(4), (7, 4, 5, 6))
         first_product(1, 1)

@@ -297,8 +297,17 @@ def tile_list_soft_gripper_valves_kernel(
             nc.sync.dma_start(out[P * n : P * (n + 1), lo : lo + width], result[:])
 
         first_product(0, 0)
-        round_w2(w2_first, 0, 0, P, nc.vector.tensor_copy, "p m t i")
-        quantise_w2(0)
+        for u in range(2):
+            nc.vector.tensor_copy(
+                w2_grouped[0][:].rearrange("p (t m i) -> p m i t", t=4, i=4)[:, :, :, 2 * u : 2 * u + 2],
+                w2_first[:].rearrange("p i (m t) -> p m i t", t=4)[:, :, :, 2 * u : 2 * u + 2],
+            )
+        for u in range(2):
+            nc.vector.quantize_mx(
+                w2_codes[0][:, QUARTER * u : QUARTER * (u + 1)].bitcast(FP8X4),
+                w2_scales[0][:, QUARTER * u : QUARTER * (u + 1)],
+                w2_grouped[0][:, S * u : S * (u + 1)],
+            )
         gather_v2(0)
         gather_v2(1)
         first_product(0, 1)
@@ -306,8 +315,8 @@ def tile_list_soft_gripper_valves_kernel(
         h00 = held([P, HALF, 4], BF16, "h00")
         grasp_code(h00, 0, 0, range(4), (4, 5, 6, 7))
         first_passes(1, 0, (2, 3))
-        round_w2(w2_late[0], 1, 0, P // 2, nc.scalar.copy, "p m t i")
-        round_w2(w2_late[1], 1, P // 2, P, nc.scalar.copy, "p m t i")
+        round_w2(w2_late[0], 1, 0, P // 2, nc.scalar.copy, "p m i t")
+        round_w2(w2_late[1], 1, P // 2, P, nc.scalar.copy, "p m i t")
         first_copies(1, 0)
         h02 = held([P, QUARTER, 4], BF16, "h02")
         grasp_code(h02, 0, HALF, (4, 5), (4, 5))

@@ -167,7 +167,7 @@ def tile_list_soft_gripper_valves_kernel(
 
         def first_passes(b, jh, slots):
             for t in slots:
-                sums = a_sums[b, jh, t] = bank(t, [P, HALF])
+                sums = a_sums[b, jh, t] = bank(t + (b == 1 and t >= 2), [P, HALF])
                 col = 512 * b + 128 * t
                 for a in range(2):
                     nc.tensor.matmul_mx(
@@ -258,7 +258,7 @@ def tile_list_soft_gripper_valves_kernel(
                 rhs=h_codes[b, lo][:].bitcast(FP8X4), rhs_scale=h_scales[b, lo][:], start=start, stop=stop,
             )
 
-        def valve(n, lo, width, banks, gate_tag=None):
+        def valve(n, lo, width, banks):
             apart = len(banks) == 2
             if apart:
                 o_sum, d_sum = bank(banks[0], [P, width])[:], bank(banks[1], [P, width])[:]
@@ -273,10 +273,7 @@ def tile_list_soft_gripper_valves_kernel(
                     d_sum, w3_codes[:, b, cols], late_scales(W3_AT + N * b + P * n, P),
                     b, lo, b == 0 and apart, b == 1,
                 )
-            if gate_tag:
-                gate = held([P, width], F32, "gate_" + gate_tag, tag=gate_tag)
-            else:
-                gate = ring.tile([P, width], F32, name="gate")
+            gate = ring.tile([P, width], F32, name="gate")
             nc.scalar.activation(gate[:], o_sum, TANH, scale=0.5)
             return gate, d_sum
 
@@ -314,14 +311,15 @@ def tile_list_soft_gripper_valves_kernel(
         first_passes(1, 0, (0, 1))
         h00 = held([P, HALF, 4], BF16, "h00")
         grasp_code(h00, 0, 0, range(4), (4, 5, 6, 7))
+        h02 = held([P, QUARTER, 4], BF16, "h02")
+        grasp_code(h02, 0, HALF, (4,), (2,))
         first_passes(1, 0, (2, 3))
         round_w2(w2_late[0], 1, 0, P // 2, nc.scalar.copy, "p m i t")
         round_w2(w2_late[1], 1, P // 2, P, nc.scalar.copy, "p m i t")
         first_copies(1, 0)
-        h02 = held([P, QUARTER, 4], BF16, "h02")
-        grasp_code(h02, 0, HALF, (4, 5), (4, 5))
         quantise_w2(1)
-        h03 = placed([P, QUARTER, 4], BF16, "h03", 52 * KIB)
+        grasp_code(h02, 0, HALF, (5,), (5,))
+        h03 = held([P, QUARTER, 4], BF16, "h03")
         grasp_code(h03, 0, 768, (6,), (6,))
 
         w4_first = placed([P, 4 * HALF], BF16, "w4_first", 54 * KIB)
@@ -339,9 +337,11 @@ def tile_list_soft_gripper_valves_kernel(
                 rounded.rearrange("p (c n i) -> p c i n", n=4, i=4),
                 w4_raw[b][:, :, lo:hi].rearrange("p i (c n) -> p c i n", n=4),
             )
+        first_passes(1, 1, (0, 1))
         h10 = held([P, HALF, 4], BF16, "h10", tag="h1")
-        grasp_code(h10, 1, 0, range(4), (7, 4, 5, 6))
-        first_product(1, 1)
+        grasp_code(h10, 1, 0, range(4), (7, 2, 5, 6))
+        first_passes(1, 1, (2, 3))
+        first_copies(1, 1)
 
         w4_codes = held([P, 2 * N], U32, "w4_codes")
         w4_scales = placed([P, 2 * N], U8, "w4_scales", 32 * KIB)
@@ -349,9 +349,9 @@ def tile_list_soft_gripper_valves_kernel(
         nc.vector.quantize_mx(w4_codes[:, 0:HALF].bitcast(FP8X4), w4_scales[:, 0:HALF], w4_first[:])
         quantise_h(h10, 1, 0, 30 * KIB)
         nc.vector.quantize_mx(w4_codes[:, HALF : 2 * N].bitcast(FP8X4), w4_scales[:, HALF : 2 * N], w4_rest[:])
-        first = [valve(0, 0, HALF, (7, 0)), valve(1, 0, HALF, (1, 2), "h13")]
+        first = [valve(0, 0, HALF, (7, 0)), valve(1, 0, HALF, (1, 3))]
         grasp_code(h03, 0, 768, (7,), (6,))
-        first.append(valve(2, 0, HALF, (3, 4)))
+        first.append(valve(2, 0, HALF, (4, 2)))
         h12 = held([P, QUARTER, 4], BF16, "h12", tag="h1")
         grasp_code(h12, 1, HALF, (4,), (5,))
         quantise_h(h02, 0, HALF, 31 * KIB)
@@ -363,10 +363,10 @@ def tile_list_soft_gripper_valves_kernel(
         h13 = held([P, QUARTER, 4], BF16, "h13")
         grasp_code(h13, 1, 768, (6,), (1,))
         second = [valve(n, HALF, QUARTER, (number,)) for n, number in enumerate((6, 5, 7))]
-        grasp_code(h13, 1, 768, (7,), (3,))
+        grasp_code(h13, 1, 768, (7,), (4,))
         store(2, 0, HALF, gate_drive(HALF, *first[2]), add_on_scalar)
         quantise_h(h13, 1, 768)
-        third = [valve(n, 768, QUARTER, (number,)) for n, number in enumerate((0, 2, 4))]
+        third = [valve(n, 768, QUARTER, (number,)) for n, number in enumerate((0, 3, 2))]
         for n in range(N // P):
             store(n, HALF, QUARTER, gate_drive(QUARTER, *second[n]), add_on_gpsimd)
         for n in range(N // P):

@@ -61,8 +61,9 @@ def tile_list_soft_gripper_valves_kernel(
 
         nc.vector.memset(w1_rows[0:96, 0:HALF].bitcast(I32), 0)
         nc.vector.memset(tab_rows[0:96, :].bitcast(I32), 0)
-        nc.vector.memset(w1_rows[0:112, HALF : 3 * HALF].bitcast(I32), 0)
-        nc.vector.memset(tab2_rows[0:112, :].bitcast(I32), 0)
+        for engine, lo, hi in ((nc.vector, 0, 48), (nc.gpsimd, 64, P)):
+            engine.memset(w1_rows[lo:hi, HALF : 3 * HALF].bitcast(I32), 0)
+            engine.memset(tab2_rows[lo:hi, :].bitcast(I32), 0)
         for plane in planes:
             nc.gpsimd.memset(plane[:].bitcast(I32), 0)
 
@@ -75,13 +76,13 @@ def tile_list_soft_gripper_valves_kernel(
         )
         nc.sync.dma_start(tab_rows[96:128, :].bitcast(I32), tab_scales.rearrange("a q t -> (a q) t").bitcast(I32))
         nc.sync.dma_start(idx2[:], offs2)
-        nc.sync.dma_start(tab2_rows[112:128, :].bitcast(I32), tab2_scales[0].bitcast(I32))
+        nc.sync.dma_start(tab2_rows[48:64, :].bitcast(I32), tab2_scales[0].bitcast(I32))
         nc.sync.dma_start(
-            w1_rows[112:128, HALF : 3 * HALF].bitcast(I32).rearrange("q (a c) -> q a c", a=2),
+            w1_rows[48:64, HALF : 3 * HALF].bitcast(I32).rearrange("q (a c) -> q a c", a=2),
             w1_scale_words.rearrange("a q c -> q a c")[:, :, HALF // 4 : H // 4],
         )
         nc.sync.dma_start(
-            staged[112:128, W3_AT:TAB2_AT].bitcast(I32).rearrange("q (a c) -> q a c", a=2),
+            staged[48:64, W3_AT:TAB2_AT].bitcast(I32).rearrange("q (a c) -> q a c", a=2),
             w3_scales.bitcast(I32).rearrange("a q c -> q a c"),
         )
         nc.sync.dma_start(tab_w[0][:], tab_words[0].rearrange("p t i -> p (t i)").bitcast(I32))
@@ -136,7 +137,7 @@ def tile_list_soft_gripper_valves_kernel(
         nc.sync.dma_start(w2_first[:], w2[:, 0:HALF].rearrange("(p i) c -> p i c", i=4))
         tab2_w = placed([P, T // 2], I32, "tab2_w", 0)
         nc.sync.dma_start(tab2_w[:], tab2_words[0].bitcast(I32))
-        move_rows(late, 112, LATE_AT, STAGED)
+        move_rows(late, 48, LATE_AT, STAGED)
 
         def late_scales(lo, width):
             return late[:, lo - LATE_AT : lo - LATE_AT + width]

@@ -70,13 +70,12 @@ def tile_list_soft_gripper_valves_kernel(
         tab_w = [placed([P, T], I32, "tab_w0", 0), None]
         w1_raw = held([P, 2, H // 2], I32, "w1_raw", tag="slot_a")
         w1_scale_words = w1_scales.bitcast(I32)
+        nc.sync.dma_start(tab_rows[96:128, :].bitcast(I32), tab_scales.rearrange("a q t -> (a q) t").bitcast(I32))
+        nc.sync.dma_start(tab2_rows[48:64, :].bitcast(I32), tab2_scales[0].bitcast(I32))
         nc.sync.dma_start(idx[:], offs)
         nc.sync.dma_start(
             w1_rows[96:128, 0:HALF].bitcast(I32), w1_scale_words.rearrange("a q c -> (a q) c")[:, 0 : HALF // 4]
         )
-        nc.sync.dma_start(tab_rows[96:128, :].bitcast(I32), tab_scales.rearrange("a q t -> (a q) t").bitcast(I32))
-        nc.sync.dma_start(idx2[:], offs2)
-        nc.sync.dma_start(tab2_rows[48:64, :].bitcast(I32), tab2_scales[0].bitcast(I32))
         nc.sync.dma_start(
             w1_rows[48:64, HALF : 3 * HALF].bitcast(I32).rearrange("q (a c) -> q a c", a=2),
             w1_scale_words.rearrange("a q c -> q a c")[:, :, HALF // 4 : H // 4],
@@ -85,6 +84,7 @@ def tile_list_soft_gripper_valves_kernel(
             staged[48:64, W3_AT:TAB2_AT].bitcast(I32).rearrange("q (a c) -> q a c", a=2),
             w3_scales.bitcast(I32).rearrange("a q c -> q a c"),
         )
+        nc.sync.dma_start(idx2[:], offs2)
         nc.sync.dma_start(tab_w[0][:], tab_words[0].rearrange("p t i -> p (t i)").bitcast(I32))
         nc.sync.dma_start(w1_raw[:], w1_words.bitcast(I32).rearrange("a p w -> p a w"))
 
@@ -367,7 +367,7 @@ def tile_list_soft_gripper_valves_kernel(
         grasp_code(h13, 1, 768, (7,), (4,))
         store(2, 0, HALF, gate_drive(HALF, *first[2]), add_on_scalar)
         quantise_h(h13, 1, 768)
-        third = [valve(n, 768, QUARTER, (number,)) for n, number in enumerate((0, 3, 2))]
+        third = [valve(n, 768, QUARTER, (number,)) for n, number in enumerate((0, 3, 1))]
         for n in range(N // P):
             store(n, HALF, QUARTER, gate_drive(QUARTER, *second[n]), add_on_gpsimd)
         for n in range(N // P):

@@ -217,10 +217,12 @@ def tile_list_soft_gripper_valves_kernel(
                 v2[jh][:].bitcast(U16), tab2_w[:].bitcast(U16).indirect(idx2[:, 32 * jh : 32 * (jh + 1)])
             )
 
-        def grasp_code(h, b, lo, tiles, banks):
+        b_sums = {}
+
+        def tactile_passes(b, tiles, banks):
             for jt, number in zip(tiles, banks):
                 jh, jl = divmod(jt, 4)
-                sums = bank(number, [P, 4, JT])
+                sums = b_sums[b, jt] = bank(number, [P, 4, JT])
                 for t in range(4):
                     nc.tensor.matmul_mx(
                         sums[:, t, :],
@@ -231,7 +233,26 @@ def tile_list_soft_gripper_valves_kernel(
                         start=True,
                         stop=True,
                     )
+
+        def grasp_code(h, b, lo, tiles, banks, on_gpsimd=()):
+            for jt, number in zip(tiles, banks):
+                if (b, jt) not in b_sums:
+                    tactile_passes(b, (jt,), (number,))
+                jh, jl = divmod(jt, 4)
+                sums = b_sums[b, jt]
                 records = slice(JT * jl, JT * (jl + 1))
+                if jt in on_gpsimd:
+                    woven = held([P, JT, 4], F32, "woven")
+                    nc.scalar.copy(
+                        woven[:].rearrange("p (c i) t -> p c t i", i=2), sums[:].rearrange("p t (c i) -> p c t i", i=2)
+                    )
+                    nc.gpsimd.tensor_tensor(
+                        h[:, JT * jt - lo : JT * (jt + 1) - lo, :],
+                        woven[:],
+                        a_sb[b, jh][:, :, records].rearrange("p t j -> p j t"),
+                        MULT,
+                    )
+                    continue
                 nc.vector.tensor_tensor(
                     h[:, JT * jt - lo : JT * (jt + 1) - lo, :].rearrange("p (c i) t -> p c t i", i=2),
                     sums[:].rearrange("p t (c i) -> p c t i", i=2),
@@ -289,8 +310,11 @@ def tile_list_soft_gripper_valves_kernel(
         def add_on_scalar(result, gated, column):
             nc.scalar.activation(result, gated, IDENTITY, bias=column, scale=0.5)
 
-        def store(n, lo, width, gated, add_bias):
-            result = ring.tile([P, width], F32, name="result")
+        def store(n, lo, width, gated, add_bias, tag=None):
+            if tag:
+                result = held([P, width], F32, "result_" + tag, tag=tag)
+            else:
+                result = ring.tile([P, width], F32, name="result")
             add_bias(result[:], gated[:], bias[:, n : n + 1])
             nc.sync.dma_start(out[P * n : P * (n + 1), lo : lo + width], result[:])
 
@@ -310,27 +334,27 @@ def tile_list_soft_gripper_valves_kernel(
         gather_v2(1)
         first_product(0, 1)
         first_passes(1, 0, (0, 1))
-        h00 = held([P, HALF, 4], BF16, "h00")
-        grasp_code(h00, 0, 0, range(4), (4, 5, 6, 7))
+        h00 = placed([P, HALF, 4], BF16, "h00", 56 * KIB)
+        grasp_code(h00, 0, 0, (0, 3, 1, 2), (4, 5, 6, 7), on_gpsimd=(3,))
         h02 = held([P, QUARTER, 4], BF16, "h02")
-        grasp_code(h02, 0, HALF, (4,), (2,))
+        grasp_code(h02, 0, HALF, (4, 5), (2, 5))
+        h03 = held([P, QUARTER, 4], BF16, "h03")
+        grasp_code(h03, 0, 768, (6,), (6,))
         first_passes(1, 0, (2, 3))
         round_w2(w2_late[0], 1, 0, P // 2, nc.scalar.copy, "p m i t")
         round_w2(w2_late[1], 1, P // 2, P, nc.scalar.copy, "p m i t")
         first_copies(1, 0)
         quantise_w2(1)
-        grasp_code(h02, 0, HALF, (5,), (5,))
-        h03 = held([P, QUARTER, 4], BF16, "h03")
-        grasp_code(h03, 0, 768, (6,), (6,))
+        quantise_h(h00, 0, 0)
+        grasp_code(h03, 0, 768, (7,), (7,))
 
         w4_first = placed([P, 4 * HALF], BF16, "w4_first", 54 * KIB)
         w4_rest = held([P, 4 * QUARTER], BF16, "w4_rest")
         round_on_gpsimd(
-            w4_first[:, 0 : 4 * QUARTER].rearrange("p (n i) -> p n i", i=4),
-            w4_raw[0][:, :, 0:QUARTER].rearrange("p i n -> p n i"),
+            w4_first[:, 0 : 4 * N].rearrange("p (n i) -> p n i", i=4),
+            w4_raw[0][:].rearrange("p i n -> p n i"),
         )
         for rounded, b, lo, hi in (
-            (w4_first[:, 4 * QUARTER : 4 * N], 0, QUARTER, N),
             (w4_first[:, 4 * N : 4 * HALF], 1, 0, P),
             (w4_rest[:], 1, P, N),
         ):
@@ -340,35 +364,33 @@ def tile_list_soft_gripper_valves_kernel(
             )
         first_passes(1, 1, (0, 1))
         h10 = held([P, HALF, 4], BF16, "h10", tag="h1")
-        grasp_code(h10, 1, 0, range(4), (7, 2, 5, 6))
+        grasp_code(h10, 1, 0, range(4), (2, 5, 6, 7))
         first_passes(1, 1, (2, 3))
         first_copies(1, 1)
 
         w4_codes = held([P, 2 * N], U32, "w4_codes")
         w4_scales = placed([P, 2 * N], U8, "w4_scales", 32 * KIB)
-        quantise_h(h00, 0, 0, 29 * KIB)
         nc.vector.quantize_mx(w4_codes[:, 0:HALF].bitcast(FP8X4), w4_scales[:, 0:HALF], w4_first[:])
         quantise_h(h10, 1, 0, 30 * KIB)
         nc.vector.quantize_mx(w4_codes[:, HALF : 2 * N].bitcast(FP8X4), w4_scales[:, HALF : 2 * N], w4_rest[:])
-        first = [valve(0, 0, HALF, (7, 0)), valve(1, 0, HALF, (1, 3))]
-        grasp_code(h03, 0, 768, (7,), (6,))
-        first.append(valve(2, 0, HALF, (4, 2)))
-        h12 = held([P, QUARTER, 4], BF16, "h12", tag="h1")
-        grasp_code(h12, 1, HALF, (4,), (5,))
+        tactile_passes(1, (4, 5), (6, 7))
+        first = [valve(n, 0, HALF, banks) for n, banks in enumerate(((0, 2), (1, 5), (3, 4)))]
         quantise_h(h02, 0, HALF, 31 * KIB)
-        quantise_h(h03, 0, 768)
-        grasp_code(h12, 1, HALF, (5,), (7,))
-        store(0, 0, HALF, gate_drive(HALF, *first[0]), add_on_scalar)
+        quantise_h(h03, 0, 768, 29 * KIB)
+        h12 = held([P, QUARTER, 4], BF16, "h12", tag="h1")
+        grasp_code(h12, 1, HALF, (4, 5), (6, 7))
+        gated = gate_drive(HALF, *first[0])
         quantise_h(h12, 1, HALF)
-        store(1, 0, HALF, gate_drive(HALF, *first[1]), add_on_scalar)
+        store(0, 0, HALF, gated, add_on_gpsimd, "h1")
         h13 = held([P, QUARTER, 4], BF16, "h13")
-        grasp_code(h13, 1, 768, (6,), (1,))
-        second = [valve(n, HALF, QUARTER, (number,)) for n, number in enumerate((6, 5, 7))]
-        grasp_code(h13, 1, 768, (7,), (4,))
-        store(2, 0, HALF, gate_drive(HALF, *first[2]), add_on_scalar)
+        grasp_code(h13, 1, 768, (6, 7), (6, 7))
+        second = [valve(n, HALF, QUARTER, (number,)) for n, number in enumerate((0, 1, 3))]
+        gated = gate_drive(HALF, *first[1])
         quantise_h(h13, 1, 768)
-        third = [valve(n, 768, QUARTER, (number,)) for n, number in enumerate((0, 3, 1))]
+        store(1, 0, HALF, gated, add_on_gpsimd, "h13")
+        store(2, 0, HALF, gate_drive(HALF, *first[2]), add_on_scalar)
+        third = [valve(n, 768, QUARTER, (number,)) for n, number in enumerate((2, 6, 5))]
         for n in range(N // P):
             store(n, HALF, QUARTER, gate_drive(QUARTER, *second[n]), add_on_gpsimd)
         for n in range(N // P):
-            store(n, 768, QUARTER, gate_drive(QUARTER, *third[n]), add_on_scalar)
+            store(n, 768, QUARTER, gate_drive(QUARTER, *third[n]), add_on_scalar, None if n else "h_codes1_768")

@@ -68,7 +68,7 @@ def tile_list_soft_gripper_valves_kernel(
             nc.gpsimd.memset(plane[:].bitcast(I32), 0)
 
         tab_w = [placed([P, T], I32, "tab_w0", 0), None]
-        w1_raw = held([P, 2, H // 2], I32, "w1_raw", tag="slot_a")
+        w1_raw = held([P, 2, H // 2], I32, "w1_raw")
         w1_scale_words = w1_scales.bitcast(I32)
         nc.sync.dma_start(tab_rows[96:128, :].bitcast(I32), tab_scales.rearrange("a q t -> (a q) t").bitcast(I32))
         nc.sync.dma_start(tab2_rows[48:64, :].bitcast(I32), tab2_scales[0].bitcast(I32))
@@ -118,15 +118,19 @@ def tile_list_soft_gripper_valves_kernel(
         v = {}
 
         def gather_v(a, jh):
-            v[a, jh] = held([P, HALF], U32, "v%d%d" % (a, jh), tag="slot_a" if (a, jh) == (0, 1) else None)
+            v[a, jh] = held([P, HALF], U32, "v%d%d" % (a, jh))
             nc.vector.tensor_copy(v[a, jh][:], tab_w[a][:].bitcast(U32).indirect(idx[:, 32 * jh : 32 * (jh + 1)]))
 
         gather_v(0, 0)
         w1_codes = held([P, 2 * 2 * H], U8, "w1_codes")
-        nc.vector.tensor_copy(
-            w1_codes[:].bitcast(U16).rearrange("p (g t c i) -> p g c t i", g=4, t=4, i=8),
-            w1_raw[:].rearrange("p a w -> p (a w)").bitcast(U16).rearrange("p (g c i t) -> p g c t i", g=4, t=4, i=8),
-        )
+        for b in range(2):
+            for a in range(2):
+                nc.scalar.copy(
+                    w1_codes[:, 2 * H * a + H * b : 2 * H * a + H * (b + 1)].bitcast(U16).rearrange(
+                        "p (t c i) -> p c t i", t=4, i=8
+                    ),
+                    w1_raw[:, a, QUARTER * b : QUARTER * (b + 1)].bitcast(U16).rearrange("p (c i t) -> p c t i", t=4, i=8),
+                )
         gather_v(0, 1)
         late = placed([P, STAGED - LATE_AT], U8, "late", 8 * KIB)
         nc.gpsimd.memset(late[:].bitcast(I32), 0)
@@ -166,11 +170,14 @@ def tile_list_soft_gripper_valves_kernel(
 
         a_sb, a_sums = {}, {}
 
-        def first_passes(b, jh, slots):
+        def first_passes(b, jh, slots, passes=range(2)):
             for t in slots:
-                sums = a_sums[b, jh, t] = bank(t + (b == 1 and t >= 2), [P, HALF])
+                if 0 in passes:
+                    early = (b, jh) == (0, 1) and t < 2
+                    a_sums[b, jh, t] = bank(t + (b == 1 and t >= 2) + 4 * early, [P, HALF])
+                sums = a_sums[b, jh, t]
                 col = 512 * b + 128 * t
-                for a in range(2):
+                for a in passes:
                     nc.tensor.matmul_mx(
                         sums[:],
                         lhsT=w1_codes[:, 2 * (H * a + col) : 2 * (H * a + col + 128)].bitcast(FP4X4),
@@ -188,10 +195,6 @@ def tile_list_soft_gripper_valves_kernel(
                 a_sb[b, jh] = held([P, 4, HALF], F32, "a_sb%d%d" % (b, jh))
             for t in range(4):
                 nc.scalar.copy(a_sb[b, jh][:, t, :], a_sums[b, jh, t][:])
-
-        def first_product(b, jh):
-            first_passes(b, jh, range(4))
-            first_copies(b, jh)
 
         w2_grouped = [held([P, 4 * HALF], BF16, "w2_grouped0"), placed([P, 4 * HALF], BF16, "w2_grouped1", 52 * KIB)]
         w2_codes = [held([P, HALF], U32, "w2_codes%d" % b) for b in range(2)]
@@ -318,7 +321,10 @@ def tile_list_soft_gripper_valves_kernel(
             add_bias(result[:], gated[:], bias[:, n : n + 1])
             nc.sync.dma_start(out[P * n : P * (n + 1), lo : lo + width], result[:])
 
-        first_product(0, 0)
+        first_passes(0, 0, range(4), (0,))
+        first_passes(0, 1, range(2), (0,))
+        first_passes(0, 0, range(4), (1,))
+        first_copies(0, 0)
         for u in range(2):
             nc.vector.tensor_copy(
                 w2_grouped[0][:].rearrange("p (t m i) -> p m i t", t=4, i=4)[:, :, :, 2 * u : 2 * u + 2],
@@ -332,7 +338,9 @@ def tile_list_soft_gripper_valves_kernel(
             )
         gather_v2(0)
         gather_v2(1)
-        first_product(0, 1)
+        first_passes(0, 1, range(2), (1,))
+        first_passes(0, 1, (2, 3))
+        first_copies(0, 1)
         first_passes(1, 0, (0, 1))
         h00 = placed([P, HALF, 4], BF16, "h00", 56 * KIB)
         grasp_code(h00, 0, 0, (0, 3, 1, 2), (4, 5, 6, 7), on_gpsimd=(3,))

@@ -23,10 +23,7 @@ HALF = 512
 QUARTER = 256
 JT = 128
 KIB = 1024
-TAB_AT, W1_AT, LATE_AT = 0, S, S + HALF
-W3_AT = LATE_AT + 2 * HALF
-TAB2_AT = W3_AT + 2 * N
-STAGED = TAB2_AT + S
+TAB_AT, W1_AT, STAGED = 0, S, S + H
 
 
 def tile_list_soft_gripper_valves_kernel(
@@ -53,43 +50,32 @@ def tile_list_soft_gripper_valves_kernel(
         idx = lists.tile([P, S // 16], U16, name="idx")
         idx2 = lists.tile([P, S // 16], U16, name="idx2")
 
-        tab_rows = held([P, T], U8, "tab_rows")
-        tab2_rows = held([P, T], U8, "tab2_rows")
-        w1_rows = held([P, 3 * HALF], U8, "w1_rows")
+        tab2_rows = placed([P, T], U8, "tab2_rows", 0)
+        tab_rows = placed([P, T], U8, "tab_rows", 50 * KIB)
+        w1_rows = held([P, H], U8, "w1_rows")
         staged = held([P, STAGED], U8, "staged")
-        planes = [held([P, LATE_AT], U8, "planes%d" % a) for a in range(2)]
+        tab2_plane = held([P, S], U8, "tab2_plane")
+        planes = [held([P, STAGED], U8, "planes0"), None]
 
-        nc.vector.memset(w1_rows[0:96, 0:HALF].bitcast(I32), 0)
-        nc.vector.memset(tab_rows[0:96, :].bitcast(I32), 0)
         for engine, lo, hi in ((nc.vector, 0, 48), (nc.gpsimd, 64, P)):
-            engine.memset(w1_rows[lo:hi, HALF : 3 * HALF].bitcast(I32), 0)
             engine.memset(tab2_rows[lo:hi, :].bitcast(I32), 0)
-        for plane in planes:
-            nc.gpsimd.memset(plane[:].bitcast(I32), 0)
+        nc.vector.memset(w1_rows[0:96, :].bitcast(I32), 0)
+        nc.vector.memset(tab_rows[0:96, :].bitcast(I32), 0)
+        nc.gpsimd.memset(tab2_plane[:].bitcast(I32), 0)
+        nc.gpsimd.memset(planes[0][:].bitcast(I32), 0)
 
-        tab_w = [placed([P, T], I32, "tab_w0", 0), None]
-        w1_raw = held([P, 2, H // 2], I32, "w1_raw")
-        w1_scale_words = w1_scales.bitcast(I32)
-        nc.sync.dma_start(tab_rows[96:128, :].bitcast(I32), tab_scales.rearrange("a q t -> (a q) t").bitcast(I32))
+        w1_word_rows = w1_words.bitcast(I32).rearrange("a p w -> p a w")
         nc.sync.dma_start(tab2_rows[48:64, :].bitcast(I32), tab2_scales[0].bitcast(I32))
-        nc.sync.dma_start(idx[:], offs)
-        nc.sync.dma_start(
-            w1_rows[96:128, 0:HALF].bitcast(I32), w1_scale_words.rearrange("a q c -> (a q) c")[:, 0 : HALF // 4]
-        )
-        nc.sync.dma_start(
-            w1_rows[48:64, HALF : 3 * HALF].bitcast(I32).rearrange("q (a c) -> q a c", a=2),
-            w1_scale_words.rearrange("a q c -> q a c")[:, :, HALF // 4 : H // 4],
-        )
-        nc.sync.dma_start(
-            staged[48:64, W3_AT:TAB2_AT].bitcast(I32).rearrange("q (a c) -> q a c", a=2),
-            w3_scales.bitcast(I32).rearrange("a q c -> q a c"),
-        )
         nc.sync.dma_start(idx2[:], offs2)
-        nc.sync.dma_start(tab_w[0][:], tab_words[0].rearrange("p t i -> p (t i)").bitcast(I32))
-        nc.sync.dma_start(w1_raw[:], w1_words.bitcast(I32).rearrange("a p w -> p a w"))
-
-        tab_picked = placed([P, S], U8, "tab_picked", 24 * KIB)
-        tab2_picked = held([P, S], U8, "tab2_picked", tag="slot_b")
+        nc.sync.dma_start(tab_rows[96:128, :].bitcast(I32), tab_scales.rearrange("a q t -> (a q) t").bitcast(I32))
+        nc.sync.dma_start(idx[:], offs)
+        nc.sync.dma_start(w1_rows[96:128, :].bitcast(I32), w1_scales.bitcast(I32).rearrange("a q c -> (a q) c"))
+        w2_first = held([P, 4, HALF], F32, "w2_first")
+        nc.sync.dma_start(w2_first[:], w2[:, 0:HALF].rearrange("(p i) c -> p i c", i=4))
+        tab2_w = placed([P, T // 2], I32, "tab2_w", 56 * KIB)
+        nc.sync.dma_start(tab2_w[:], tab2_words[0].bitcast(I32))
+        w1_raw = [held([P, 2, QUARTER], I32, "w1_raw0"), None]
+        nc.sync.dma_start(w1_raw[0][:], w1_word_rows[:, :, 0:QUARTER])
 
         def deal_w1_scales(lo, hi):
             nc.vector.tensor_copy(
@@ -97,171 +83,191 @@ def tile_list_soft_gripper_valves_kernel(
                 w1_rows[:, lo:hi].rearrange("p (b c i t) -> p c b t i", c=8, t=4, i=16),
             )
 
-        deal_w1_scales(0, HALF)
-        nc.vector.tensor_copy(tab_picked[:], tab_rows[:].indirect(idx[:]))
-        nc.vector.tensor_copy(staged[:, TAB_AT:W1_AT].bitcast(I32), tab_picked[:].bitcast(I32))
-
-        def move_rows(plane, first, lo, hi):
+        def move_rows(plane, source, first, lo, hi):
             for r in range(4):
                 nc.sync.dma_start(
-                    plane[r:P:32, :].bitcast(I32), staged[first + r : first + 16 : 4, lo:hi].bitcast(I32)
+                    plane[r:P:32, :].bitcast(I32), source[first + r : first + 16 : 4, lo:hi].bitcast(I32)
                 )
 
-        move_rows(planes[0], 96, 0, LATE_AT)
-        tab_w[1] = placed([P, T], I32, "tab_w1", 24 * KIB)
-        nc.sync.dma_start(tab_w[1][:], tab_words[1].rearrange("p t i -> p (t i)").bitcast(I32))
-        move_rows(planes[1], 112, 0, LATE_AT)
-        deal_w1_scales(HALF, 3 * HALF)
+        tab2_picked = held([P, S], U8, "tab2_picked")
         nc.vector.tensor_copy(tab2_picked[:], tab2_rows[:].indirect(idx2[:]))
-        nc.vector.tensor_copy(staged[:, TAB2_AT:STAGED].bitcast(I32), tab2_picked[:].bitcast(I32))
+        move_rows(tab2_plane, tab2_picked, 48, 0, S)
+        tab_w = [placed([P, T], I32, "tab_w0", 0), None]
+        nc.sync.dma_start(tab_w[0][:], tab_words[0].rearrange("p t i -> p (t i)").bitcast(I32))
 
-        v = {}
-
-        def gather_v(a, jh):
-            v[a, jh] = held([P, HALF], U32, "v%d%d" % (a, jh))
-            nc.vector.tensor_copy(v[a, jh][:], tab_w[a][:].bitcast(U32).indirect(idx[:, 32 * jh : 32 * (jh + 1)]))
-
-        gather_v(0, 0)
-        w1_codes = held([P, 2 * 2 * H], U8, "w1_codes")
-        for b in range(2):
-            for a in range(2):
-                nc.scalar.copy(
-                    w1_codes[:, 2 * H * a + H * b : 2 * H * a + H * (b + 1)].bitcast(U16).rearrange(
-                        "p (t c i) -> p c t i", t=4, i=8
-                    ),
-                    w1_raw[:, a, QUARTER * b : QUARTER * (b + 1)].bitcast(U16).rearrange("p (c i t) -> p c t i", t=4, i=8),
-                )
-        gather_v(0, 1)
-        late = placed([P, STAGED - LATE_AT], U8, "late", 8 * KIB)
-        nc.gpsimd.memset(late[:].bitcast(I32), 0)
-        gather_v(1, 0)
-        gather_v(1, 1)
-
-        w2_first = held([P, 4, HALF], F32, "w2_first", tag="slot_b")
-        nc.sync.dma_start(w2_first[:], w2[:, 0:HALF].rearrange("(p i) c -> p i c", i=4))
-        tab2_w = placed([P, T // 2], I32, "tab2_w", 0)
-        nc.sync.dma_start(tab2_w[:], tab2_words[0].bitcast(I32))
-        move_rows(late, 48, LATE_AT, STAGED)
-
-        def late_scales(lo, width):
-            return late[:, lo - LATE_AT : lo - LATE_AT + width]
+        deal_w1_scales(0, HALF)
+        tab_picked = placed([P, S], U8, "tab_picked", 32 * KIB)
+        nc.vector.tensor_copy(tab_picked[:], tab_rows[:].indirect(idx[:]))
+        deal_w1_scales(HALF, H)
+        nc.vector.tensor_copy(staged[:, TAB_AT:W1_AT].bitcast(I32), tab_picked[:].bitcast(I32))
+        move_rows(planes[0], staged, 96, 0, STAGED)
+        tab_w[1] = placed([P, T], I32, "tab_w1", 32 * KIB + 768)
+        nc.sync.dma_start(tab_w[1][:], tab_words[1].rearrange("p t i -> p (t i)").bitcast(I32))
+        planes[1] = placed([P, STAGED], U8, "planes1", 30 * KIB + QUARTER)
+        nc.vector.memset(planes[1][:].bitcast(I32), 0)
+        move_rows(planes[1], staged, 112, 0, STAGED)
 
         def w1_scales_of(a, b, t):
-            if b == 0:
-                return planes[a][:, W1_AT + P * t : W1_AT + P * (t + 1)]
-            return late_scales(LATE_AT + HALF * a + P * t, P)
+            return planes[a][:, W1_AT + HALF * b + P * t : W1_AT + HALF * b + P * (t + 1)]
 
-        w2_late = [placed([P, 4, QUARTER], F32, "w2_late%d" % u, (20, 24)[u] * KIB + (64, 256)[u]) for u in range(2)]
-        for u in range(2):
-            nc.sync.dma_start(
-                w2_late[u][:], w2[:, HALF + QUARTER * u : HALF + QUARTER * (u + 1)].rearrange("(p i) c -> p i c", i=4)
-            )
-        w4_raw = [placed([P, 4, N], F32, "w4_raw%d" % b, at * KIB + 256) for b, at in enumerate((28, 39))]
-        for b in range(2):
-            nc.sync.dma_start(
-                w4_raw[b][:].rearrange("p i n -> p (i n)"),
-                w4[HALF * b : HALF * (b + 1), :].rearrange("(p i) n -> p (i n)", i=4),
-            )
-        w3_codes = placed([P, 2, N], I32, "w3_codes", 34 * KIB + 256)
-        nc.sync.dma_start(w3_codes[:], w3_words.rearrange("a p c i -> p a (c i)").bitcast(I32))
-        bias = placed([P, N // P], F32, "bias", 24 * KIB + 64)
-        with nc.allow_non_contiguous_dma(reason="one bias value a partition"):
-            nc.sync.dma_start(bias[:], bv.rearrange("(c p) -> p c", p=P))
-
-        a_sb, a_sums = {}, {}
-
-        def first_passes(b, jh, slots, passes=range(2)):
-            for t in slots:
-                if 0 in passes:
-                    early = (b, jh) == (0, 1) and t < 2
-                    a_sums[b, jh, t] = bank(t + (b == 1 and t >= 2) + 4 * early, [P, HALF])
-                sums = a_sums[b, jh, t]
-                col = 512 * b + 128 * t
-                for a in passes:
-                    nc.tensor.matmul_mx(
-                        sums[:],
-                        lhsT=w1_codes[:, 2 * (H * a + col) : 2 * (H * a + col + 128)].bitcast(FP4X4),
-                        lhsT_scale=w1_scales_of(a, b, t),
-                        rhs=v[a, jh][:].bitcast(FP8X4),
-                        rhs_scale=planes[a][:, TAB_AT + HALF * jh : TAB_AT + HALF * (jh + 1)],
-                        start=(a == 0),
-                        stop=(a == 1),
-                    )
-
-        def first_copies(b, jh):
-            if b == 1:
-                a_sb[b, jh] = placed([P, 4, HALF], F32, "a_sb1%d" % jh, (16, 44)[jh] * KIB)
-            else:
-                a_sb[b, jh] = held([P, 4, HALF], F32, "a_sb%d%d" % (b, jh))
-            for t in range(4):
-                nc.scalar.copy(a_sb[b, jh][:, t, :], a_sums[b, jh, t][:])
-
-        w2_grouped = [held([P, 4 * HALF], BF16, "w2_grouped0"), placed([P, 4 * HALF], BF16, "w2_grouped1", 52 * KIB)]
+        w2_grouped = [placed([P, 4 * HALF], BF16, "w2_grouped0", 80 * KIB), placed([P, 4 * HALF], BF16, "w2_grouped1", 72 * KIB)]
         w2_codes = [held([P, HALF], U32, "w2_codes%d" % b) for b in range(2)]
-        w2_scales = [held([P, HALF], U8, "w2_scales%d" % b) for b in range(2)]
+        w2_scales = [placed([P, HALF], U8, "w2_scales0", 32 * KIB + QUARTER), held([P, HALF], U8, "w2_scales1")]
 
-        def round_on_gpsimd(dst, src):
-            nc.gpsimd.tensor_scalar(dst, src, 1.0, 0.0, MULT, ADD)
-
-        def round_w2(raw, b, lo, hi, copy, order):
-            copy(
-                w2_grouped[b][:].rearrange("p (t m i) -> p t m i", t=4, i=4)[:, :, lo:hi, :].rearrange("p t m i -> " + order),
-                raw[:].rearrange("p i (m t) -> " + order, t=4),
+        def round_w2(raw, b, lo, hi):
+            nc.scalar.copy(
+                w2_grouped[b][:].rearrange("p (t m i) -> p t m i", t=4, i=4)[:, :, lo:hi, :].rearrange("p t m i -> p m i t"),
+                raw[:].rearrange("p i (m t) -> p m i t", t=4),
             )
 
         def quantise_w2(b):
             nc.vector.quantize_mx(w2_codes[b][:].bitcast(FP8X4), w2_scales[b][:], w2_grouped[b][:])
 
-        v2 = {}
+        w1_codes = [held([P, 2, 2 * HALF], U8, "w1_codes%d" % b) for b in range(2)]
+
+        def deal_w1_words(b):
+            for a in range(2):
+                nc.scalar.copy(
+                    w1_codes[b][:, a, :].bitcast(U16).rearrange("p (t c i) -> p c t i", t=4, i=8),
+                    w1_raw[b][:, a, :].bitcast(U16).rearrange("p (c i t) -> p c t i", t=4, i=8),
+                )
+
+        v, v2 = {}, {}
+
+        def gather_v(a, jh):
+            v[a, jh] = held([P, HALF], U32, "v%d%d" % (a, jh))
+            nc.vector.tensor_copy(v[a, jh][:], tab_w[a][:].bitcast(U32).indirect(idx[:, 32 * jh : 32 * (jh + 1)]))
 
         def gather_v2(jh):
-            v2[jh] = held([P, 2 * HALF], U8, "v2%d" % jh)
+            v2[jh] = placed([P, 2 * HALF], U8, "v2%d" % jh, (84, 82)[jh] * KIB)
             nc.vector.tensor_copy(
                 v2[jh][:].bitcast(U16), tab2_w[:].bitcast(U16).indirect(idx2[:, 32 * jh : 32 * (jh + 1)])
             )
 
-        b_sums = {}
+        def pressure_pass(sums, a, b, t, lo, width, start, stop):
+            jh, at = divmod(lo, HALF)
+            nc.tensor.matmul_mx(
+                sums,
+                lhsT=w1_codes[b][:, a, 2 * P * t : 2 * P * (t + 1)].bitcast(FP4X4),
+                lhsT_scale=w1_scales_of(a, b, t),
+                rhs=v[a, jh][:, at : at + width].bitcast(FP8X4),
+                rhs_scale=planes[a][:, TAB_AT + lo : TAB_AT + lo + width],
+                start=start,
+                stop=stop,
+            )
 
-        def tactile_passes(b, tiles, banks):
-            for jt, number in zip(tiles, banks):
-                jh, jl = divmod(jt, 4)
-                sums = b_sums[b, jt] = bank(number, [P, 4, JT])
+        def tactile_pass(sums, b, t, lo, width):
+            jh, at = divmod(lo, HALF)
+            nc.tensor.matmul_mx(
+                sums,
+                lhsT=w2_codes[b][:, P * t : P * (t + 1)].bitcast(FP8X4),
+                lhsT_scale=w2_scales[b][:, P * t : P * (t + 1)],
+                rhs=v2[jh][:, 2 * at : 2 * (at + width)].bitcast(FP4X4),
+                rhs_scale=tab2_plane[:, lo : lo + width],
+                start=True,
+                stop=True,
+            )
+
+        copied, wide, tiles = {}, {}, {}
+
+        def copy_out(b, jh, at=None):
+            name = "copied%d%d" % (b, jh)
+            copied[b, jh] = held([P, 4, HALF], F32, name) if at is None else placed([P, 4, HALF], F32, name, at)
+            for t in range(4):
+                nc.scalar.copy(copied[b, jh][:, t, :], wide[b, jh, t][:])
+
+        def wide_pressure(jh, slots, banks):
+            for t, number in zip(slots, banks):
+                wide[1, jh, t] = bank(number, [P, HALF])
+                for a in range(2):
+                    pressure_pass(wide[1, jh, t][:], a, 1, t, HALF * jh, HALF, a == 0, a == 1)
+
+        def pressure_tiles(a, which):
+            for jt in which:
+                if a == 0:
+                    tiles[0, jt] = bank(jt, [P, 4, JT])
                 for t in range(4):
-                    nc.tensor.matmul_mx(
-                        sums[:, t, :],
-                        lhsT=w2_codes[b][:, 128 * t : 128 * (t + 1)].bitcast(FP8X4),
-                        lhsT_scale=w2_scales[b][:, 128 * t : 128 * (t + 1)],
-                        rhs=v2[jh][:, 2 * JT * jl : 2 * JT * (jl + 1)].bitcast(FP4X4),
-                        rhs_scale=late_scales(TAB2_AT + JT * jt, JT),
-                        start=True,
-                        stop=True,
-                    )
+                    pressure_pass(tiles[0, jt][:, t, :], a, 0, t, JT * jt, JT, (a, t) == (0, 0), (a, t) == (1, 3))
 
-        def grasp_code(h, b, lo, tiles, banks, on_gpsimd=()):
-            for jt, number in zip(tiles, banks):
-                if (b, jt) not in b_sums:
-                    tactile_passes(b, (jt,), (number,))
+        def tactile_tiles(which, banks):
+            for jt, number in zip(which, banks):
+                tiles[1, jt] = bank(number, [P, 4, JT])
+                for t in range(4):
+                    tactile_pass(tiles[1, jt][:, t, :], 1, t, JT * jt, JT)
+
+        def grasp_code(h, b, lo, which, on_gpsimd=()):
+            for jt in which:
                 jh, jl = divmod(jt, 4)
-                sums = b_sums[b, jt]
+                sums = tiles[b, jt]
                 records = slice(JT * jl, JT * (jl + 1))
                 if jt in on_gpsimd:
-                    woven = held([P, JT, 4], F32, "woven")
+                    woven = placed([P, JT, 4], F32, "woven", 80 * KIB)
                     nc.scalar.copy(
                         woven[:].rearrange("p (c i) t -> p c t i", i=2), sums[:].rearrange("p t (c i) -> p c t i", i=2)
                     )
                     nc.gpsimd.tensor_tensor(
                         h[:, JT * jt - lo : JT * (jt + 1) - lo, :],
                         woven[:],
-                        a_sb[b, jh][:, :, records].rearrange("p t j -> p j t"),
+                        copied[b, jh][:, :, records].rearrange("p t j -> p j t"),
                         MULT,
                     )
                     continue
                 nc.vector.tensor_tensor(
                     h[:, JT * jt - lo : JT * (jt + 1) - lo, :].rearrange("p (c i) t -> p c t i", i=2),
                     sums[:].rearrange("p t (c i) -> p c t i", i=2),
-                    a_sb[b, jh][:, :, records].rearrange("p t (c i) -> p c t i", i=2),
+                    copied[b, jh][:, :, records].rearrange("p t (c i) -> p c t i", i=2),
                     MULT,
                 )
+
+        round_w2(w2_first, 0, 0, P)
+        deal_w1_words(0)
+        gather_v2(0)
+        quantise_w2(0)
+        gather_v2(1)
+        w1_raw[1] = placed([P, 2, QUARTER], I32, "w1_raw1", 80 * KIB)
+        nc.sync.dma_start(w1_raw[1][:], w1_word_rows[:, :, QUARTER:HALF])
+        for jh in range(2):
+            for t in range(4):
+                wide[0, jh, t] = bank(4 * jh + t, [P, HALF])
+                tactile_pass(wide[0, jh, t][:], 0, t, HALF * jh, HALF)
+        for jh in range(2):
+            copy_out(0, jh)
+
+        w2_late = [placed([P, 4, QUARTER], F32, "w2_late%d" % u, (56 + 4 * u) * KIB) for u in range(2)]
+        for u in range(2):
+            nc.sync.dma_start(
+                w2_late[u][:], w2[:, HALF + QUARTER * u : HALF + QUARTER * (u + 1)].rearrange("(p i) c -> p i c", i=4)
+            )
+        for jh in range(2):
+            gather_v(0, jh)
+        pressure_tiles(0, range(8))
+
+        w4_raw = [placed([P, 4, N], F32, "w4_raw%d" % b, 10 * b * KIB) for b in range(2)]
+
+        def load_w4(b):
+            nc.sync.dma_start(
+                w4_raw[b][:].rearrange("p i n -> p (i n)"),
+                w4[HALF * b : HALF * (b + 1), :].rearrange("(p i) n -> p (i n)", i=4),
+            )
+
+        load_w4(0)
+        w3_codes = placed([P, 2, N], I32, "w3_codes", 6 * KIB)
+        nc.sync.dma_start(w3_codes[:], w3_words.rearrange("a p c i -> p a (c i)").bitcast(I32))
+        w3_planes = placed([P, N], U8, "w3_planes", 9 * KIB + QUARTER)
+        nc.vector.memset(w3_planes[:].bitcast(I32), 0)
+        for q in range(4):
+            nc.sync.dma_start(
+                w3_planes[32 * q + 4 : 32 * q + 12, :].bitcast(I32), w3_scales.bitcast(I32)[:, 4 * q : 4 * q + 4, :]
+            )
+        load_w4(1)
+        bias = placed([P, N // P], F32, "bias", 9 * KIB)
+        with nc.allow_non_contiguous_dma(reason="one bias value a partition"):
+            nc.sync.dma_start(bias[:], bv.rearrange("(c p) -> p c", p=P))
+
+        for jh in range(2):
+            gather_v(1, jh)
+        pressure_tiles(1, (0, 3, 1, 2, 4, 5, 6, 7))
+        deal_w1_words(1)
 
         h_codes = {}
         h_scales = {}
@@ -292,10 +298,9 @@ def tile_list_soft_gripper_valves_kernel(
                 o_sum, d_sum = both[:, 0, :], both[:, 1, :]
             cols = slice(P * n, P * (n + 1))
             for b in range(2):
-                w4_cols = slice(N * b + P * n, N * b + P * (n + 1))
-                valve_pass(o_sum, w4_codes[:, w4_cols], w4_scales[:, w4_cols], b, lo, b == 0, b == 1 and apart)
+                valve_pass(o_sum, w4_codes[n][:, P * b : P * (b + 1)], w4_scales[n][:, P * b : P * (b + 1)], b, lo, b == 0, b == 1 and apart)
                 valve_pass(
-                    d_sum, w3_codes[:, b, cols], late_scales(W3_AT + N * b + P * n, P),
+                    d_sum, w3_codes[:, b, cols], w3_planes[4 + 4 * b : P, cols],
                     b, lo, b == 0 and apart, b == 1,
                 )
             gate = ring.tile([P, width], F32, name="gate")
@@ -313,92 +318,69 @@ def tile_list_soft_gripper_valves_kernel(
         def add_on_scalar(result, gated, column):
             nc.scalar.activation(result, gated, IDENTITY, bias=column, scale=0.5)
 
-        def store(n, lo, width, gated, add_bias, tag=None):
-            if tag:
-                result = held([P, width], F32, "result_" + tag, tag=tag)
+        def store(n, lo, width, gated, add_bias, at=None):
+            if at:
+                result = placed([P, width], F32, "result_held", at)
             else:
                 result = ring.tile([P, width], F32, name="result")
             add_bias(result[:], gated[:], bias[:, n : n + 1])
             nc.sync.dma_start(out[P * n : P * (n + 1), lo : lo + width], result[:])
 
-        first_passes(0, 0, range(4), (0,))
-        first_passes(0, 1, range(2), (0,))
-        first_passes(0, 0, range(4), (1,))
-        first_copies(0, 0)
-        for u in range(2):
-            nc.vector.tensor_copy(
-                w2_grouped[0][:].rearrange("p (t m i) -> p m i t", t=4, i=4)[:, :, :, 2 * u : 2 * u + 2],
-                w2_first[:].rearrange("p i (m t) -> p m i t", t=4)[:, :, :, 2 * u : 2 * u + 2],
-            )
-        for u in range(2):
-            nc.vector.quantize_mx(
-                w2_codes[0][:, QUARTER * u : QUARTER * (u + 1)].bitcast(FP8X4),
-                w2_scales[0][:, QUARTER * u : QUARTER * (u + 1)],
-                w2_grouped[0][:, S * u : S * (u + 1)],
-            )
-        gather_v2(0)
-        gather_v2(1)
-        first_passes(0, 1, range(2), (1,))
-        first_passes(0, 1, (2, 3))
-        first_copies(0, 1)
-        first_passes(1, 0, (0, 1))
-        h00 = placed([P, HALF, 4], BF16, "h00", 56 * KIB)
-        grasp_code(h00, 0, 0, (0, 3, 1, 2), (4, 5, 6, 7), on_gpsimd=(3,))
+        h00 = placed([P, HALF, 4], BF16, "h00", 76 * KIB)
+        grasp_code(h00, 0, 0, (0, 3, 1, 2), on_gpsimd=(3,))
         h02 = held([P, QUARTER, 4], BF16, "h02")
-        grasp_code(h02, 0, HALF, (4, 5), (2, 5))
-        h03 = held([P, QUARTER, 4], BF16, "h03")
-        grasp_code(h03, 0, 768, (6,), (6,))
-        first_passes(1, 0, (2, 3))
-        round_w2(w2_late[0], 1, 0, P // 2, nc.scalar.copy, "p m i t")
-        round_w2(w2_late[1], 1, P // 2, P, nc.scalar.copy, "p m i t")
-        first_copies(1, 0)
-        quantise_w2(1)
+        grasp_code(h02, 0, HALF, (4, 5))
+        wide_pressure(0, range(4), (0, 3, 1, 2))
+        round_w2(w2_late[0], 1, 0, P // 2)
+        round_w2(w2_late[1], 1, P // 2, P)
+        copy_out(1, 0, 63 * KIB)
         quantise_h(h00, 0, 0)
-        grasp_code(h03, 0, 768, (7,), (7,))
+        quantise_w2(1)
+        h03 = placed([P, QUARTER, 4], BF16, "h03", 60 * KIB)
+        grasp_code(h03, 0, 768, (6, 7))
 
-        w4_first = placed([P, 4 * HALF], BF16, "w4_first", 54 * KIB)
-        w4_rest = held([P, 4 * QUARTER], BF16, "w4_rest")
-        round_on_gpsimd(
-            w4_first[:, 0 : 4 * N].rearrange("p (n i) -> p n i", i=4),
-            w4_raw[0][:].rearrange("p i n -> p n i"),
+        w4_grouped = placed([P, 2 * 4 * N], BF16, "w4_grouped", 73 * KIB)
+        nc.gpsimd.tensor_scalar(
+            w4_grouped[:].rearrange("p (n b c i) -> p n b c i", b=2, c=P, i=4)[:, :, 0, :, :],
+            w4_raw[0][:].rearrange("p i (n c) -> p n c i", c=P),
+            1.0, 0.0, MULT, ADD,
         )
-        for rounded, b, lo, hi in (
-            (w4_first[:, 4 * N : 4 * HALF], 1, 0, P),
-            (w4_rest[:], 1, P, N),
-        ):
+        for t, number in enumerate((0, 3, 1, 2)):
+            tactile_tiles((t,), (number,))
+            wide_pressure(1, (t,), (4 + t,))
+        h10 = held([P, HALF, 4], BF16, "h10")
+        grasp_code(h10, 1, 0, range(4))
+        copy_out(1, 1)
+        for n in range(N // P):
             nc.scalar.copy(
-                rounded.rearrange("p (c n i) -> p c i n", n=4, i=4),
-                w4_raw[b][:, :, lo:hi].rearrange("p i (c n) -> p c i n", n=4),
+                w4_grouped[:, HALF * (2 * n + 1) : HALF * (2 * n + 2)].rearrange("p (c m i) -> p c i m", m=4, i=4),
+                w4_raw[1][:, :, P * n : P * (n + 1)].rearrange("p i (c m) -> p c i m", m=4),
             )
-        first_passes(1, 1, (0, 1))
-        h10 = held([P, HALF, 4], BF16, "h10", tag="h1")
-        grasp_code(h10, 1, 0, range(4), (2, 5, 6, 7))
-        first_passes(1, 1, (2, 3))
-        first_copies(1, 1)
 
-        w4_codes = held([P, 2 * N], U32, "w4_codes")
-        w4_scales = placed([P, 2 * N], U8, "w4_scales", 32 * KIB)
-        nc.vector.quantize_mx(w4_codes[:, 0:HALF].bitcast(FP8X4), w4_scales[:, 0:HALF], w4_first[:])
-        quantise_h(h10, 1, 0, 30 * KIB)
-        nc.vector.quantize_mx(w4_codes[:, HALF : 2 * N].bitcast(FP8X4), w4_scales[:, HALF : 2 * N], w4_rest[:])
-        tactile_passes(1, (4, 5), (6, 7))
-        first = [valve(n, 0, HALF, banks) for n, banks in enumerate(((0, 2), (1, 5), (3, 4)))]
-        quantise_h(h02, 0, HALF, 31 * KIB)
-        quantise_h(h03, 0, 768, 29 * KIB)
-        h12 = held([P, QUARTER, 4], BF16, "h12", tag="h1")
-        grasp_code(h12, 1, HALF, (4, 5), (6, 7))
+        quantise_h(h10, 1, 0, KIB)
+        quantise_h(h02, 0, HALF, KIB + HALF)
+        quantise_h(h03, 0, 768, KIB + 768)
+        w4_codes = [held([P, 2 * P], U32, "w4_codes%d" % n) for n in range(N // P)]
+        w4_scales = [held([P, 2 * P], U8, "w4_scales%d" % n) for n in range(N // P)]
+        for n in range(N // P):
+            nc.vector.quantize_mx(w4_codes[n][:].bitcast(FP8X4), w4_scales[n][:], w4_grouped[:, S * n : S * (n + 1)])
+        tactile_tiles((4, 5, 6, 7), (0, 3, 1, 2))
+        first = [valve(n, 0, HALF, banks) for n, banks in enumerate(((5, 4), (7, 6)))]
+        h12 = placed([P, QUARTER, 4], BF16, "h12", 10 * KIB)
+        grasp_code(h12, 1, HALF, (4, 5))
+        first.append(valve(2, 0, HALF, (5, 0)))
         gated = gate_drive(HALF, *first[0])
         quantise_h(h12, 1, HALF)
-        store(0, 0, HALF, gated, add_on_gpsimd, "h1")
-        h13 = held([P, QUARTER, 4], BF16, "h13")
-        grasp_code(h13, 1, 768, (6, 7), (6, 7))
-        second = [valve(n, HALF, QUARTER, (number,)) for n, number in enumerate((0, 1, 3))]
+        store(0, 0, HALF, gated, add_on_gpsimd, 10 * KIB)
+        second = [valve(n, HALF, QUARTER, (number,)) for n, number in enumerate((7, 3, 4))]
+        h13 = placed([P, QUARTER, 4], BF16, "h13", 12 * KIB)
+        grasp_code(h13, 1, 768, (6, 7))
         gated = gate_drive(HALF, *first[1])
         quantise_h(h13, 1, 768)
-        store(1, 0, HALF, gated, add_on_gpsimd, "h13")
-        store(2, 0, HALF, gate_drive(HALF, *first[2]), add_on_scalar)
-        third = [valve(n, 768, QUARTER, (number,)) for n, number in enumerate((2, 6, 5))]
-        for n in range(N // P):
-            store(n, HALF, QUARTER, gate_drive(QUARTER, *second[n]), add_on_gpsimd)
-        for n in range(N // P):
-            store(n, 768, QUARTER, gate_drive(QUARTER, *third[n]), add_on_scalar, None if n else "h_codes1_768")
+        store(1, 0, HALF, gated, add_on_scalar)
+        third = [valve(n, 768, QUARTER, (number,)) for n, number in enumerate((5, 1, 2))]
+        store(2, 0, HALF, gate_drive(HALF, *first[2]), add_on_gpsimd)
+        for n, add_bias in enumerate((add_on_gpsimd, add_on_gpsimd, add_on_scalar)):
+            store(n, HALF, QUARTER, gate_drive(QUARTER, *second[n]), add_bias)
+        for n, add_bias in enumerate((add_on_scalar, add_on_gpsimd, add_on_scalar)):
+            store(n, 768, QUARTER, gate_drive(QUARTER, *third[n]), add_bias)

@@ -92,7 +92,7 @@ def tile_list_soft_gripper_valves_kernel(
         tab2_picked = held([P, S], U8, "tab2_picked")
         nc.vector.tensor_copy(tab2_picked[:], tab2_rows[:].indirect(idx2[:]))
         move_rows(tab2_plane, tab2_picked, 48, 0, S)
-        tab_w = [placed([P, T], I32, "tab_w0", 0), None]
+        tab_w = [placed([P, T], I32, "tab_w0", 2 * KIB), None]
         nc.sync.dma_start(tab_w[0][:], tab_words[0].rearrange("p t i -> p (t i)").bitcast(I32))
 
         deal_w1_scales(0, HALF)
@@ -230,8 +230,7 @@ def tile_list_soft_gripper_valves_kernel(
             for t in range(4):
                 wide[0, jh, t] = bank(4 * jh + t, [P, HALF])
                 tactile_pass(wide[0, jh, t][:], 0, t, HALF * jh, HALF)
-        for jh in range(2):
-            copy_out(0, jh)
+        copy_out(0, 0)
 
         w2_late = [placed([P, 4, QUARTER], F32, "w2_late%d" % u, (56 + 4 * u) * KIB) for u in range(2)]
         for u in range(2):
@@ -240,6 +239,7 @@ def tile_list_soft_gripper_valves_kernel(
             )
         for jh in range(2):
             gather_v(0, jh)
+        copy_out(0, 1, 17 * KIB)
         pressure_tiles(0, range(8))
 
         w4_raw = [placed([P, 4, N], F32, "w4_raw%d" % b, 10 * b * KIB) for b in range(2)]
@@ -330,14 +330,14 @@ def tile_list_soft_gripper_valves_kernel(
         grasp_code(h00, 0, 0, (0, 3, 1, 2), on_gpsimd=(3,))
         h02 = held([P, QUARTER, 4], BF16, "h02")
         grasp_code(h02, 0, HALF, (4, 5))
+        h03 = held([P, QUARTER, 4], BF16, "h03")
+        grasp_code(h03, 0, 768, (6, 7))
         wide_pressure(0, range(4), (0, 3, 1, 2))
         round_w2(w2_late[0], 1, 0, P // 2)
         round_w2(w2_late[1], 1, P // 2, P)
         copy_out(1, 0, 63 * KIB)
-        quantise_h(h00, 0, 0)
         quantise_w2(1)
-        h03 = placed([P, QUARTER, 4], BF16, "h03", 60 * KIB)
-        grasp_code(h03, 0, 768, (6, 7))
+        quantise_h(h00, 0, 0, 60 * KIB)
 
         w4_grouped = placed([P, 2 * 4 * N], BF16, "w4_grouped", 73 * KIB)
         nc.gpsimd.tensor_scalar(
@@ -345,9 +345,11 @@ def tile_list_soft_gripper_valves_kernel(
             w4_raw[0][:].rearrange("p i (n c) -> p n c i", c=P),
             1.0, 0.0, MULT, ADD,
         )
-        for t, number in enumerate((0, 3, 1, 2)):
-            tactile_tiles((t,), (number,))
-            wide_pressure(1, (t,), (4 + t,))
+        wide_pressure(1, (0, 1), (4, 5))
+        tactile_tiles((0, 1, 2), (6, 7, 0))
+        wide_pressure(1, (2,), (1,))
+        tactile_tiles((3,), (3,))
+        wide_pressure(1, (3,), (2,))
         h10 = held([P, HALF, 4], BF16, "h10")
         grasp_code(h10, 1, 0, range(4))
         copy_out(1, 1)
@@ -364,21 +366,21 @@ def tile_list_soft_gripper_valves_kernel(
         w4_scales = [held([P, 2 * P], U8, "w4_scales%d" % n) for n in range(N // P)]
         for n in range(N // P):
             nc.vector.quantize_mx(w4_codes[n][:].bitcast(FP8X4), w4_scales[n][:], w4_grouped[:, S * n : S * (n + 1)])
-        tactile_tiles((4, 5, 6, 7), (0, 3, 1, 2))
-        first = [valve(n, 0, HALF, banks) for n, banks in enumerate(((5, 4), (7, 6)))]
+        tactile_tiles((4, 5, 6, 7), (6, 7, 0, 3))
+        first = [valve(n, 0, HALF, banks) for n, banks in enumerate(((5, 4), (2, 1)))]
         h12 = placed([P, QUARTER, 4], BF16, "h12", 10 * KIB)
         grasp_code(h12, 1, HALF, (4, 5))
-        first.append(valve(2, 0, HALF, (5, 0)))
+        first.append(valve(2, 0, HALF, (5, 6)))
         gated = gate_drive(HALF, *first[0])
         quantise_h(h12, 1, HALF)
         store(0, 0, HALF, gated, add_on_gpsimd, 10 * KIB)
-        second = [valve(n, HALF, QUARTER, (number,)) for n, number in enumerate((7, 3, 4))]
+        second = [valve(n, HALF, QUARTER, (number,)) for n, number in enumerate((2, 7, 4))]
         h13 = placed([P, QUARTER, 4], BF16, "h13", 12 * KIB)
         grasp_code(h13, 1, 768, (6, 7))
         gated = gate_drive(HALF, *first[1])
         quantise_h(h13, 1, 768)
         store(1, 0, HALF, gated, add_on_scalar)
-        third = [valve(n, 768, QUARTER, (number,)) for n, number in enumerate((5, 1, 2))]
+        third = [valve(n, 768, QUARTER, (number,)) for n, number in enumerate((5, 0, 3))]
         store(2, 0, HALF, gate_drive(HALF, *first[2]), add_on_gpsimd)
         for n, add_bias in enumerate((add_on_gpsimd, add_on_gpsimd, add_on_scalar)):
             store(n, HALF, QUARTER, gate_drive(QUARTER, *second[n]), add_bias)

@@ -23,7 +23,7 @@ HALF = 512
 QUARTER = 256
 JT = 128
 KIB = 1024
-TAB_AT, W1_AT, STAGED = 0, S, S + H
+TAB_AT, W1_AT, STAGED = 0, S, S + HALF
 
 
 def tile_list_soft_gripper_valves_kernel(
@@ -52,24 +52,36 @@ def tile_list_soft_gripper_valves_kernel(
 
         tab2_rows = placed([P, T], U8, "tab2_rows", 0)
         tab_rows = placed([P, T], U8, "tab_rows", 50 * KIB)
-        w1_rows = held([P, H], U8, "w1_rows")
+        w1_rows = [held([P, HALF], U8, "w1_rows0"), placed([P, H], U8, "w1_rows1", 86 * KIB)]
         staged = held([P, STAGED], U8, "staged")
         tab2_plane = held([P, S], U8, "tab2_plane")
         planes = [held([P, STAGED], U8, "planes0"), None]
+        late = held([P, H], U8, "late")
 
         for engine, lo, hi in ((nc.vector, 0, 48), (nc.gpsimd, 64, P)):
             engine.memset(tab2_rows[lo:hi, :].bitcast(I32), 0)
-        nc.vector.memset(w1_rows[0:96, :].bitcast(I32), 0)
+        nc.vector.memset(w1_rows[0][0:96, :].bitcast(I32), 0)
         nc.vector.memset(tab_rows[0:96, :].bitcast(I32), 0)
         nc.gpsimd.memset(tab2_plane[:].bitcast(I32), 0)
         nc.gpsimd.memset(planes[0][:].bitcast(I32), 0)
+        for engine, lo, hi in ((nc.vector, 0, 48), (nc.gpsimd, 64, P)):
+            engine.memset(w1_rows[1][lo:hi, :].bitcast(I32), 0)
+        nc.gpsimd.memset(late[:].bitcast(I32), 0)
+
+        w1_scale_words = w1_scales.bitcast(I32)
 
         w1_word_rows = w1_words.bitcast(I32).rearrange("a p w -> p a w")
         nc.sync.dma_start(tab2_rows[48:64, :].bitcast(I32), tab2_scales[0].bitcast(I32))
         nc.sync.dma_start(idx2[:], offs2)
         nc.sync.dma_start(tab_rows[96:128, :].bitcast(I32), tab_scales.rearrange("a q t -> (a q) t").bitcast(I32))
         nc.sync.dma_start(idx[:], offs)
-        nc.sync.dma_start(w1_rows[96:128, :].bitcast(I32), w1_scales.bitcast(I32).rearrange("a q c -> (a q) c"))
+        nc.sync.dma_start(
+            w1_rows[0][96:128, :].bitcast(I32), w1_scale_words.rearrange("a q c -> (a q) c")[:, 0 : HALF // 4]
+        )
+        nc.sync.dma_start(
+            w1_rows[1][48:64, :].bitcast(I32).rearrange("q (a c) -> q a c", a=2),
+            w1_scale_words.rearrange("a q c -> q a c")[:, :, HALF // 4 : H // 4],
+        )
         w2_first = held([P, 4, HALF], F32, "w2_first")
         nc.sync.dma_start(w2_first[:], w2[:, 0:HALF].rearrange("(p i) c -> p i c", i=4))
         tab2_w = placed([P, T // 2], I32, "tab2_w", 56 * KIB)
@@ -77,10 +89,10 @@ def tile_list_soft_gripper_valves_kernel(
         w1_raw = [held([P, 2, QUARTER], I32, "w1_raw0"), None]
         nc.sync.dma_start(w1_raw[0][:], w1_word_rows[:, :, 0:QUARTER])
 
-        def deal_w1_scales(lo, hi):
+        def deal_w1_scales(dealt, rows):
             nc.vector.tensor_copy(
-                staged[:, W1_AT + lo : W1_AT + hi].rearrange("p (b t c i) -> p c b t i", c=8, t=4, i=16),
-                w1_rows[:, lo:hi].rearrange("p (b c i t) -> p c b t i", c=8, t=4, i=16),
+                dealt.rearrange("p (b t c i) -> p c b t i", c=8, t=4, i=16),
+                rows.rearrange("p (b c i t) -> p c b t i", c=8, t=4, i=16),
             )
 
         def move_rows(plane, source, first, lo, hi):
@@ -95,20 +107,21 @@ def tile_list_soft_gripper_valves_kernel(
         tab_w = [placed([P, T], I32, "tab_w0", 2 * KIB), None]
         nc.sync.dma_start(tab_w[0][:], tab_words[0].rearrange("p t i -> p (t i)").bitcast(I32))
 
-        deal_w1_scales(0, HALF)
         tab_picked = placed([P, S], U8, "tab_picked", 32 * KIB)
         nc.vector.tensor_copy(tab_picked[:], tab_rows[:].indirect(idx[:]))
-        deal_w1_scales(HALF, H)
+        deal_w1_scales(staged[:, W1_AT:STAGED], w1_rows[0][:])
         nc.vector.tensor_copy(staged[:, TAB_AT:W1_AT].bitcast(I32), tab_picked[:].bitcast(I32))
         move_rows(planes[0], staged, 96, 0, STAGED)
         tab_w[1] = placed([P, T], I32, "tab_w1", 32 * KIB + 768)
         nc.sync.dma_start(tab_w[1][:], tab_words[1].rearrange("p t i -> p (t i)").bitcast(I32))
-        planes[1] = placed([P, STAGED], U8, "planes1", 30 * KIB + QUARTER)
+        planes[1] = placed([P, STAGED], U8, "planes1", 30 * KIB + 768)
         nc.vector.memset(planes[1][:].bitcast(I32), 0)
         move_rows(planes[1], staged, 112, 0, STAGED)
 
         def w1_scales_of(a, b, t):
-            return planes[a][:, W1_AT + HALF * b + P * t : W1_AT + HALF * b + P * (t + 1)]
+            if b == 0:
+                return planes[a][:, W1_AT + P * t : W1_AT + P * (t + 1)]
+            return late[:, HALF * a + P * t : HALF * a + P * (t + 1)]
 
         w2_grouped = [placed([P, 4 * HALF], BF16, "w2_grouped0", 80 * KIB), placed([P, 4 * HALF], BF16, "w2_grouped1", 72 * KIB)]
         w2_codes = [held([P, HALF], U32, "w2_codes%d" % b) for b in range(2)]
@@ -134,9 +147,13 @@ def tile_list_soft_gripper_valves_kernel(
 
         v, v2 = {}, {}
 
-        def gather_v(a, jh):
+        def gather_v(a, jh, width=HALF):
             v[a, jh] = held([P, HALF], U32, "v%d%d" % (a, jh))
-            nc.vector.tensor_copy(v[a, jh][:], tab_w[a][:].bitcast(U32).indirect(idx[:, 32 * jh : 32 * (jh + 1)]))
+            for lo in range(0, HALF, width):
+                at = (HALF * jh + lo) // 16
+                nc.vector.tensor_copy(
+                    v[a, jh][:, lo : lo + width], tab_w[a][:].bitcast(U32).indirect(idx[:, at : at + width // 16])
+                )
 
         def gather_v2(jh):
             v2[jh] = placed([P, 2 * HALF], U8, "v2%d" % jh, (84, 82)[jh] * KIB)
@@ -232,11 +249,18 @@ def tile_list_soft_gripper_valves_kernel(
                 tactile_pass(wide[0, jh, t][:], 0, t, HALF * jh, HALF)
         copy_out(0, 0)
 
-        w2_late = [placed([P, 4, QUARTER], F32, "w2_late%d" % u, (56 + 4 * u) * KIB) for u in range(2)]
-        for u in range(2):
+        w2_late = [placed([P, 4, QUARTER], F32, "w2_late%d" % u, (56, 86)[u] * KIB) for u in range(2)]
+
+        def load_w2_late(u):
             nc.sync.dma_start(
                 w2_late[u][:], w2[:, HALF + QUARTER * u : HALF + QUARTER * (u + 1)].rearrange("(p i) c -> p i c", i=4)
             )
+
+        load_w2_late(0)
+        staged_late = placed([P, H], U8, "staged_late", 60 * KIB)
+        deal_w1_scales(staged_late[:], w1_rows[1][:])
+        move_rows(late, staged_late, 48, 0, H)
+        load_w2_late(1)
         for jh in range(2):
             gather_v(0, jh)
         copy_out(0, 1, 17 * KIB)
@@ -265,8 +289,8 @@ def tile_list_soft_gripper_valves_kernel(
             nc.sync.dma_start(bias[:], bv.rearrange("(c p) -> p c", p=P))
 
         for jh in range(2):
-            gather_v(1, jh)
-        pressure_tiles(1, (0, 3, 1, 2, 4, 5, 6, 7))
+            gather_v(1, jh, QUARTER)
+        pressure_tiles(1, range(8))
         deal_w1_words(1)
 
         h_codes = {}
@@ -327,17 +351,17 @@ def tile_list_soft_gripper_valves_kernel(
             nc.sync.dma_start(out[P * n : P * (n + 1), lo : lo + width], result[:])
 
         h00 = placed([P, HALF, 4], BF16, "h00", 76 * KIB)
-        grasp_code(h00, 0, 0, (0, 3, 1, 2), on_gpsimd=(3,))
+        grasp_code(h00, 0, 0, range(4), on_gpsimd=(1,))
         h02 = held([P, QUARTER, 4], BF16, "h02")
         grasp_code(h02, 0, HALF, (4, 5))
         h03 = held([P, QUARTER, 4], BF16, "h03")
         grasp_code(h03, 0, 768, (6, 7))
-        wide_pressure(0, range(4), (0, 3, 1, 2))
+        wide_pressure(0, range(4), range(4))
         round_w2(w2_late[0], 1, 0, P // 2)
         round_w2(w2_late[1], 1, P // 2, P)
-        copy_out(1, 0, 63 * KIB)
+        copy_out(1, 0, 89 * KIB)
         quantise_w2(1)
-        quantise_h(h00, 0, 0, 60 * KIB)
+        quantise_h(h00, 0, 0, 86 * KIB)
 
         w4_grouped = placed([P, 2 * 4 * N], BF16, "w4_grouped", 73 * KIB)
         nc.gpsimd.tensor_scalar(
@@ -347,9 +371,9 @@ def tile_list_soft_gripper_valves_kernel(
         )
         wide_pressure(1, (0, 1), (4, 5))
         tactile_tiles((0, 1, 2), (6, 7, 0))
-        wide_pressure(1, (2,), (1,))
-        tactile_tiles((3,), (3,))
-        wide_pressure(1, (3,), (2,))
+        wide_pressure(1, (2,), (2,))
+        tactile_tiles((3,), (1,))
+        wide_pressure(1, (3,), (3,))
         h10 = held([P, HALF, 4], BF16, "h10")
         grasp_code(h10, 1, 0, range(4))
         copy_out(1, 1)
@@ -366,21 +390,21 @@ def tile_list_soft_gripper_valves_kernel(
         w4_scales = [held([P, 2 * P], U8, "w4_scales%d" % n) for n in range(N // P)]
         for n in range(N // P):
             nc.vector.quantize_mx(w4_codes[n][:].bitcast(FP8X4), w4_scales[n][:], w4_grouped[:, S * n : S * (n + 1)])
-        tactile_tiles((4, 5, 6, 7), (6, 7, 0, 3))
-        first = [valve(n, 0, HALF, banks) for n, banks in enumerate(((5, 4), (2, 1)))]
+        tactile_tiles((4, 5, 6, 7), (6, 7, 0, 1))
+        first = [valve(n, 0, HALF, banks) for n, banks in enumerate(((5, 4), (3, 2)))]
         h12 = placed([P, QUARTER, 4], BF16, "h12", 10 * KIB)
         grasp_code(h12, 1, HALF, (4, 5))
         first.append(valve(2, 0, HALF, (5, 6)))
         gated = gate_drive(HALF, *first[0])
         quantise_h(h12, 1, HALF)
         store(0, 0, HALF, gated, add_on_gpsimd, 10 * KIB)
-        second = [valve(n, HALF, QUARTER, (number,)) for n, number in enumerate((2, 7, 4))]
+        second = [valve(n, HALF, QUARTER, (number,)) for n, number in enumerate((3, 7, 4))]
         h13 = placed([P, QUARTER, 4], BF16, "h13", 12 * KIB)
         grasp_code(h13, 1, 768, (6, 7))
         gated = gate_drive(HALF, *first[1])
         quantise_h(h13, 1, 768)
         store(1, 0, HALF, gated, add_on_scalar)
-        third = [valve(n, 768, QUARTER, (number,)) for n, number in enumerate((5, 0, 3))]
+        third = [valve(n, 768, QUARTER, (number,)) for n, number in enumerate((5, 0, 1))]
         store(2, 0, HALF, gate_drive(HALF, *first[2]), add_on_gpsimd)
         for n, add_bias in enumerate((add_on_gpsimd, add_on_gpsimd, add_on_scalar)):
             store(n, HALF, QUARTER, gate_drive(QUARTER, *second[n]), add_bias)

@@ -39,10 +39,10 @@ def tile_list_soft_gripper_valves_kernel(
         psum = ctx.enter_context(tc.psum_pool(name="psum", bufs=1))
 
         def held(shape, dtype, name, tag=None):
-            return keep.tile(shape, dtype, name=name, tag=tag or name, align_bytes=64)
+            return keep.tile(shape, dtype, name=name, tag=tag or name, align_bytes=256)
 
         def placed(shape, dtype, name, at):
-            return laid.tile(shape, dtype, name=name, tag=name, align_bytes=64, offset=at)
+            return laid.tile(shape, dtype, name=name, tag=name, align_bytes=256, offset=at)
 
         def bank(number, shape):
             return psum.tile(shape, F32, name="bank%d" % number, tag="bank%d" % number)
@@ -114,9 +114,8 @@ def tile_list_soft_gripper_valves_kernel(
         move_rows(planes[0], staged, 96, 0, STAGED)
         tab_w[1] = placed([P, T], I32, "tab_w1", 32 * KIB + 768)
         nc.sync.dma_start(tab_w[1][:], tab_words[1].rearrange("p t i -> p (t i)").bitcast(I32))
-        planes[1] = placed([P, STAGED], U8, "planes1", 30 * KIB + 768)
-        nc.vector.memset(planes[1][:].bitcast(I32), 0)
-        move_rows(planes[1], staged, 112, 0, STAGED)
+        w1_raw[1] = placed([P, 2, QUARTER], I32, "w1_raw1", 30 * KIB + QUARTER)
+        nc.sync.dma_start(w1_raw[1][:], w1_word_rows[:, :, QUARTER:HALF])
 
         def w1_scales_of(a, b, t):
             if b == 0:
@@ -218,7 +217,7 @@ def tile_list_soft_gripper_valves_kernel(
                 sums = tiles[b, jt]
                 records = slice(JT * jl, JT * (jl + 1))
                 if jt in on_gpsimd:
-                    woven = placed([P, JT, 4], F32, "woven", 80 * KIB)
+                    woven = placed([P, JT, 4], F32, "woven", 30 * KIB + QUARTER)
                     nc.scalar.copy(
                         woven[:].rearrange("p (c i) t -> p c t i", i=2), sums[:].rearrange("p t (c i) -> p c t i", i=2)
                     )
@@ -240,9 +239,10 @@ def tile_list_soft_gripper_valves_kernel(
         deal_w1_words(0)
         gather_v2(0)
         quantise_w2(0)
+        planes[1] = placed([P, STAGED], U8, "planes1", 80 * KIB)
+        nc.vector.memset(planes[1][:].bitcast(I32), 0)
+        move_rows(planes[1], staged, 112, 0, STAGED)
         gather_v2(1)
-        w1_raw[1] = placed([P, 2, QUARTER], I32, "w1_raw1", 80 * KIB)
-        nc.sync.dma_start(w1_raw[1][:], w1_word_rows[:, :, QUARTER:HALF])
         for jh in range(2):
             for t in range(4):
                 wide[0, jh, t] = bank(4 * jh + t, [P, HALF])
@@ -346,7 +346,7 @@ def tile_list_soft_gripper_valves_kernel(
             if at:
                 result = placed([P, width], F32, "result_held", at)
             else:
-                result = ring.tile([P, width], F32, name="result")
+                result = ring.tile([P, width], F32, name="result", align_bytes=256)
             add_bias(result[:], gated[:], bias[:, n : n + 1])
             nc.sync.dma_start(out[P * n : P * (n + 1), lo : lo + width], result[:])
 

@@ -50,9 +50,9 @@ def tile_list_soft_gripper_valves_kernel(
         idx = lists.tile([P, S // 16], U16, name="idx")
         idx2 = lists.tile([P, S // 16], U16, name="idx2")
 
-        tab2_rows = placed([P, T], U8, "tab2_rows", 0)
-        tab_rows = placed([P, T], U8, "tab_rows", 50 * KIB)
-        w1_rows = [held([P, HALF], U8, "w1_rows0"), placed([P, H], U8, "w1_rows1", 86 * KIB)]
+        tab2_rows = placed([P, T], U8, "tab2_rows", 6 * KIB)
+        tab_rows = held([P, T], U8, "tab_rows")
+        w1_rows = [held([P, HALF], U8, "w1_rows0"), placed([P, H], U8, "w1_rows1", 90 * KIB)]
         staged = held([P, STAGED], U8, "staged")
         tab2_plane = held([P, S], U8, "tab2_plane")
         planes = [held([P, STAGED], U8, "planes0"), None]
@@ -84,10 +84,11 @@ def tile_list_soft_gripper_valves_kernel(
         )
         w2_first = held([P, 4, HALF], F32, "w2_first")
         nc.sync.dma_start(w2_first[:], w2[:, 0:HALF].rearrange("(p i) c -> p i c", i=4))
-        tab2_w = placed([P, T // 2], I32, "tab2_w", 56 * KIB)
+        tab2_w = placed([P, T // 2], I32, "tab2_w", 60 * KIB)
         nc.sync.dma_start(tab2_w[:], tab2_words[0].bitcast(I32))
-        w1_raw = [held([P, 2, QUARTER], I32, "w1_raw0"), None]
-        nc.sync.dma_start(w1_raw[0][:], w1_word_rows[:, :, 0:QUARTER])
+        w1_first = held([P, 2, QUARTER], I32, "w1_first")
+        nc.sync.dma_start(w1_first[:], w1_word_rows[:, :, 0:QUARTER])
+        w1_raw = {(0, a): w1_first[:, a, :] for a in range(2)}
 
         def deal_w1_scales(dealt, rows):
             nc.vector.tensor_copy(
@@ -104,27 +105,27 @@ def tile_list_soft_gripper_valves_kernel(
         tab2_picked = held([P, S], U8, "tab2_picked")
         nc.vector.tensor_copy(tab2_picked[:], tab2_rows[:].indirect(idx2[:]))
         move_rows(tab2_plane, tab2_picked, 48, 0, S)
-        tab_w = [placed([P, T], I32, "tab_w0", 2 * KIB), None]
+        tab_w = [placed([P, T], I32, "tab_w0", 9 * KIB + 768), None]
         nc.sync.dma_start(tab_w[0][:], tab_words[0].rearrange("p t i -> p (t i)").bitcast(I32))
 
-        tab_picked = placed([P, S], U8, "tab_picked", 32 * KIB)
+        tab_picked = placed([P, S], U8, "tab_picked", 40 * KIB)
         nc.vector.tensor_copy(tab_picked[:], tab_rows[:].indirect(idx[:]))
         deal_w1_scales(staged[:, W1_AT:STAGED], w1_rows[0][:])
         nc.vector.tensor_copy(staged[:, TAB_AT:W1_AT].bitcast(I32), tab_picked[:].bitcast(I32))
         move_rows(planes[0], staged, 96, 0, STAGED)
-        tab_w[1] = placed([P, T], I32, "tab_w1", 32 * KIB + 768)
+        tab_w[1] = placed([P, T], I32, "tab_w1", 40 * KIB + 768)
         nc.sync.dma_start(tab_w[1][:], tab_words[1].rearrange("p t i -> p (t i)").bitcast(I32))
-        w1_raw[1] = placed([P, 2, QUARTER], I32, "w1_raw1", 30 * KIB + QUARTER)
-        nc.sync.dma_start(w1_raw[1][:], w1_word_rows[:, :, QUARTER:HALF])
+        w1_raw[1, 0] = placed([P, QUARTER], I32, "w1_raw10", 39 * KIB + QUARTER)
+        nc.sync.dma_start(w1_raw[1, 0][:], w1_word_rows[:, 0, QUARTER:HALF])
 
         def w1_scales_of(a, b, t):
             if b == 0:
                 return planes[a][:, W1_AT + P * t : W1_AT + P * (t + 1)]
             return late[:, HALF * a + P * t : HALF * a + P * (t + 1)]
 
-        w2_grouped = [placed([P, 4 * HALF], BF16, "w2_grouped0", 80 * KIB), placed([P, 4 * HALF], BF16, "w2_grouped1", 72 * KIB)]
+        w2_grouped = [placed([P, 4 * HALF], BF16, "w2_grouped0", 84 * KIB), placed([P, 4 * HALF], BF16, "w2_grouped1", 76 * KIB)]
         w2_codes = [held([P, HALF], U32, "w2_codes%d" % b) for b in range(2)]
-        w2_scales = [placed([P, HALF], U8, "w2_scales0", 32 * KIB + QUARTER), held([P, HALF], U8, "w2_scales1")]
+        w2_scales = [placed([P, HALF], U8, "w2_scales0", 40 * KIB + QUARTER), held([P, HALF], U8, "w2_scales1")]
 
         def round_w2(raw, b, lo, hi):
             nc.scalar.copy(
@@ -141,7 +142,7 @@ def tile_list_soft_gripper_valves_kernel(
             for a in range(2):
                 nc.scalar.copy(
                     w1_codes[b][:, a, :].bitcast(U16).rearrange("p (t c i) -> p c t i", t=4, i=8),
-                    w1_raw[b][:, a, :].bitcast(U16).rearrange("p (c i t) -> p c t i", t=4, i=8),
+                    w1_raw[b, a][:].bitcast(U16).rearrange("p (c i t) -> p c t i", t=4, i=8),
                 )
 
         v, v2 = {}, {}
@@ -155,7 +156,7 @@ def tile_list_soft_gripper_valves_kernel(
                 )
 
         def gather_v2(jh):
-            v2[jh] = placed([P, 2 * HALF], U8, "v2%d" % jh, (84, 82)[jh] * KIB)
+            v2[jh] = placed([P, 2 * HALF], U8, "v2%d" % jh, (88, 86)[jh] * KIB)
             nc.vector.tensor_copy(
                 v2[jh][:].bitcast(U16), tab2_w[:].bitcast(U16).indirect(idx2[:, 32 * jh : 32 * (jh + 1)])
             )
@@ -186,11 +187,14 @@ def tile_list_soft_gripper_valves_kernel(
 
         copied, wide, tiles = {}, {}, {}
 
+        def copy_slots(b, jh, slots):
+            for t in slots:
+                nc.scalar.copy(copied[b, jh][:, t, :], wide[b, jh, t][:])
+
         def copy_out(b, jh, at=None):
             name = "copied%d%d" % (b, jh)
             copied[b, jh] = held([P, 4, HALF], F32, name) if at is None else placed([P, 4, HALF], F32, name, at)
-            for t in range(4):
-                nc.scalar.copy(copied[b, jh][:, t, :], wide[b, jh, t][:])
+            copy_slots(b, jh, range(4))
 
         def wide_pressure(jh, slots, banks):
             for t, number in zip(slots, banks):
@@ -217,7 +221,7 @@ def tile_list_soft_gripper_valves_kernel(
                 sums = tiles[b, jt]
                 records = slice(JT * jl, JT * (jl + 1))
                 if jt in on_gpsimd:
-                    woven = placed([P, JT, 4], F32, "woven", 30 * KIB + QUARTER)
+                    woven = placed([P, JT, 4], F32, "woven", 65 * KIB)
                     nc.scalar.copy(
                         woven[:].rearrange("p (c i) t -> p c t i", i=2), sums[:].rearrange("p t (c i) -> p c t i", i=2)
                     )
@@ -239,7 +243,7 @@ def tile_list_soft_gripper_valves_kernel(
         deal_w1_words(0)
         gather_v2(0)
         quantise_w2(0)
-        planes[1] = placed([P, STAGED], U8, "planes1", 80 * KIB)
+        planes[1] = placed([P, STAGED], U8, "planes1", 84 * KIB)
         nc.vector.memset(planes[1][:].bitcast(I32), 0)
         move_rows(planes[1], staged, 112, 0, STAGED)
         gather_v2(1)
@@ -249,42 +253,44 @@ def tile_list_soft_gripper_valves_kernel(
                 tactile_pass(wide[0, jh, t][:], 0, t, HALF * jh, HALF)
         copy_out(0, 0)
 
-        w2_late = [placed([P, 4, QUARTER], F32, "w2_late%d" % u, (56, 86)[u] * KIB) for u in range(2)]
+        w2_late = [placed([P, 4, QUARTER], F32, "w2_late%d" % u, (60, 90)[u] * KIB) for u in range(2)]
 
         def load_w2_late(u):
             nc.sync.dma_start(
                 w2_late[u][:], w2[:, HALF + QUARTER * u : HALF + QUARTER * (u + 1)].rearrange("(p i) c -> p i c", i=4)
             )
 
+        w1_raw[1, 1] = placed([P, QUARTER], I32, "w1_raw11", 65 * KIB)
+        nc.sync.dma_start(w1_raw[1, 1][:], w1_word_rows[:, 1, QUARTER:HALF])
         load_w2_late(0)
-        staged_late = placed([P, H], U8, "staged_late", 60 * KIB)
+        staged_late = placed([P, H], U8, "staged_late", 64 * KIB)
         deal_w1_scales(staged_late[:], w1_rows[1][:])
         move_rows(late, staged_late, 48, 0, H)
         load_w2_late(1)
         for jh in range(2):
             gather_v(0, jh)
-        copy_out(0, 1, 17 * KIB)
+        copy_out(0, 1, 25 * KIB + HALF)
         pressure_tiles(0, range(8))
 
-        w4_raw = [placed([P, 4, N], F32, "w4_raw%d" % b, 10 * b * KIB) for b in range(2)]
-
-        def load_w4(b):
-            nc.sync.dma_start(
-                w4_raw[b][:].rearrange("p i n -> p (i n)"),
-                w4[HALF * b : HALF * (b + 1), :].rearrange("(p i) n -> p (i n)", i=4),
-            )
-
-        load_w4(0)
-        w3_codes = placed([P, 2, N], I32, "w3_codes", 6 * KIB)
+        w4_raw = placed([P, 4, N], F32, "w4_raw", 4 * KIB)
+        nc.sync.dma_start(
+            w4_raw[:].rearrange("p i n -> p (i n)"), w4[0:HALF, :].rearrange("(p i) n -> p (i n)", i=4)
+        )
+        w3_codes = placed([P, 2, N], I32, "w3_codes", 21 * KIB + 768)
         nc.sync.dma_start(w3_codes[:], w3_words.rearrange("a p c i -> p a (c i)").bitcast(I32))
-        w3_planes = placed([P, N], U8, "w3_planes", 9 * KIB + QUARTER)
+        w3_planes = placed([P, N], U8, "w3_planes", 25 * KIB)
         nc.vector.memset(w3_planes[:].bitcast(I32), 0)
         for q in range(4):
             nc.sync.dma_start(
                 w3_planes[32 * q + 4 : 32 * q + 12, :].bitcast(I32), w3_scales.bitcast(I32)[:, 4 * q : 4 * q + 4, :]
             )
-        load_w4(1)
-        bias = placed([P, N // P], F32, "bias", 9 * KIB)
+        w4_rows = w4[HALF:H, :].rearrange("(p i) n -> p i n", i=4)
+        copied[1, 1] = placed([P, 4, HALF], F32, "copied11", 13 * KIB + 768)
+        w4_pair = copied[1, 1][:, 2:4, :].rearrange("p u (v n) -> p (u v) n", v=2)
+        nc.sync.dma_start(w4_pair, w4_rows[:, :, 0:QUARTER])
+        w4_last = placed([P, 4, P], F32, "w4_last", 10 * KIB)
+        nc.sync.dma_start(w4_last[:], w4_rows[:, :, QUARTER:N])
+        bias = placed([P, N // P], F32, "bias", 24 * KIB + 768)
         with nc.allow_non_contiguous_dma(reason="one bias value a partition"):
             nc.sync.dma_start(bias[:], bv.rearrange("(c p) -> p c", p=P))
 
@@ -322,7 +328,7 @@ def tile_list_soft_gripper_valves_kernel(
                 o_sum, d_sum = both[:, 0, :], both[:, 1, :]
             cols = slice(P * n, P * (n + 1))
             for b in range(2):
-                valve_pass(o_sum, w4_codes[n][:, P * b : P * (b + 1)], w4_scales[n][:, P * b : P * (b + 1)], b, lo, b == 0, b == 1 and apart)
+                valve_pass(o_sum, w4_codes[b][:, cols], w4_scales[b][:, cols], b, lo, b == 0, b == 1 and apart)
                 valve_pass(
                     d_sum, w3_codes[:, b, cols], w3_planes[4 + 4 * b : P, cols],
                     b, lo, b == 0 and apart, b == 1,
@@ -344,13 +350,13 @@ def tile_list_soft_gripper_valves_kernel(
 
         def store(n, lo, width, gated, add_bias, at=None):
             if at:
-                result = placed([P, width], F32, "result_held", at)
+                result = placed([P, width], F32, "result_held%d" % n, at)
             else:
                 result = ring.tile([P, width], F32, name="result", align_bytes=256)
             add_bias(result[:], gated[:], bias[:, n : n + 1])
             nc.sync.dma_start(out[P * n : P * (n + 1), lo : lo + width], result[:])
 
-        h00 = placed([P, HALF, 4], BF16, "h00", 76 * KIB)
+        h00 = placed([P, HALF, 4], BF16, "h00", 80 * KIB)
         grasp_code(h00, 0, 0, range(4), on_gpsimd=(1,))
         h02 = held([P, QUARTER, 4], BF16, "h02")
         grasp_code(h02, 0, HALF, (4, 5))
@@ -359,14 +365,14 @@ def tile_list_soft_gripper_valves_kernel(
         wide_pressure(0, range(4), range(4))
         round_w2(w2_late[0], 1, 0, P // 2)
         round_w2(w2_late[1], 1, P // 2, P)
-        copy_out(1, 0, 89 * KIB)
+        copy_out(1, 0, 93 * KIB)
         quantise_w2(1)
-        quantise_h(h00, 0, 0, 86 * KIB)
+        quantise_h(h00, 0, 0, 90 * KIB)
 
-        w4_grouped = placed([P, 2 * 4 * N], BF16, "w4_grouped", 73 * KIB)
+        w4_first = placed([P, 4 * N], BF16, "w4_first", 78 * KIB)
         nc.gpsimd.tensor_scalar(
-            w4_grouped[:].rearrange("p (n b c i) -> p n b c i", b=2, c=P, i=4)[:, :, 0, :, :],
-            w4_raw[0][:].rearrange("p i (n c) -> p n c i", c=P),
+            w4_first[:].rearrange("p (n i) -> p n i", i=4),
+            w4_raw[:].rearrange("p i n -> p n i"),
             1.0, 0.0, MULT, ADD,
         )
         wide_pressure(1, (0, 1), (4, 5))
@@ -376,37 +382,50 @@ def tile_list_soft_gripper_valves_kernel(
         wide_pressure(1, (3,), (3,))
         h10 = held([P, HALF, 4], BF16, "h10")
         grasp_code(h10, 1, 0, range(4))
-        copy_out(1, 1)
-        for n in range(N // P):
+        w4_late = [held([P, 4 * P], BF16, "w4_late%d" % n) for n in range(N // P)]
+
+        def round_w4_late(n, raw):
             nc.scalar.copy(
-                w4_grouped[:, HALF * (2 * n + 1) : HALF * (2 * n + 2)].rearrange("p (c m i) -> p c i m", m=4, i=4),
-                w4_raw[1][:, :, P * n : P * (n + 1)].rearrange("p i (c m) -> p c i m", m=4),
+                w4_late[n][:].rearrange("p (c m i) -> p c i m", m=4, i=4), raw.rearrange("p i (c m) -> p c i m", m=4)
             )
 
-        quantise_h(h10, 1, 0, KIB)
-        quantise_h(h02, 0, HALF, KIB + HALF)
-        quantise_h(h03, 0, 768, KIB + 768)
-        w4_codes = [held([P, 2 * P], U32, "w4_codes%d" % n) for n in range(N // P)]
-        w4_scales = [held([P, 2 * P], U8, "w4_scales%d" % n) for n in range(N // P)]
-        for n in range(N // P):
-            nc.vector.quantize_mx(w4_codes[n][:].bitcast(FP8X4), w4_scales[n][:], w4_grouped[:, S * n : S * (n + 1)])
+        copy_slots(1, 1, (0, 1))
+        for n in range(2):
+            round_w4_late(n, w4_pair[:, :, P * n : P * (n + 1)])
+        copy_slots(1, 1, (2, 3))
+        round_w4_late(2, w4_last[:])
+
+        w4_codes = [held([P, N], U32, "w4_codes%d" % b) for b in range(2)]
+        w4_scales = [placed([P, N], U8, "w4_scales%d" % b, 5 * KIB + HALF * b) for b in range(2)]
+
+        def quantise_w4_late(n):
+            cols = slice(P * n, P * (n + 1))
+            nc.vector.quantize_mx(w4_codes[1][:, cols].bitcast(FP8X4), w4_scales[1][:, cols], w4_late[n][:])
+
+        nc.vector.quantize_mx(w4_codes[0][:].bitcast(FP8X4), w4_scales[0][:], w4_first[:])
+        quantise_h(h10, 1, 0, 4 * KIB)
+        quantise_w4_late(0)
+        quantise_w4_late(1)
+        quantise_h(h02, 0, HALF, 4 * KIB + HALF)
+        quantise_h(h03, 0, 768, 4 * KIB + 768)
+        quantise_w4_late(2)
         tactile_tiles((4, 5, 6, 7), (6, 7, 0, 1))
         first = [valve(n, 0, HALF, banks) for n, banks in enumerate(((5, 4), (3, 2)))]
-        h12 = placed([P, QUARTER, 4], BF16, "h12", 10 * KIB)
+        h12 = placed([P, QUARTER, 4], BF16, "h12", 8 * KIB + QUARTER)
         grasp_code(h12, 1, HALF, (4, 5))
         first.append(valve(2, 0, HALF, (5, 6)))
         gated = gate_drive(HALF, *first[0])
         quantise_h(h12, 1, HALF)
-        store(0, 0, HALF, gated, add_on_gpsimd, 10 * KIB)
+        store(0, 0, HALF, gated, add_on_gpsimd, 8 * KIB + QUARTER)
         second = [valve(n, HALF, QUARTER, (number,)) for n, number in enumerate((3, 7, 4))]
-        h13 = placed([P, QUARTER, 4], BF16, "h13", 12 * KIB)
+        h13 = placed([P, QUARTER, 4], BF16, "h13", 11 * KIB + 768)
         grasp_code(h13, 1, 768, (6, 7))
         gated = gate_drive(HALF, *first[1])
         quantise_h(h13, 1, 768)
-        store(1, 0, HALF, gated, add_on_scalar)
+        store(1, 0, HALF, gated, add_on_gpsimd, 11 * KIB + 768)
         third = [valve(n, 768, QUARTER, (number,)) for n, number in enumerate((5, 0, 1))]
         store(2, 0, HALF, gate_drive(HALF, *first[2]), add_on_gpsimd)
-        for n, add_bias in enumerate((add_on_gpsimd, add_on_gpsimd, add_on_scalar)):
+        for n, add_bias in enumerate((add_on_scalar, add_on_gpsimd, add_on_scalar)):
             store(n, HALF, QUARTER, gate_drive(QUARTER, *second[n]), add_bias)
         for n, add_bias in enumerate((add_on_scalar, add_on_gpsimd, add_on_scalar)):
             store(n, 768, QUARTER, gate_drive(QUARTER, *third[n]), add_bias)

@@ -86,9 +86,8 @@ def tile_list_soft_gripper_valves_kernel(
         nc.sync.dma_start(w2_first[:], w2[:, 0:HALF].rearrange("(p i) c -> p i c", i=4))
         tab2_w = placed([P, T // 2], I32, "tab2_w", 60 * KIB)
         nc.sync.dma_start(tab2_w[:], tab2_words[0].bitcast(I32))
-        w1_first = held([P, 2, QUARTER], I32, "w1_first")
-        nc.sync.dma_start(w1_first[:], w1_word_rows[:, :, 0:QUARTER])
-        w1_raw = {(0, a): w1_first[:, a, :] for a in range(2)}
+        w1_raw = [held([P, 2, QUARTER], I32, "w1_raw0"), None]
+        nc.sync.dma_start(w1_raw[0][:], w1_word_rows[:, :, 0:QUARTER])
 
         def deal_w1_scales(dealt, rows):
             nc.vector.tensor_copy(
@@ -115,8 +114,8 @@ def tile_list_soft_gripper_valves_kernel(
         move_rows(planes[0], staged, 96, 0, STAGED)
         tab_w[1] = placed([P, T], I32, "tab_w1", 40 * KIB + 768)
         nc.sync.dma_start(tab_w[1][:], tab_words[1].rearrange("p t i -> p (t i)").bitcast(I32))
-        w1_raw[1, 0] = placed([P, QUARTER], I32, "w1_raw10", 39 * KIB + QUARTER)
-        nc.sync.dma_start(w1_raw[1, 0][:], w1_word_rows[:, 0, QUARTER:HALF])
+        w1_raw[1] = placed([P, 2, QUARTER], I32, "w1_raw1", 38 * KIB + QUARTER)
+        nc.sync.dma_start(w1_raw[1][:], w1_word_rows[:, :, QUARTER:HALF])
 
         def w1_scales_of(a, b, t):
             if b == 0:
@@ -142,7 +141,7 @@ def tile_list_soft_gripper_valves_kernel(
             for a in range(2):
                 nc.scalar.copy(
                     w1_codes[b][:, a, :].bitcast(U16).rearrange("p (t c i) -> p c t i", t=4, i=8),
-                    w1_raw[b, a][:].bitcast(U16).rearrange("p (c i t) -> p c t i", t=4, i=8),
+                    w1_raw[b][:, a, :].bitcast(U16).rearrange("p (c i t) -> p c t i", t=4, i=8),
                 )
 
         v, v2 = {}, {}
@@ -221,7 +220,7 @@ def tile_list_soft_gripper_valves_kernel(
                 sums = tiles[b, jt]
                 records = slice(JT * jl, JT * (jl + 1))
                 if jt in on_gpsimd:
-                    woven = placed([P, JT, 4], F32, "woven", 65 * KIB)
+                    woven = placed([P, JT, 4], F32, "woven", 38 * KIB + QUARTER)
                     nc.scalar.copy(
                         woven[:].rearrange("p (c i) t -> p c t i", i=2), sums[:].rearrange("p t (c i) -> p c t i", i=2)
                     )
@@ -260,8 +259,6 @@ def tile_list_soft_gripper_valves_kernel(
                 w2_late[u][:], w2[:, HALF + QUARTER * u : HALF + QUARTER * (u + 1)].rearrange("(p i) c -> p i c", i=4)
             )
 
-        w1_raw[1, 1] = placed([P, QUARTER], I32, "w1_raw11", 65 * KIB)
-        nc.sync.dma_start(w1_raw[1, 1][:], w1_word_rows[:, 1, QUARTER:HALF])
         load_w2_late(0)
         staged_late = placed([P, H], U8, "staged_late", 64 * KIB)
         deal_w1_scales(staged_late[:], w1_rows[1][:])
@@ -276,6 +273,12 @@ def tile_list_soft_gripper_valves_kernel(
         nc.sync.dma_start(
             w4_raw[:].rearrange("p i n -> p (i n)"), w4[0:HALF, :].rearrange("(p i) n -> p (i n)", i=4)
         )
+        w4_rows = w4[HALF:H, :].rearrange("(p i) n -> p i n", i=4)
+        copied[1, 1] = placed([P, 4, HALF], F32, "copied11", 13 * KIB + 768)
+        w4_pair = copied[1, 1][:, 2:4, :].rearrange("p u (v n) -> p (u v) n", v=2)
+        nc.sync.dma_start(w4_pair, w4_rows[:, :, 0:QUARTER])
+        w4_last = placed([P, 4, P], F32, "w4_last", 10 * KIB)
+        nc.sync.dma_start(w4_last[:], w4_rows[:, :, QUARTER:N])
         w3_codes = placed([P, 2, N], I32, "w3_codes", 21 * KIB + 768)
         nc.sync.dma_start(w3_codes[:], w3_words.rearrange("a p c i -> p a (c i)").bitcast(I32))
         w3_planes = placed([P, N], U8, "w3_planes", 25 * KIB)
@@ -284,12 +287,6 @@ def tile_list_soft_gripper_valves_kernel(
             nc.sync.dma_start(
                 w3_planes[32 * q + 4 : 32 * q + 12, :].bitcast(I32), w3_scales.bitcast(I32)[:, 4 * q : 4 * q + 4, :]
             )
-        w4_rows = w4[HALF:H, :].rearrange("(p i) n -> p i n", i=4)
-        copied[1, 1] = placed([P, 4, HALF], F32, "copied11", 13 * KIB + 768)
-        w4_pair = copied[1, 1][:, 2:4, :].rearrange("p u (v n) -> p (u v) n", v=2)
-        nc.sync.dma_start(w4_pair, w4_rows[:, :, 0:QUARTER])
-        w4_last = placed([P, 4, P], F32, "w4_last", 10 * KIB)
-        nc.sync.dma_start(w4_last[:], w4_rows[:, :, QUARTER:N])
         bias = placed([P, N // P], F32, "bias", 24 * KIB + 768)
         with nc.allow_non_contiguous_dma(reason="one bias value a partition"):
             nc.sync.dma_start(bias[:], bv.rearrange("(c p) -> p c", p=P))

@@ -368,8 +368,8 @@ def tile_list_soft_gripper_valves_kernel(
 
         w4_first = placed([P, 4 * N], BF16, "w4_first", 78 * KIB)
         nc.gpsimd.tensor_scalar(
-            w4_first[:].rearrange("p (n i) -> p n i", i=4),
-            w4_raw[:].rearrange("p i n -> p n i"),
+            w4_first[:, 0 : 4 * QUARTER].rearrange("p (n i) -> p n i", i=4),
+            w4_raw[:, :, 0:QUARTER].rearrange("p i n -> p n i"),
             1.0, 0.0, MULT, ADD,
         )
         wide_pressure(1, (0, 1), (4, 5))
@@ -387,6 +387,10 @@ def tile_list_soft_gripper_valves_kernel(
             )
 
         copy_slots(1, 1, (0, 1))
+        nc.scalar.copy(
+            w4_first[:, 4 * QUARTER : 4 * N].rearrange("p (c m i) -> p c i m", m=4, i=4),
+            w4_raw[:, :, QUARTER:N].rearrange("p i (c m) -> p c i m", m=4),
+        )
         for n in range(2):
             round_w4_late(n, w4_pair[:, :, P * n : P * (n + 1)])
         copy_slots(1, 1, (2, 3))

@@ -50,10 +50,10 @@ def tile_list_soft_gripper_valves_kernel(
         idx = lists.tile([P, S // 16], U16, name="idx")
         idx2 = lists.tile([P, S // 16], U16, name="idx2")
 
-        tab2_rows = placed([P, T], U8, "tab2_rows", 6 * KIB)
+        tab2_rows = placed([P, T], U8, "tab2_rows", 37 * KIB)
         tab_rows = held([P, T], U8, "tab_rows")
         w1_rows = [held([P, HALF], U8, "w1_rows0"), placed([P, H], U8, "w1_rows1", 90 * KIB)]
-        staged = held([P, STAGED], U8, "staged")
+        staged = placed([P, STAGED], U8, "staged", KIB)
         tab2_plane = held([P, S], U8, "tab2_plane")
         planes = [held([P, STAGED], U8, "planes0"), None]
         late = held([P, H], U8, "late")
@@ -104,17 +104,17 @@ def tile_list_soft_gripper_valves_kernel(
         tab2_picked = held([P, S], U8, "tab2_picked")
         nc.vector.tensor_copy(tab2_picked[:], tab2_rows[:].indirect(idx2[:]))
         move_rows(tab2_plane, tab2_picked, 48, 0, S)
-        tab_w = [placed([P, T], I32, "tab_w0", 9 * KIB + 768), None]
+        tab_w = [placed([P, T], I32, "tab_w0", 40 * KIB + 768), None]
         nc.sync.dma_start(tab_w[0][:], tab_words[0].rearrange("p t i -> p (t i)").bitcast(I32))
 
-        tab_picked = placed([P, S], U8, "tab_picked", 40 * KIB)
+        tab_picked = placed([P, S], U8, "tab_picked", 25 * KIB + HALF)
         nc.vector.tensor_copy(tab_picked[:], tab_rows[:].indirect(idx[:]))
         deal_w1_scales(staged[:, W1_AT:STAGED], w1_rows[0][:])
         nc.vector.tensor_copy(staged[:, TAB_AT:W1_AT].bitcast(I32), tab_picked[:].bitcast(I32))
         move_rows(planes[0], staged, 96, 0, STAGED)
-        tab_w[1] = placed([P, T], I32, "tab_w1", 40 * KIB + 768)
+        tab_w[1] = placed([P, T], I32, "tab_w1", 9 * KIB + 768)
         nc.sync.dma_start(tab_w[1][:], tab_words[1].rearrange("p t i -> p (t i)").bitcast(I32))
-        w1_raw[1] = placed([P, 2, QUARTER], I32, "w1_raw1", 38 * KIB + QUARTER)
+        w1_raw[1] = placed([P, 2, QUARTER], I32, "w1_raw1", 26 * KIB + QUARTER)
         nc.sync.dma_start(w1_raw[1][:], w1_word_rows[:, :, QUARTER:HALF])
 
         def w1_scales_of(a, b, t):
@@ -124,7 +124,7 @@ def tile_list_soft_gripper_valves_kernel(
 
         w2_grouped = [placed([P, 4 * HALF], BF16, "w2_grouped0", 84 * KIB), placed([P, 4 * HALF], BF16, "w2_grouped1", 76 * KIB)]
         w2_codes = [held([P, HALF], U32, "w2_codes%d" % b) for b in range(2)]
-        w2_scales = [placed([P, HALF], U8, "w2_scales0", 40 * KIB + QUARTER), held([P, HALF], U8, "w2_scales1")]
+        w2_scales = [placed([P, HALF], U8, "w2_scales0", 25 * KIB + 768), held([P, HALF], U8, "w2_scales1")]
 
         def round_w2(raw, b, lo, hi):
             nc.scalar.copy(
@@ -220,7 +220,7 @@ def tile_list_soft_gripper_valves_kernel(
                 sums = tiles[b, jt]
                 records = slice(JT * jl, JT * (jl + 1))
                 if jt in on_gpsimd:
-                    woven = placed([P, JT, 4], F32, "woven", 38 * KIB + QUARTER)
+                    woven = placed([P, JT, 4], F32, "woven", 26 * KIB + QUARTER)
                     nc.scalar.copy(
                         woven[:].rearrange("p (c i) t -> p c t i", i=2), sums[:].rearrange("p t (c i) -> p c t i", i=2)
                     )
@@ -260,16 +260,18 @@ def tile_list_soft_gripper_valves_kernel(
             )
 
         load_w2_late(0)
-        staged_late = placed([P, H], U8, "staged_late", 64 * KIB)
+        for jh in range(2):
+            gather_v(0, jh)
+        staged_late = placed([P, H], U8, "staged_late", 55 * KIB + 768)
         deal_w1_scales(staged_late[:], w1_rows[1][:])
         move_rows(late, staged_late, 48, 0, H)
         load_w2_late(1)
-        for jh in range(2):
-            gather_v(0, jh)
-        copy_out(0, 1, 25 * KIB + HALF)
+        copy_out(0, 1, 33 * KIB)
         pressure_tiles(0, range(8))
 
-        w4_raw = placed([P, 4, N], F32, "w4_raw", 4 * KIB)
+        for jh in range(2):
+            gather_v(1, jh, QUARTER)
+        w4_raw = placed([P, 4, N], F32, "w4_raw", 2 * KIB)
         nc.sync.dma_start(
             w4_raw[:].rearrange("p i n -> p (i n)"), w4[0:HALF, :].rearrange("(p i) n -> p (i n)", i=4)
         )
@@ -282,7 +284,7 @@ def tile_list_soft_gripper_valves_kernel(
         w3_codes = placed([P, 2, N], I32, "w3_codes", 21 * KIB + 768)
         nc.sync.dma_start(w3_codes[:], w3_words.rearrange("a p c i -> p a (c i)").bitcast(I32))
         w3_planes = placed([P, N], U8, "w3_planes", 25 * KIB)
-        nc.vector.memset(w3_planes[:].bitcast(I32), 0)
+        nc.gpsimd.memset(w3_planes[:].bitcast(I32), 0)
         for q in range(4):
             nc.sync.dma_start(
                 w3_planes[32 * q + 4 : 32 * q + 12, :].bitcast(I32), w3_scales.bitcast(I32)[:, 4 * q : 4 * q + 4, :]
@@ -291,8 +293,6 @@ def tile_list_soft_gripper_valves_kernel(
         with nc.allow_non_contiguous_dma(reason="one bias value a partition"):
             nc.sync.dma_start(bias[:], bv.rearrange("(c p) -> p c", p=P))
 
-        for jh in range(2):
-            gather_v(1, jh, QUARTER)
         pressure_tiles(1, range(8))
         deal_w1_words(1)
 

from contextlib import ExitStack

import concourse.mybir as mybir

K, K2, H, N, T, S = 1024, 512, 1024, 384, 4096, 1024
FLOPS = 2 * S * (K * H + K2 * H + 2 * H * N)

F32 = mybir.dt.float32
BF16 = mybir.dt.bfloat16
I32 = mybir.dt.int32
U32 = mybir.dt.uint32
U16 = mybir.dt.uint16
U8 = mybir.dt.uint8
FP8X4 = mybir.dt.float8_e4m3fn_x4
FP4X4 = mybir.dt.float4_e2m1fn_x4
MULT = mybir.AluOpType.mult
ADD = mybir.AluOpType.add
TANH = mybir.ActivationFunctionType.Tanh
IDENTITY = mybir.ActivationFunctionType.Identity

P = 128
HALF = 512
QUARTER = 256
JT = 128
KIB = 1024
TAB_AT, W1_AT, STAGED = 0, S, S + HALF


def tile_list_soft_gripper_valves_kernel(
    tc, tab_words, tab_scales, offs, tab2_words, tab2_scales, offs2,
    w1_words, w1_scales, w2, w3_words, w3_scales, w4, bv, out,
):
    nc = tc.nc
    with ExitStack() as ctx:
        lists = ctx.enter_context(tc.tile_pool(name="lists", bufs=1))
        keep = ctx.enter_context(tc.tile_pool(name="keep", bufs=1))
        laid = ctx.enter_context(tc.tile_pool(name="laid", bufs=1))
        ring = ctx.enter_context(tc.tile_pool(name="ring", bufs=9))
        psum = ctx.enter_context(tc.psum_pool(name="psum", bufs=1))

        def held(shape, dtype, name, tag=None):
            return keep.tile(shape, dtype, name=name, tag=tag or name, align_bytes=256)

        def placed(shape, dtype, name, at):
            return laid.tile(shape, dtype, name=name, tag=name, align_bytes=256, offset=at)

        def bank(number, shape):
            return psum.tile(shape, F32, name="bank%d" % number, tag="bank%d" % number)

        idx = lists.tile([P, S // 16], U16, name="idx")
        idx2 = lists.tile([P, S // 16], U16, name="idx2")

        tab2_rows = placed([P, T], U8, "tab2_rows", 37 * KIB)
        tab_rows = held([P, T], U8, "tab_rows")
        w1_rows = [held([P, HALF], U8, "w1_rows0"), placed([P, H], U8, "w1_rows1", 90 * KIB)]
        staged = placed([P, STAGED], U8, "staged", KIB)
        tab2_plane = held([P, S], U8, "tab2_plane")
        planes = [held([P, STAGED], U8, "planes0"), None]
        late = held([P, H], U8, "late")

        for engine, lo, hi in ((nc.vector, 0, 48), (nc.gpsimd, 64, P)):
            engine.memset(tab2_rows[lo:hi, :].bitcast(I32), 0)
        nc.vector.memset(w1_rows[0][0:96, :].bitcast(I32), 0)
        nc.vector.memset(tab_rows[0:96, :].bitcast(I32), 0)
        nc.gpsimd.memset(tab2_plane[:].bitcast(I32), 0)
        nc.gpsimd.memset(planes[0][:].bitcast(I32), 0)
        for engine, lo, hi in ((nc.vector, 0, 48), (nc.gpsimd, 64, P)):
            engine.memset(w1_rows[1][lo:hi, :].bitcast(I32), 0)
        nc.gpsimd.memset(late[:].bitcast(I32), 0)

        w1_scale_words = w1_scales.bitcast(I32)

        w1_word_rows = w1_words.bitcast(I32).rearrange("a p w -> p a w")
        nc.sync.dma_start(tab2_rows[48:64, :].bitcast(I32), tab2_scales[0].bitcast(I32))
        nc.sync.dma_start(idx2[:], offs2)
        nc.sync.dma_start(tab_rows[96:128, :].bitcast(I32), tab_scales.rearrange("a q t -> (a q) t").bitcast(I32))
        nc.sync.dma_start(idx[:], offs)
        nc.sync.dma_start(
            w1_rows[0][96:128, :].bitcast(I32), w1_scale_words.rearrange("a q c -> (a q) c")[:, 0 : HALF // 4]
        )
        nc.sync.dma_start(
            w1_rows[1][48:64, :].bitcast(I32).rearrange("q (a c) -> q a c", a=2),
            w1_scale_words.rearrange("a q c -> q a c")[:, :, HALF // 4 : H // 4],
        )
        w2_first = held([P, 4, HALF], F32, "w2_first")
        nc.sync.dma_start(w2_first[:], w2[:, 0:HALF].rearrange("(p i) c -> p i c", i=4))
        tab2_w = placed([P, T // 2], I32, "tab2_w", 60 * KIB)
        nc.sync.dma_start(tab2_w[:], tab2_words[0].bitcast(I32))
        w1_raw = [held([P, 2, QUARTER], I32, "w1_raw0"), None]
        nc.sync.dma_start(w1_raw[0][:], w1_word_rows[:, :, 0:QUARTER])

        def deal_w1_scales(dealt, rows):
            nc.vector.tensor_copy(
                dealt.rearrange("p (b t c i) -> p c b t i", c=8, t=4, i=16),
                rows.rearrange("p (b c i t) -> p c b t i", c=8, t=4, i=16),
            )

        def move_rows(plane, source, first, lo, hi):
            for r in range(4):
                nc.sync.dma_start(
                    plane[r:P:32, :].bitcast(I32), source[first + r : first + 16 : 4, lo:hi].bitcast(I32)
                )

        tab2_picked = held([P, S], U8, "tab2_picked")
        nc.vector.tensor_copy(tab2_picked[:], tab2_rows[:].indirect(idx2[:]))
        move_rows(tab2_plane, tab2_picked, 48, 0, S)
        tab_w = [placed([P, T], I32, "tab_w0", 40 * KIB + 768), None]
        nc.sync.dma_start(tab_w[0][:], tab_words[0].rearrange("p t i -> p (t i)").bitcast(I32))

        tab_picked = placed([P, S], U8, "tab_picked", 25 * KIB + HALF)
        nc.vector.tensor_copy(tab_picked[:], tab_rows[:].indirect(idx[:]))
        deal_w1_scales(staged[:, W1_AT:STAGED], w1_rows[0][:])
        nc.vector.tensor_copy(staged[:, TAB_AT:W1_AT].bitcast(I32), tab_picked[:].bitcast(I32))
        move_rows(planes[0], staged, 96, 0, STAGED)
        tab_w[1] = placed([P, T], I32, "tab_w1", 9 * KIB + 768)
        nc.sync.dma_start(tab_w[1][:], tab_words[1].rearrange("p t i -> p (t i)").bitcast(I32))
        w1_raw[1] = placed([P, 2, QUARTER], I32, "w1_raw1", 26 * KIB + QUARTER)
        nc.sync.dma_start(w1_raw[1][:], w1_word_rows[:, :, QUARTER:HALF])

        def w1_scales_of(a, b, t):
            if b == 0:
                return planes[a][:, W1_AT + P * t : W1_AT + P * (t + 1)]
            return late[:, HALF * a + P * t : HALF * a + P * (t + 1)]

        w2_grouped = [placed([P, 4 * HALF], BF16, "w2_grouped0", 84 * KIB), placed([P, 4 * HALF], BF16, "w2_grouped1", 76 * KIB)]
        w2_codes = [held([P, HALF], U32, "w2_codes%d" % b) for b in range(2)]
        w2_scales = [placed([P, HALF], U8, "w2_scales0", 25 * KIB + 768), held([P, HALF], U8, "w2_scales1")]

        def round_w2(raw, b, lo, hi):
            nc.scalar.copy(
                w2_grouped[b][:].rearrange("p (t m i) -> p t m i", t=4, i=4)[:, :, lo:hi, :].rearrange("p t m i -> p m i t"),
                raw[:].rearrange("p i (m t) -> p m i t", t=4),
            )

        def quantise_w2(b):
            nc.vector.quantize_mx(w2_codes[b][:].bitcast(FP8X4), w2_scales[b][:], w2_grouped[b][:])

        w1_codes = [held([P, 2, 2 * HALF], U8, "w1_codes%d" % b) for b in range(2)]

        def deal_w1_words(b):
            for a in range(2):
                nc.scalar.copy(
                    w1_codes[b][:, a, :].bitcast(U16).rearrange("p (t c i) -> p c t i", t=4, i=8),
                    w1_raw[b][:, a, :].bitcast(U16).rearrange("p (c i t) -> p c t i", t=4, i=8),
                )

        v, v2 = {}, {}

        def gather_v(a, jh, width=HALF):
            v[a, jh] = held([P, HALF], U32, "v%d%d" % (a, jh))
            for lo in range(0, HALF, width):
                at = (HALF * jh + lo) // 16
                nc.vector.tensor_copy(
                    v[a, jh][:, lo : lo + width], tab_w[a][:].bitcast(U32).indirect(idx[:, at : at + width // 16])
                )

        def gather_v2(jh):
            v2[jh] = placed([P, 2 * HALF], U8, "v2%d" % jh, (88, 86)[jh] * KIB)
            nc.vector.tensor_copy(
                v2[jh][:].bitcast(U16), tab2_w[:].bitcast(U16).indirect(idx2[:, 32 * jh : 32 * (jh + 1)])
            )

        def pressure_pass(sums, a, b, t, lo, width, start, stop):
            jh, at = divmod(lo, HALF)
            nc.tensor.matmul_mx(
                sums,
                lhsT=w1_codes[b][:, a, 2 * P * t : 2 * P * (t + 1)].bitcast(FP4X4),
                lhsT_scale=w1_scales_of(a, b, t),
                rhs=v[a, jh][:, at : at + width].bitcast(FP8X4),
                rhs_scale=planes[a][:, TAB_AT + lo : TAB_AT + lo + width],
                start=start,
                stop=stop,
            )

        def tactile_pass(sums, b, t, lo, width):
            jh, at = divmod(lo, HALF)
            nc.tensor.matmul_mx(
                sums,
                lhsT=w2_codes[b][:, P * t : P * (t + 1)].bitcast(FP8X4),
                lhsT_scale=w2_scales[b][:, P * t : P * (t + 1)],
                rhs=v2[jh][:, 2 * at : 2 * (at + width)].bitcast(FP4X4),
                rhs_scale=tab2_plane[:, lo : lo + width],
                start=True,
                stop=True,
            )

        copied, wide, tiles = {}, {}, {}

        def copy_slots(b, jh, slots):
            for t in slots:
                nc.scalar.copy(copied[b, jh][:, t, :], wide[b, jh, t][:])

        def copy_out(b, jh, at=None):
            name = "copied%d%d" % (b, jh)
            copied[b, jh] = held([P, 4, HALF], F32, name) if at is None else placed([P, 4, HALF], F32, name, at)
            copy_slots(b, jh, range(4))

        def wide_pressure(jh, slots, banks):
            for t, number in zip(slots, banks):
                wide[1, jh, t] = bank(number, [P, HALF])
                for a in range(2):
                    pressure_pass(wide[1, jh, t][:], a, 1, t, HALF * jh, HALF, a == 0, a == 1)

        def pressure_tiles(a, which):
            for jt in which:
                if a == 0:
                    tiles[0, jt] = bank(jt, [P, 4, JT])
                for t in range(4):
                    pressure_pass(tiles[0, jt][:, t, :], a, 0, t, JT * jt, JT, (a, t) == (0, 0), (a, t) == (1, 3))

        def tactile_tiles(which, banks):
            for jt, number in zip(which, banks):
                tiles[1, jt] = bank(number, [P, 4, JT])
                for t in range(4):
                    tactile_pass(tiles[1, jt][:, t, :], 1, t, JT * jt, JT)

        def grasp_code(h, b, lo, which, on_gpsimd=()):
            for jt in which:
                jh, jl = divmod(jt, 4)
                sums = tiles[b, jt]
                records = slice(JT * jl, JT * (jl + 1))
                if jt in on_gpsimd:
                    woven = placed([P, JT, 4], F32, "woven", 26 * KIB + QUARTER)
                    nc.scalar.copy(
                        woven[:].rearrange("p (c i) t -> p c t i", i=2), sums[:].rearrange("p t (c i) -> p c t i", i=2)
                    )
                    nc.gpsimd.tensor_tensor(
                        h[:, JT * jt - lo : JT * (jt + 1) - lo, :],
                        woven[:],
                        copied[b, jh][:, :, records].rearrange("p t j -> p j t"),
                        MULT,
                    )
                    continue
                nc.vector.tensor_tensor(
                    h[:, JT * jt - lo : JT * (jt + 1) - lo, :].rearrange("p (c i) t -> p c t i", i=2),
                    sums[:].rearrange("p t (c i) -> p c t i", i=2),
                    copied[b, jh][:, :, records].rearrange("p t (c i) -> p c t i", i=2),
                    MULT,
                )

        round_w2(w2_first, 0, 0, P)
        deal_w1_words(0)
        gather_v2(0)
        quantise_w2(0)
        planes[1] = placed([P, STAGED], U8, "planes1", 84 * KIB)
        nc.vector.memset(planes[1][:].bitcast(I32), 0)
        move_rows(planes[1], staged, 112, 0, STAGED)
        gather_v2(1)
        for jh in range(2):
            for t in range(4):
                wide[0, jh, t] = bank(4 * jh + t, [P, HALF])
                tactile_pass(wide[0, jh, t][:], 0, t, HALF * jh, HALF)
        copy_out(0, 0)

        w2_late = [placed([P, 4, QUARTER], F32, "w2_late%d" % u, (60, 90)[u] * KIB) for u in range(2)]

        def load_w2_late(u):
            nc.sync.dma_start(
                w2_late[u][:], w2[:, HALF + QUARTER * u : HALF + QUARTER * (u + 1)].rearrange("(p i) c -> p i c", i=4)
            )

        load_w2_late(0)
        for jh in range(2):
            gather_v(0, jh)
        staged_late = placed([P, H], U8, "staged_late", 55 * KIB + 768)
        deal_w1_scales(staged_late[:], w1_rows[1][:])
        move_rows(late, staged_late, 48, 0, H)
        load_w2_late(1)
        copy_out(0, 1, 33 * KIB)
        pressure_tiles(0, range(8))

        for jh in range(2):
            gather_v(1, jh, QUARTER)
        w4_raw = placed([P, 4, N], F32, "w4_raw", 2 * KIB)
        nc.sync.dma_start(
            w4_raw[:].rearrange("p i n -> p (i n)"), w4[0:HALF, :].rearrange("(p i) n -> p (i n)", i=4)
        )
        w4_rows = w4[HALF:H, :].rearrange("(p i) n -> p i n", i=4)
        copied[1, 1] = placed([P, 4, HALF], F32, "copied11", 13 * KIB + 768)
        w4_pair = copied[1, 1][:, 2:4, :].rearrange("p u (v n) -> p (u v) n", v=2)
        nc.sync.dma_start(w4_pair, w4_rows[:, :, 0:QUARTER])
        w4_last = placed([P, 4, P], F32, "w4_last", 10 * KIB)
        nc.sync.dma_start(w4_last[:], w4_rows[:, :, QUARTER:N])
        w3_codes = placed([P, 2, N], I32, "w3_codes", 21 * KIB + 768)
        nc.sync.dma_start(w3_codes[:], w3_words.rearrange("a p c i -> p a (c i)").bitcast(I32))
        w3_planes = placed([P, N], U8, "w3_planes", 25 * KIB)
        nc.gpsimd.memset(w3_planes[:].bitcast(I32), 0)
        for q in range(4):
            nc.sync.dma_start(
                w3_planes[32 * q + 4 : 32 * q + 12, :].bitcast(I32), w3_scales.bitcast(I32)[:, 4 * q : 4 * q + 4, :]
            )
        bias = placed([P, N // P], F32, "bias", 24 * KIB + 768)
        with nc.allow_non_contiguous_dma(reason="one bias value a partition"):
            nc.sync.dma_start(bias[:], bv.rearrange("(c p) -> p c", p=P))

        pressure_tiles(1, range(8))
        deal_w1_words(1)

        h_codes = {}
        h_scales = {}

        def quantise_h(h, b, lo, scales_at=None):
            width = h.shape[1]
            h_codes[b, lo] = held([P, width], U32, "h_codes%d_%d" % (b, lo))
            if scales_at:
                h_scales[b, lo] = placed([P, width], U8, "h_scales%d_%d" % (b, lo), scales_at)
            else:
                h_scales[b, lo] = held([P, width], U8, "h_scales%d_%d" % (b, lo))
            nc.vector.quantize_mx(
                h_codes[b, lo][:].bitcast(FP8X4), h_scales[b, lo][:], h[:].rearrange("p j t -> p (j t)")
            )

        def valve_pass(sums, weights, scales, b, lo, start, stop):
            nc.tensor.matmul_mx(
                sums, lhsT=weights.bitcast(FP8X4), lhsT_scale=scales,
                rhs=h_codes[b, lo][:].bitcast(FP8X4), rhs_scale=h_scales[b, lo][:], start=start, stop=stop,
            )

        def valve(n, lo, width, banks):
            apart = len(banks) == 2
            if apart:
                o_sum, d_sum = bank(banks[0], [P, width])[:], bank(banks[1], [P, width])[:]
            else:
                both = bank(banks[0], [P, 2, width])
                o_sum, d_sum = both[:, 0, :], both[:, 1, :]
            cols = slice(P * n, P * (n + 1))
            for b in range(2):
                valve_pass(o_sum, w4_codes[b][:, cols], w4_scales[b][:, cols], b, lo, b == 0, b == 1 and apart)
                valve_pass(
                    d_sum, w3_codes[:, b, cols], w3_planes[4 + 4 * b : P, cols],
                    b, lo, b == 0 and apart, b == 1,
                )
            gate = ring.tile([P, width], F32, name="gate")
            nc.scalar.activation(gate[:], o_sum, TANH, scale=0.5)
            return gate, d_sum

        def gate_drive(width, gate, d_sum):
            gated = ring.tile([P, width], F32, name="gated")
            nc.vector.scalar_tensor_tensor(gated[:], gate[:], 1.0, d_sum, ADD, MULT)
            return gated

        def add_on_gpsimd(result, gated, column):
            nc.gpsimd.tensor_scalar(result, gated, 0.5, column, MULT, ADD)

        def add_on_scalar(result, gated, column):
            nc.scalar.activation(result, gated, IDENTITY, bias=column, scale=0.5)

        def store(n, lo, width, gated, add_bias, at=None):
            if at:
                result = placed([P, width], F32, "result_held%d" % n, at)
            else:
                result = ring.tile([P, width], F32, name="result", align_bytes=256)
            add_bias(result[:], gated[:], bias[:, n : n + 1])
            nc.sync.dma_start(out[P * n : P * (n + 1), lo : lo + width], result[:])

        h00 = placed([P, HALF, 4], BF16, "h00", 80 * KIB)
        grasp_code(h00, 0, 0, range(4), on_gpsimd=(1,))
        h02 = held([P, QUARTER, 4], BF16, "h02")
        grasp_code(h02, 0, HALF, (4, 5))
        h03 = held([P, QUARTER, 4], BF16, "h03")
        grasp_code(h03, 0, 768, (6, 7))
        wide_pressure(0, range(4), range(4))
        round_w2(w2_late[0], 1, 0, P // 2)
        round_w2(w2_late[1], 1, P // 2, P)
        copy_out(1, 0, 93 * KIB)
        quantise_w2(1)
        quantise_h(h00, 0, 0, 90 * KIB)

        w4_first = placed([P, 4 * N], BF16, "w4_first", 78 * KIB)
        nc.gpsimd.tensor_scalar(
            w4_first[:, 0 : 4 * QUARTER].rearrange("p (n i) -> p n i", i=4),
            w4_raw[:, :, 0:QUARTER].rearrange("p i n -> p n i"),
            1.0, 0.0, MULT, ADD,
        )
        wide_pressure(1, (0, 1), (4, 5))
        tactile_tiles((0, 1, 2), (6, 7, 0))
        wide_pressure(1, (2,), (2,))
        tactile_tiles((3,), (1,))
        wide_pressure(1, (3,), (3,))
        h10 = held([P, HALF, 4], BF16, "h10")
        grasp_code(h10, 1, 0, range(4))
        w4_late = [held([P, 4 * P], BF16, "w4_late%d" % n) for n in range(N // P)]

        def round_w4_late(n, raw):
            nc.scalar.copy(
                w4_late[n][:].rearrange("p (c m i) -> p c i m", m=4, i=4), raw.rearrange("p i (c m) -> p c i m", m=4)
            )

        copy_slots(1, 1, (0, 1))
        nc.scalar.copy(
            w4_first[:, 4 * QUARTER : 4 * N].rearrange("p (c m i) -> p c i m", m=4, i=4),
            w4_raw[:, :, QUARTER:N].rearrange("p i (c m) -> p c i m", m=4),
        )
        for n in range(2):
            round_w4_late(n, w4_pair[:, :, P * n : P * (n + 1)])
        copy_slots(1, 1, (2, 3))
        round_w4_late(2, w4_last[:])

        w4_codes = [held([P, N], U32, "w4_codes%d" % b) for b in range(2)]
        w4_scales = [placed([P, N], U8, "w4_scales%d" % b, 5 * KIB + HALF * b) for b in range(2)]

        def quantise_w4_late(n):
            cols = slice(P * n, P * (n + 1))
            nc.vector.quantize_mx(w4_codes[1][:, cols].bitcast(FP8X4), w4_scales[1][:, cols], w4_late[n][:])

        nc.vector.quantize_mx(w4_codes[0][:].bitcast(FP8X4), w4_scales[0][:], w4_first[:])
        quantise_h(h10, 1, 0, 4 * KIB)
        quantise_w4_late(0)
        quantise_w4_late(1)
        quantise_h(h02, 0, HALF, 4 * KIB + HALF)
        quantise_h(h03, 0, 768, 4 * KIB + 768)
        quantise_w4_late(2)
        tactile_tiles((4, 5, 6, 7), (6, 7, 0, 1))
        first = [valve(n, 0, HALF, banks) for n, banks in enumerate(((5, 4), (3, 2)))]
        h12 = placed([P, QUARTER, 4], BF16, "h12", 8 * KIB + QUARTER)
        grasp_code(h12, 1, HALF, (4, 5))
        first.append(valve(2, 0, HALF, (5, 6)))
        gated = gate_drive(HALF, *first[0])
        quantise_h(h12, 1, HALF)
        store(0, 0, HALF, gated, add_on_gpsimd, 8 * KIB + QUARTER)
        second = [valve(n, HALF, QUARTER, (number,)) for n, number in enumerate((3, 7, 4))]
        h13 = placed([P, QUARTER, 4], BF16, "h13", 11 * KIB + 768)
        grasp_code(h13, 1, 768, (6, 7))
        gated = gate_drive(HALF, *first[1])
        quantise_h(h13, 1, 768)
        store(1, 0, HALF, gated, add_on_gpsimd, 11 * KIB + 768)
        third = [valve(n, 768, QUARTER, (number,)) for n, number in enumerate((5, 0, 1))]
        store(2, 0, HALF, gate_drive(HALF, *first[2]), add_on_gpsimd)
        for n, add_bias in enumerate((add_on_scalar, add_on_gpsimd, add_on_scalar)):
            store(n, HALF, QUARTER, gate_drive(QUARTER, *second[n]), add_bias)
        for n, add_bias in enumerate((add_on_scalar, add_on_gpsimd, add_on_scalar)):
            store(n, 768, QUARTER, gate_drive(QUARTER, *third[n]), add_bias)
